import numpy as np
import ml_dtypes


def mxq(x, axis, fmt="e4m3"):
    dtype, down = {"e4m3": (ml_dtypes.float8_e4m3fn, 7), "e5m2": (ml_dtypes.float8_e5m2, 14)}[fmt]
    v = np.moveaxis(np.asarray(x, np.float32).astype(ml_dtypes.bfloat16).astype(np.float64), axis, -1)
    blocks = v.reshape(v.shape[:-1] + (-1, 32))
    amax = np.abs(blocks).max(-1, keepdims=True)
    byte = np.maximum(np.where(amax > 0, np.frexp(amax)[1] - 1 + 127, 0) - down, 1)
    scale = np.exp2(byte - 127.0)
    codes = (blocks / scale).astype(np.float32).astype(dtype).astype(np.float64)
    return np.moveaxis((codes * scale).reshape(v.shape), -1, axis)


WIDE = False


def mx_kscale(k):
    if not WIDE:
        return np.ones(k)
    levels = np.array([10, -10, 5, -5, 0])
    if k % 512:
        return np.exp2(np.random.permutation(np.resize(levels, k // 32))).repeat(32)
    a = np.empty((k // 512, 16))
    for p in range(k // 512):
        a[p, :8] = np.random.permutation(np.resize(levels, 8))
        for g in range(8):
            far = levels[np.abs(levels - a[p, g]) >= 10]
            a[p, g + 8] = far[np.random.randint(len(far))]
    return np.exp2(a.ravel()).repeat(32)


def f64(x):
    return np.asarray(x).astype(np.float64)


def striped(idx):
    return np.tile(idx.reshape(-1, 16).T, (8, 1)).astype(np.uint16)


def unstriped(offs):
    return offs[:16].T.reshape(-1).astype(np.int64)


E2M1 = np.array([0.0, 0.5, 1.0, 1.5, 2.0, 3.0, 4.0, 6.0, -0.0, -0.5, -1.0, -1.5, -2.0, -3.0, -4.0, -6.0])


def pack_weight(w, fmt):
    k, n = w.shape
    w = f64(np.asarray(w, np.float32).astype(ml_dtypes.bfloat16)).reshape(k // 32, 32, n)
    amax = np.abs(w).max(1)
    if fmt == "e4m3":
        byte = np.frexp(amax)[1] - 1 + 127 - 7
    else:
        mant, ex = np.frexp(amax / 6.0)
        byte = np.where(mant > 0.5, ex, ex - 1) + 127
    byte = np.clip(np.where(amax > 0, byte, 1), 1, 254)
    scaled = (w * np.exp2(127.0 - byte)[:, None, :]).reshape(k, n).astype(np.float32)
    by_word = np.ascontiguousarray(scaled.reshape(k // 512, 128, 4, n).transpose(0, 1, 3, 2))
    if fmt == "e4m3":
        words = by_word.astype(ml_dtypes.float8_e4m3fn).view(np.uint8)
    else:
        c = by_word.astype(ml_dtypes.float4_e2m1fn).view(np.uint8) & 0xF
        words = (c[..., 0::2] | (c[..., 1::2] << 4)).reshape(k // 512, 128, 2 * n)
    return np.ascontiguousarray(words), np.ascontiguousarray(byte.astype(np.uint8).reshape(k // 512, 16, n))


def unpack_weight(words, scales, fmt):
    g, _, n = scales.shape
    words = np.ascontiguousarray(words).reshape(g, 128, n, -1)
    if fmt == "e4m3":
        vals = words.view(ml_dtypes.float8_e4m3fn).astype(np.float64)
    else:
        nib = np.empty((g, 128, n, 4), np.uint8)
        nib[..., 0::2] = words & 0xF
        nib[..., 1::2] = words >> 4
        vals = E2M1[nib]
    vals = vals * np.repeat(np.exp2(scales.astype(np.float64) - 127.0), 8, axis=1)[..., None]
    return vals.transpose(0, 1, 3, 2).reshape(g * 512, n)


def d_relu(v):
    return (v > 0).astype(np.float64)


K, T, G, C1, E, C2, H = 512, 1024, 4, 256, 8, 128, 512
N = 512


def by_expert(wq, xq, E, C):
    return np.concatenate([wq[e].T @ xq[:, e * C:(e + 1) * C] for e in range(E)], axis=1)


def setup_inputs():
    n = np.random.standard_normal
    v = mx_kscale(N)
    u = mx_kscale(H)
    slots1 = np.random.permutation(T)
    slots2 = np.concatenate([q * C1 + np.random.permutation(C1) for q in range(G)])
    dy = pack_weight(n((N, T)) * v[:, None], "e4m3")
    wet = [pack_weight(m, "e4m3") for m in n((E, N, H)) / np.sqrt(N) / v[None, :, None] * u]
    wgt = [pack_weight(m, "e4m3") for m in n((G, H, K)) / np.sqrt(H) / u[None, :, None]]
    return {
        "dy_words": dy[0],
        "dy_scales": dy[1],
        "wet_words": np.stack([m[0] for m in wet]),
        "wet_scales": np.stack([m[1] for m in wet]),
        "wgt_words": np.stack([m[0] for m in wgt]),
        "wgt_scales": np.stack([m[1] for m in wgt]),
        "a": (n((H, T))).astype(np.float32),
        "gate": (np.tile(np.random.uniform(0.2, 1.0, T), (128, 1))).astype(np.float32),
        "offs": striped(slots1),
        "offs2": striped(slots2),
        "dst": striped(slots1[slots2]),
    }


def reference(dy_words, dy_scales, wet_words, wet_scales, wgt_words, wgt_scales, a, gate, offs, offs2, dst):
    wet = np.stack([unpack_weight(wet_words[e], wet_scales[e], "e4m3") for e in range(E)])
    wgt = np.stack([unpack_weight(wgt_words[e], wgt_scales[e], "e4m3") for e in range(G)])
    gq = unpack_weight(dy_words, dy_scales, "e4m3")[:, unstriped(dst)]
    z = f64(gate[:1]) * by_expert(wet, gq, E, C2)
    da = np.zeros((H, T))
    da[:, unstriped(offs2)] = z
    dx = by_expert(wgt, mxq(da * d_relu(f64(a)), 0, "e4m3"), G, C1)
    out = np.zeros((K, T))
    out[:, unstriped(offs)] = dx
    return out

@@ -1,0 +1,189 @@
+from contextlib import ExitStack
+
+import concourse.mybir as mybir
+from concourse.masks import make_identity
+
+K, T, G, C1, E, C2, H, N = 512, 1024, 4, 256, 8, 128, 512, 512
+FLOPS = 2 * T * N * H + 2 * T * H * K
+
+F32 = mybir.dt.float32
+BF16 = mybir.dt.bfloat16
+I32 = mybir.dt.int32
+U32 = mybir.dt.uint32
+U16 = mybir.dt.uint16
+U8 = mybir.dt.uint8
+FP8X4 = mybir.dt.float8_e4m3fn_x4
+ACT = mybir.ActivationFunctionType
+MULT = mybir.AluOpType.mult
+
+P = 128
+PACK = 4
+PER_COL = 16
+EPG = E // G
+
+
+def tile_moe_hib_relu_kernel(
+    tc, dy_words, dy_scales, wet_words, wet_scales, wgt_words, wgt_scales, a, gate, offs, offs2, dst, out
+):
+    nc = tc.nc
+
+    with ExitStack() as ctx:
+        keep = ctx.enter_context(tc.tile_pool(name="keep", bufs=1))
+        ring = ctx.enter_context(tc.tile_pool(name="ring", bufs=2))
+        psum = ctx.enter_context(tc.psum_pool(name="psum", bufs=2))
+
+        dst_l = keep.tile([P, T // PER_COL], U16, name="dst_l")
+        offs2_l = keep.tile([P, T // PER_COL], U16, name="offs2_l")
+        offs_l = keep.tile([P, T // PER_COL], U16, name="offs_l")
+        dy_w = keep.tile([P, T], U32, name="dy_w", align_bytes=64)
+        dy_s = keep.tile([P, T], U8, name="dy_s", align_bytes=64)
+        gq_w = keep.tile([P, T], U32, name="gq_w", align_bytes=64)
+        gq_s = keep.tile([P, T], U8, name="gq_s", align_bytes=64)
+        wet_w = [keep.tile([P, EPG, H], U32, name="wet_w%d" % f, align_bytes=64) for f in range(G)]
+        wet_s = keep.tile([P, E, H], U8, name="wet_s", align_bytes=64)
+        wgt_w = keep.tile([P, G, K], U32, name="wgt_w", align_bytes=64)
+        wgt_s = keep.tile([P, G, K], U8, name="wgt_s", align_bytes=64)
+        a_sb = [keep.tile([P, PACK, C1], F32, name="a_sb%d" % f) for f in range(G)]
+        gate_rows = keep.tile([P, C2], F32, name="gate_rows")
+        gate_col = keep.tile([P, E], F32, name="gate_col")
+        ident0 = keep.tile([P, P], F32, name="ident0")
+        ident = keep.tile([P, P], F32, name="ident")
+
+        def load_list(tile, src):
+            nc.sync.dma_start(tile[:], src)
+
+        def load_plane(tile, rows):
+            for q in range(4):
+                nc.sync.dma_start(tile[32 * q : 32 * q + 4].bitcast(I32), rows[4 * q : 4 * q + 4].bitcast(I32))
+
+        nc.vector.memset(dy_s[:].bitcast(I32), 0)
+        nc.vector.memset(wet_s[:].bitcast(I32), 0)
+        nc.vector.memset(wgt_s[:].bitcast(I32), 0)
+        make_identity(nc, ident0[:])
+        nc.scalar.copy(ident[:], ident0[:])
+
+        wet_words_p = wet_words.rearrange("e s p i d -> p (e s) (i d)")
+        a_p = a.rearrange("(p t) j -> p t j", t=PACK)
+
+        def load_wet(f):
+            nc.sync.dma_start(wet_w[f][:].bitcast(I32), wet_words_p[:, EPG * f : EPG * (f + 1), :].bitcast(I32))
+
+        load_list(dst_l, dst)
+        nc.sync.dma_start(dy_w[:].bitcast(I32), dy_words.rearrange("s p t d -> p (s t d)").bitcast(I32))
+        load_plane(dy_s, dy_scales.rearrange("s b t -> b (s t)"))
+        nc.sync.dma_start(gate_rows[:], gate.rearrange("r (e u) -> (r e) u", u=C2)[0:P, :])
+        load_wet(0)
+        load_plane(wet_s, wet_scales.rearrange("e s b i -> b (e s) i"))
+        load_list(offs2_l, offs2)
+        for f in range(1, G):
+            load_wet(f)
+        for f in range(G):
+            nc.sync.dma_start(a_sb[f][:], a_p[:, :, C1 * f : C1 * (f + 1)])
+        load_plane(wgt_s, wgt_scales.rearrange("f s b k -> b (f s) k"))
+        nc.sync.dma_start(wgt_w[:].bitcast(I32), wgt_words.rearrange("f s p k d -> p (f s) (k d)").bitcast(I32))
+        load_list(offs_l, offs)
+
+        gate_ps = psum.tile([P, P], F32, name="gate_ps", tag="dx", bufs=3)
+        nc.tensor.transpose(gate_ps[:], gate_rows[:], ident[:])
+        nc.scalar.copy(gate_col[:], gate_ps[:, 0:E])
+
+        def cols(lo, hi):
+            return slice(lo // PER_COL, hi // PER_COL)
+
+        def gather(lo, hi):
+            nc.vector.tensor_copy(gq_w[:, lo:hi], dy_w[:].indirect(dst_l[:, cols(lo, hi)]))
+            nc.vector.tensor_copy(gq_s[:, lo:hi], dy_s[:].indirect(dst_l[:, cols(lo, hi)]))
+
+        gather(0, C2)
+        gather(C2, C1)
+        gather(C1, T)
+
+        z = [keep.tile([P, PACK, C1], F32, name="z%d" % f) for f in range(G)]
+        zwin = [[keep.tile([P, T], F32, name="zwin%d_%d" % (f, t)) for t in range(PACK)] for f in range(G)]
+        dz = [keep.tile([P, C1, PACK], BF16, name="dz%d" % f, align_bytes=64) for f in range(G)]
+        mask = [keep.tile([P, C1 * PACK], BF16, name="mask%d" % f, align_bytes=64) for f in range(G)]
+        dx = [keep.tile([P, K // P, 2 * C1], F32, name="dx%d" % h) for h in range(G // 2)]
+        owin = [keep.tile([P, T], F32, name="owin%d" % c) for c in range(K // P)]
+
+        def expert(e):
+            f, h = divmod(e, EPG)
+            slots = slice(C2 * e, C2 * (e + 1))
+            zt_ps = psum.tile([P, H], F32, name="zt_ps", tag="zt")
+            nc.tensor.matmul_mx(
+                out=zt_ps[:],
+                lhsT=gq_w[:, slots].bitcast(FP8X4),
+                lhsT_scale=gq_s[:, slots],
+                rhs=wet_w[f][:, h, :].bitcast(FP8X4),
+                rhs_scale=wet_s[:, e, :],
+                start=True,
+                stop=True,
+            )
+            zt = ring.tile([P, PACK, P], F32, name="zt")
+            nc.scalar.activation(
+                zt[:], zt_ps[:].rearrange("m (p t) -> m t p", t=PACK), ACT.Copy, scale=gate_col[:, e : e + 1]
+            )
+            z_ps = psum.tile([P, PACK, C2], F32, name="z_ps", tag="z")
+            for t in range(PACK):
+                nc.tensor.transpose(z_ps[:, t, :], zt[:, t, :], ident[:])
+            nc.scalar.copy(z[f][:, :, C2 * h : C2 * (h + 1)], z_ps[:])
+
+        def scatter_z(f, lo, hi, last):
+            for t in range(PACK):
+                nc.vector.tensor_copy(
+                    zwin[f][t][:].indirect(offs2_l[:, cols(C1 * f + lo, C1 * f + hi)]), z[f][:, t, lo:hi]
+                )
+                if last:
+                    nc.scalar.copy(dz[f][:, :, t], zwin[f][t][:, C1 * f : C1 * (f + 1)])
+
+        def make_mask(f):
+            sign = ring.tile([P, C1, PACK], BF16, name="sign")
+            nc.scalar.activation(sign[:], a_sb[f][:].rearrange("p t j -> p j t"), ACT.Sign)
+            nc.scalar.activation(mask[f][:], sign[:].rearrange("p j t -> p (j t)"), ACT.Relu)
+
+        def group(f):
+            da = ring.tile([P, C1 * PACK], BF16, name="da", align_bytes=64)
+            nc.vector.tensor_tensor(da[:], dz[f][:].rearrange("p j t -> p (j t)"), mask[f][:], MULT)
+            da_w = ring.tile([P, C1], U32, name="da_w", align_bytes=64)
+            da_s = ring.tile([P, C1], U8, name="da_s", align_bytes=64)
+            nc.vector.quantize_mx(out=da_w[:].bitcast(FP8X4), scales=da_s[:], in_=da[:])
+            for half in range(2):
+                dx_ps = psum.tile([P, 2, C1], F32, name="dx_ps", tag="dx", bufs=3)
+                for u in range(2):
+                    ks = slice(P * (2 * half + u), P * (2 * half + u + 1))
+                    nc.tensor.matmul_mx(
+                        out=dx_ps[:, u, :],
+                        lhsT=wgt_w[:, f, ks].bitcast(FP8X4),
+                        lhsT_scale=wgt_s[:, f, ks],
+                        rhs=da_w[:].bitcast(FP8X4),
+                        rhs_scale=da_s[:],
+                        start=True,
+                        stop=True,
+                    )
+                nc.scalar.copy(dx[f // 2][:, 2 * half : 2 * half + 2, C1 * (f % 2) : C1 * (f % 2 + 1)], dx_ps[:])
+
+        def scatter_dx(h, c):
+            nc.vector.tensor_copy(
+                owin[c][:].indirect(offs_l[:, cols(2 * C1 * h, 2 * C1 * (h + 1))]), dx[h][:, c, :]
+            )
+
+        for e in range(E):
+            expert(e)
+        scatter_z(0, 0, C2, False)
+        scatter_z(0, C2, C1, True)
+        make_mask(0)
+        scatter_z(1, 0, C1, True)
+        make_mask(1)
+        group(0)
+        scatter_z(2, 0, C1, True)
+        make_mask(2)
+        group(1)
+        scatter_z(3, 0, C1, True)
+        make_mask(3)
+        group(2)
+        scatter_dx(0, 0)
+        group(3)
+        for c in range(1, K // P):
+            scatter_dx(0, c)
+        for c in range(K // P):
+            scatter_dx(1, c)
+            nc.sync.dma_start(out[P * c : P * (c + 1), :], owin[c][:])

@@ -40,9 +40,9 @@ def tile_moe_hib_relu_kernel(
         gq_w = keep.tile([P, T], U32, name="gq_w", align_bytes=64)
         gq_s = keep.tile([P, T], U8, name="gq_s", align_bytes=64)
         wet_w = [keep.tile([P, EPG, H], U32, name="wet_w%d" % f, align_bytes=64) for f in range(G)]
-        wet_s = keep.tile([P, E, H], U8, name="wet_s", align_bytes=64)
+        wet_s = [keep.tile([P, H], U8, name="wet_s%d" % h, align_bytes=64) for h in range(2)]
         wgt_w = keep.tile([P, G, K], U32, name="wgt_w", align_bytes=64)
-        wgt_s = keep.tile([P, G, K], U8, name="wgt_s", align_bytes=64)
+        wgt_s = keep.tile([P, K], U8, name="wgt_s", align_bytes=64)
         a_sb = [keep.tile([P, PACK, C1], F32, name="a_sb%d" % f) for f in range(G)]
         gate_rows = keep.tile([P, C2], F32, name="gate_rows")
         gate_col = keep.tile([P, E], F32, name="gate_col")
@@ -52,14 +52,16 @@ def tile_moe_hib_relu_kernel(
         def load_list(tile, src):
             nc.sync.dma_start(tile[:], src)
 
-        def load_plane(tile, rows):
+        def load_planes(tile, rows):
+            n = rows.shape[0]
             for q in range(4):
-                nc.sync.dma_start(tile[32 * q : 32 * q + 4].bitcast(I32), rows[4 * q : 4 * q + 4].bitcast(I32))
+                nc.sync.dma_start(
+                    tile[32 * q : 32 * q + 4 * n, :].bitcast(I32), rows[:, 4 * q : 4 * q + 4, :].bitcast(I32)
+                )
 
-        nc.vector.memset(dy_s[:].bitcast(I32), 0)
-        nc.vector.memset(wet_s[:].bitcast(I32), 0)
-        nc.vector.memset(wgt_s[:].bitcast(I32), 0)
         make_identity(nc, ident0[:])
+        nc.gpsimd.memset(wet_s[1][:].bitcast(I32), 0)
+        nc.gpsimd.memset(wgt_s[:].bitcast(I32), 0)
         nc.scalar.copy(ident[:], ident0[:])
 
         wet_words_p = wet_words.rearrange("e s p i d -> p (e s) (i d)")
@@ -68,22 +70,24 @@ def tile_moe_hib_relu_kernel(
         def load_wet(f):
             nc.sync.dma_start(wet_w[f][:].bitcast(I32), wet_words_p[:, EPG * f : EPG * (f + 1), :].bitcast(I32))
 
+        wet_rows = wet_scales.rearrange("e s b i -> (e s) b i")
         load_list(dst_l, dst)
-        nc.sync.dma_start(dy_w[:].bitcast(I32), dy_words.rearrange("s p t d -> p (s t d)").bitcast(I32))
-        load_plane(dy_s, dy_scales.rearrange("s b t -> b (s t)"))
         nc.sync.dma_start(gate_rows[:], gate.rearrange("r (e u) -> (r e) u", u=C2)[0:P, :])
+        load_planes(dy_s, dy_scales.to_broadcast([8, 16, T]))
+        nc.sync.dma_start(dy_w[:].bitcast(I32), dy_words.rearrange("s p t d -> p (s t d)").bitcast(I32))
         load_wet(0)
-        load_plane(wet_s, wet_scales.rearrange("e s b i -> b (e s) i"))
+        load_planes(wet_s[0], wet_rows)
         load_list(offs2_l, offs2)
+        load_planes(wet_s[1], wet_rows[4:8])
         for f in range(1, G):
             load_wet(f)
         for f in range(G):
             nc.sync.dma_start(a_sb[f][:], a_p[:, :, C1 * f : C1 * (f + 1)])
-        load_plane(wgt_s, wgt_scales.rearrange("f s b k -> b (f s) k"))
+        load_planes(wgt_s, wgt_scales.rearrange("f s b k -> (f s) b k"))
         nc.sync.dma_start(wgt_w[:].bitcast(I32), wgt_words.rearrange("f s p k d -> p (f s) (k d)").bitcast(I32))
         load_list(offs_l, offs)
 
-        gate_ps = psum.tile([P, P], F32, name="gate_ps", tag="dx", bufs=3)
+        gate_ps = psum.tile([P, P], F32, name="gate_ps", tag="first", bufs=1)
         nc.tensor.transpose(gate_ps[:], gate_rows[:], ident[:])
         nc.scalar.copy(gate_col[:], gate_ps[:, 0:E])
 
@@ -99,91 +103,128 @@ def tile_moe_hib_relu_kernel(
         gather(C1, T)
 
         z = [keep.tile([P, PACK, C1], F32, name="z%d" % f) for f in range(G)]
-        zwin = [[keep.tile([P, T], F32, name="zwin%d_%d" % (f, t)) for t in range(PACK)] for f in range(G)]
-        dz = [keep.tile([P, C1, PACK], BF16, name="dz%d" % f, align_bytes=64) for f in range(G)]
-        mask = [keep.tile([P, C1 * PACK], BF16, name="mask%d" % f, align_bytes=64) for f in range(G)]
-        dx = [keep.tile([P, K // P, 2 * C1], F32, name="dx%d" % h) for h in range(G // 2)]
-        owin = [keep.tile([P, T], F32, name="owin%d" % c) for c in range(K // P)]
+        dx = [[keep.tile([P, 2 * C1], F32, name="dx%d_%d" % (h, c)) for c in range(K // P)] for h in range(G // 2)]
+
+        def slot(name, shape, dtype, tag):
+            return keep.tile(shape, dtype, name=name, tag=tag, align_bytes=64)
 
         def expert(e):
             f, h = divmod(e, EPG)
             slots = slice(C2 * e, C2 * (e + 1))
-            zt_ps = psum.tile([P, H], F32, name="zt_ps", tag="zt")
+            zt_ps = psum.tile([P, H], F32, name="zt_ps", tag="first", bufs=1)
             nc.tensor.matmul_mx(
                 out=zt_ps[:],
                 lhsT=gq_w[:, slots].bitcast(FP8X4),
                 lhsT_scale=gq_s[:, slots],
                 rhs=wet_w[f][:, h, :].bitcast(FP8X4),
-                rhs_scale=wet_s[:, e, :],
+                rhs_scale=wet_s[e // 4][4 * (e % 4) : P, :],
                 start=True,
                 stop=True,
             )
-            zt = ring.tile([P, PACK, P], F32, name="zt")
-            nc.scalar.activation(
-                zt[:], zt_ps[:].rearrange("m (p t) -> m t p", t=PACK), ACT.Copy, scale=gate_col[:, e : e + 1]
-            )
-            z_ps = psum.tile([P, PACK, C2], F32, name="z_ps", tag="z")
-            for t in range(PACK):
-                nc.tensor.transpose(z_ps[:, t, :], zt[:, t, :], ident[:])
-            nc.scalar.copy(z[f][:, :, C2 * h : C2 * (h + 1)], z_ps[:])
-
-        def scatter_z(f, lo, hi, last):
-            for t in range(PACK):
-                nc.vector.tensor_copy(
-                    zwin[f][t][:].indirect(offs2_l[:, cols(C1 * f + lo, C1 * f + hi)]), z[f][:, t, lo:hi]
+            zt = slot("zt", [P, PACK, P], F32, "zt%d" % e)
+            step = PACK // 2 if e == 0 else PACK
+            for t0 in range(0, PACK, step):
+                ts = slice(t0, t0 + step)
+                nc.scalar.activation(
+                    zt[:, ts, :],
+                    zt_ps[:].rearrange("m (p t) -> m t p", t=PACK)[:, ts, :],
+                    ACT.Copy,
+                    scale=gate_col[:, e : e + 1],
                 )
-                if last:
-                    nc.scalar.copy(dz[f][:, :, t], zwin[f][t][:, C1 * f : C1 * (f + 1)])
+                z_ps = psum.tile([P, step, C2], F32, name="z_ps", tag="z")
+                for t in range(step):
+                    nc.tensor.transpose(z_ps[:, t, :], zt[:, t0 + t, :], ident[:])
+                nc.scalar.copy(z[f][:, ts, C2 * h : C2 * (h + 1)], z_ps[:])
+
+        def scatter_z(win, f, t, lo, hi):
+            nc.vector.tensor_copy(win[:].indirect(offs2_l[:, cols(C1 * f + lo, C1 * f + hi)]), z[f][:, t, lo:hi])
+
+        def round_z(dz, win, f, t):
+            nc.scalar.copy(dz[:, t, :], win[:, C1 * f : C1 * (f + 1)])
 
         def make_mask(f):
-            sign = ring.tile([P, C1, PACK], BF16, name="sign")
+            mask = slot("mask%d" % f, [P, C1, PACK], BF16, "mask%d" % f)
+            sign = slot("sign", [P, C1, PACK], BF16, "wet_w1")
             nc.scalar.activation(sign[:], a_sb[f][:].rearrange("p t j -> p j t"), ACT.Sign)
-            nc.scalar.activation(mask[f][:], sign[:].rearrange("p j t -> p (j t)"), ACT.Relu)
+            nc.scalar.activation(mask[:], sign[:], ACT.Relu)
+            return mask
 
-        def group(f):
-            da = ring.tile([P, C1 * PACK], BF16, name="da", align_bytes=64)
-            nc.vector.tensor_tensor(da[:], dz[f][:].rearrange("p j t -> p (j t)"), mask[f][:], MULT)
-            da_w = ring.tile([P, C1], U32, name="da_w", align_bytes=64)
-            da_s = ring.tile([P, C1], U8, name="da_s", align_bytes=64)
-            nc.vector.quantize_mx(out=da_w[:].bitcast(FP8X4), scales=da_s[:], in_=da[:])
-            for half in range(2):
-                dx_ps = psum.tile([P, 2, C1], F32, name="dx_ps", tag="dx", bufs=3)
+        def apply_mask(da, dz, f):
+            js = slice(C1 * (f % 2), C1 * (f % 2 + 1))
+            nc.gpsimd.tensor_tensor(da[:, js, :], dz[:].rearrange("p t j -> p j t"), relu_mask[f][:], MULT)
+
+        def quantise_and_multiply(h, da):
+            da_w = ring.tile([P, 2 * C1], U32, name="da_w", align_bytes=64)
+            da_s = ring.tile([P, 2 * C1], U8, name="da_s", align_bytes=64)
+            nc.vector.quantize_mx(out=da_w[:].bitcast(FP8X4), scales=da_s[:], in_=da[:].rearrange("p j t -> p (j t)"))
+            for c in range(K // P):
+                ks = slice(P * c, P * (c + 1))
+                dx_ps = psum.tile([P, 2 * C1], F32, name="dx_ps", tag="dx", bufs=3)
                 for u in range(2):
-                    ks = slice(P * (2 * half + u), P * (2 * half + u + 1))
+                    js = slice(C1 * u, C1 * (u + 1))
                     nc.tensor.matmul_mx(
-                        out=dx_ps[:, u, :],
-                        lhsT=wgt_w[:, f, ks].bitcast(FP8X4),
-                        lhsT_scale=wgt_s[:, f, ks],
-                        rhs=da_w[:].bitcast(FP8X4),
-                        rhs_scale=da_s[:],
+                        out=dx_ps[:, js],
+                        lhsT=wgt_w[:, 2 * h + u, ks].bitcast(FP8X4),
+                        lhsT_scale=wgt_s[4 * (2 * h + u) : P, ks],
+                        rhs=da_w[:, js].bitcast(FP8X4),
+                        rhs_scale=da_s[:, js],
                         start=True,
                         stop=True,
                     )
-                nc.scalar.copy(dx[f // 2][:, 2 * half : 2 * half + 2, C1 * (f % 2) : C1 * (f % 2 + 1)], dx_ps[:])
+                nc.scalar.copy(dx[h][c][:], dx_ps[:])
 
-        def scatter_dx(h, c):
-            nc.vector.tensor_copy(
-                owin[c][:].indirect(offs_l[:, cols(2 * C1 * h, 2 * C1 * (h + 1))]), dx[h][:, c, :]
-            )
+        def scatter_dx(win, h, c):
+            nc.vector.tensor_copy(win[:].indirect(offs_l[:, cols(2 * C1 * h, 2 * C1 * (h + 1))]), dx[h][c][:])
+
+        def window(name, tag):
+            return slot(name, [P, T], F32, tag)
 
         for e in range(E):
             expert(e)
-        scatter_z(0, 0, C2, False)
-        scatter_z(0, C2, C1, True)
-        make_mask(0)
-        scatter_z(1, 0, C1, True)
-        make_mask(1)
-        group(0)
-        scatter_z(2, 0, C1, True)
-        make_mask(2)
-        group(1)
-        scatter_z(3, 0, C1, True)
-        make_mask(3)
-        group(2)
-        scatter_dx(0, 0)
-        group(3)
-        for c in range(1, K // P):
-            scatter_dx(0, c)
+
+        relu_mask = [make_mask(f) for f in range(2)]
+
+        da0 = slot("da0", [P, 2 * C1, PACK], BF16, "da")
+        dz = slot("dz0", [P, PACK, C1], BF16, "zt3")
+        wins = [window("zwin0_%d" % t, "zwin0_%d" % t) for t in range(PACK)]
+        for t in range(PACK):
+            scatter_z(wins[t], 0, t, 0, C2)
+        for t in range(PACK):
+            scatter_z(wins[t], 0, t, C2, C1)
+            round_z(dz, wins[t], 0, t)
+        apply_mask(da0, dz, 0)
+
+        dz = slot("dz1", [P, PACK, C1], BF16, "zt5")
+        for t in range(PACK):
+            win = window("zwin1_%d" % t, "zwin1_%d" % t)
+            scatter_z(win, 1, t, 0, C1)
+            round_z(dz, win, 1, t)
+        apply_mask(da0, dz, 1)
+
+        relu_mask.extend(make_mask(f) for f in range(2, G))
+        dz2 = slot("dz2", [P, PACK, C1], BF16, "zt7")
+        for t in range(PACK):
+            win = window("zwin2_%d" % t, "zwin2_%d" % t)
+            scatter_z(win, 2, t, 0, C1)
+            round_z(dz2, win, 2, t)
+
+        dz = slot("dz3", [P, PACK, C1], BF16, "dz3")
+        for t, tag in enumerate(["zwin3_0", "zwin3_1", "zt5", "mask1"]):
+            win = window("zwin3_%d" % t, tag)
+            scatter_z(win, 3, t, 0, C1)
+            round_z(dz, win, 3, t)
+            if t == 1:
+                quantise_and_multiply(0, da0)
+                da1 = slot("da1", [P, 2 * C1, PACK], BF16, "da")
+                apply_mask(da1, dz2, 2)
+        apply_mask(da1, dz, 3)
+
+        owin = []
+        for c, tag in enumerate(["owin0", "owin1", "dz3", "mask3"]):
+            owin.append(window("owin%d" % c, tag))
+            scatter_dx(owin[c], 0, c)
+            if c == 1:
+                quantise_and_multiply(1, da1)
         for c in range(K // P):
-            scatter_dx(1, c)
+            scatter_dx(owin[c], 1, c)
             nc.sync.dma_start(out[P * c : P * (c + 1), :], owin[c][:])

@@ -37,8 +37,6 @@ def tile_moe_hib_relu_kernel(
         offs_l = keep.tile([P, T // PER_COL], U16, name="offs_l")
         dy_w = keep.tile([P, T], U32, name="dy_w", align_bytes=64)
         dy_s = keep.tile([P, T], U8, name="dy_s", align_bytes=64)
-        gq_w = keep.tile([P, T], U32, name="gq_w", align_bytes=64)
-        gq_s = keep.tile([P, T], U8, name="gq_s", align_bytes=64)
         wet_w = [keep.tile([P, EPG, H], U32, name="wet_w%d" % f, align_bytes=64) for f in range(G)]
         wet_s = [keep.tile([P, H], U8, name="wet_s%d" % h, align_bytes=64) for h in range(2)]
         wgt_w = keep.tile([P, G, K], U32, name="wgt_w", align_bytes=64)
@@ -72,14 +70,15 @@ def tile_moe_hib_relu_kernel(
 
         wet_rows = wet_scales.rearrange("e s b i -> (e s) b i")
         load_list(dst_l, dst)
-        nc.sync.dma_start(gate_rows[:], gate.rearrange("r (e u) -> (r e) u", u=C2)[0:P, :])
         load_planes(dy_s, dy_scales.to_broadcast([8, 16, T]))
         nc.sync.dma_start(dy_w[:].bitcast(I32), dy_words.rearrange("s p t d -> p (s t d)").bitcast(I32))
+        nc.sync.dma_start(gate_rows[:], gate.rearrange("r (e u) -> (r e) u", u=C2)[0:P, :])
         load_wet(0)
         load_planes(wet_s[0], wet_rows)
         load_list(offs2_l, offs2)
+        load_wet(1)
         load_planes(wet_s[1], wet_rows[4:8])
-        for f in range(1, G):
+        for f in range(2, G):
             load_wet(f)
         for f in range(G):
             nc.sync.dma_start(a_sb[f][:], a_p[:, :, C1 * f : C1 * (f + 1)])
@@ -94,35 +93,37 @@ def tile_moe_hib_relu_kernel(
         def cols(lo, hi):
             return slice(lo // PER_COL, hi // PER_COL)
 
-        def gather(lo, hi):
-            nc.vector.tensor_copy(gq_w[:, lo:hi], dy_w[:].indirect(dst_l[:, cols(lo, hi)]))
-            nc.vector.tensor_copy(gq_s[:, lo:hi], dy_s[:].indirect(dst_l[:, cols(lo, hi)]))
-
-        gather(0, C2)
-        gather(C2, C1)
-        gather(C1, T)
-
-        z = [keep.tile([P, PACK, C1], F32, name="z%d" % f) for f in range(G)]
-        dx = [[keep.tile([P, 2 * C1], F32, name="dx%d_%d" % (h, c)) for c in range(K // P)] for h in range(G // 2)]
-
         def slot(name, shape, dtype, tag):
             return keep.tile(shape, dtype, name=name, tag=tag, align_bytes=64)
 
+        def gather(src, dtype, lo, hi, tag):
+            tile = slot(tag, [P, hi - lo], dtype, tag)
+            nc.vector.tensor_copy(tile[:], src[:].indirect(dst_l[:, cols(lo, hi)]))
+            return [tile[:, m - lo : m - lo + C2] for m in range(lo, hi, C2)]
+
+        gq_s = gather(dy_s, U8, 0, T // 2, "gq_s_first")
+        gq_w = gather(dy_w, U32, 0, C2, "gq_w0")
+        gq_w.extend(gather(dy_w, U32, C2, C1, "gq_w1"))
+        gq_w.extend(gather(dy_w, U32, C1, T, "gq_w2"))
+
+        z_first = [keep.tile([P, PACK, C2], F32, name="z_first%d" % h) for h in range(EPG)]
+        z = [None] + [keep.tile([P, PACK, C1], F32, name="z%d" % f) for f in range(1, G)]
+        dx = [[keep.tile([P, 2 * C1], F32, name="dx%d_%d" % (h, c)) for c in range(K // P)] for h in range(G // 2)]
+
         def expert(e):
             f, h = divmod(e, EPG)
-            slots = slice(C2 * e, C2 * (e + 1))
-            zt_ps = psum.tile([P, H], F32, name="zt_ps", tag="first", bufs=1)
+            zt_ps = psum.tile([P, H], F32, name="zt_ps", tag="first" if e == 0 or e % 2 else "second", bufs=1)
             nc.tensor.matmul_mx(
                 out=zt_ps[:],
-                lhsT=gq_w[:, slots].bitcast(FP8X4),
-                lhsT_scale=gq_s[:, slots],
+                lhsT=gq_w[e].bitcast(FP8X4),
+                lhsT_scale=gq_s[e],
                 rhs=wet_w[f][:, h, :].bitcast(FP8X4),
                 rhs_scale=wet_s[e // 4][4 * (e % 4) : P, :],
                 start=True,
                 stop=True,
             )
-            zt = slot("zt", [P, PACK, P], F32, "zt%d" % e)
-            step = PACK // 2 if e == 0 else PACK
+            zt = slot("zt", [P, PACK, P], F32, "zt%d" % (0 if e == 2 else e))
+            step = 1 if e == 0 else PACK
             for t0 in range(0, PACK, step):
                 ts = slice(t0, t0 + step)
                 nc.scalar.activation(
@@ -134,17 +135,21 @@ def tile_moe_hib_relu_kernel(
                 z_ps = psum.tile([P, step, C2], F32, name="z_ps", tag="z")
                 for t in range(step):
                     nc.tensor.transpose(z_ps[:, t, :], zt[:, t0 + t, :], ident[:])
-                nc.scalar.copy(z[f][:, ts, C2 * h : C2 * (h + 1)], z_ps[:])
+                if f == 0:
+                    nc.scalar.copy(z_first[h][:, ts, :], z_ps[:])
+                else:
+                    nc.scalar.copy(z[f][:, ts, C2 * h : C2 * (h + 1)], z_ps[:])
 
         def scatter_z(win, f, t, lo, hi):
-            nc.vector.tensor_copy(win[:].indirect(offs2_l[:, cols(C1 * f + lo, C1 * f + hi)]), z[f][:, t, lo:hi])
+            src = z_first[lo // C2] if f == 0 else z[f]
+            nc.vector.tensor_copy(win[:].indirect(offs2_l[:, cols(C1 * f + lo, C1 * f + hi)]), src[:, t, :])
 
         def round_z(dz, win, f, t):
             nc.scalar.copy(dz[:, t, :], win[:, C1 * f : C1 * (f + 1)])
 
         def make_mask(f):
             mask = slot("mask%d" % f, [P, C1, PACK], BF16, "mask%d" % f)
-            sign = slot("sign", [P, C1, PACK], BF16, "wet_w1")
+            sign = slot("sign", [P, C1, PACK], BF16, "zt4")
             nc.scalar.activation(sign[:], a_sb[f][:].rearrange("p t j -> p j t"), ACT.Sign)
             nc.scalar.activation(mask[:], sign[:], ACT.Relu)
             return mask
@@ -179,7 +184,9 @@ def tile_moe_hib_relu_kernel(
         def window(name, tag):
             return slot(name, [P, T], F32, tag)
 
-        for e in range(E):
+        expert(0)
+        gq_s.extend(gather(dy_s, U8, T // 2, T, "gq_w0"))
+        for e in range(1, E):
             expert(e)
 
         relu_mask = [make_mask(f) for f in range(2)]

@@ -26,41 +26,40 @@ def tile_moe_hib_relu_kernel(
     tc, dy_words, dy_scales, wet_words, wet_scales, wgt_words, wgt_scales, a, gate, offs, offs2, dst, out
 ):
     nc = tc.nc
+    HALF = T // 2
+    EARLY = 5 * C2
 
     with ExitStack() as ctx:
         keep = ctx.enter_context(tc.tile_pool(name="keep", bufs=1))
-        ring = ctx.enter_context(tc.tile_pool(name="ring", bufs=2))
         psum = ctx.enter_context(tc.psum_pool(name="psum", bufs=2))
+
+        def slot(name, shape, dtype, tag=None):
+            return keep.tile(shape, dtype, name=name, tag=tag or name, align_bytes=64)
 
         dst_l = keep.tile([P, T // PER_COL], U16, name="dst_l")
         offs2_l = keep.tile([P, T // PER_COL], U16, name="offs2_l")
         offs_l = keep.tile([P, T // PER_COL], U16, name="offs_l")
-        dy_w = keep.tile([P, T], U32, name="dy_w", align_bytes=64)
-        dy_s = keep.tile([P, T], U8, name="dy_s", align_bytes=64)
-        wet_w = [keep.tile([P, EPG, H], U32, name="wet_w%d" % f, align_bytes=64) for f in range(G)]
-        wet_s = [keep.tile([P, H], U8, name="wet_s%d" % h, align_bytes=64) for h in range(2)]
-        wgt_w = keep.tile([P, G, K], U32, name="wgt_w", align_bytes=64)
-        wgt_s = keep.tile([P, K], U8, name="wgt_s", align_bytes=64)
-        a_sb = [keep.tile([P, PACK, C1], F32, name="a_sb%d" % f) for f in range(G)]
-        gate_rows = keep.tile([P, C2], F32, name="gate_rows")
-        gate_col = keep.tile([P, E], F32, name="gate_col")
-        ident0 = keep.tile([P, P], F32, name="ident0")
-        ident = keep.tile([P, P], F32, name="ident")
+        dy_w = slot("dy_w", [P, T], U32)
+        dy_s = slot("dy_s", [P, T], U8)
+        wet_w = [slot("wet_w%d" % f, [P, EPG, H], U32) for f in range(G)]
+        wet_s = [slot("wet_s%d" % h, [P, H], U8) for h in range(2)]
+        wgt_w = slot("wgt_w", [P, G, K], U32)
+        wgt_s = slot("wgt_s", [P, K], U8)
+        a_sb = [slot("a_sb%d" % h, [P, PACK, HALF], F32) for h in range(2)]
+        gate_rows = slot("gate_rows", [P, C2], F32)
+        gate_col = slot("gate_col", [P, E], F32)
+        ident = slot("ident", [P, P], F32)
 
-        def load_list(tile, src):
-            nc.sync.dma_start(tile[:], src)
-
-        def load_planes(tile, rows):
+        def load_planes(queue, tile, rows):
             n = rows.shape[0]
             for q in range(4):
-                nc.sync.dma_start(
+                queue.dma_start(
                     tile[32 * q : 32 * q + 4 * n, :].bitcast(I32), rows[:, 4 * q : 4 * q + 4, :].bitcast(I32)
                 )
 
-        make_identity(nc, ident0[:])
+        make_identity(nc, ident[:])
         nc.gpsimd.memset(wet_s[1][:].bitcast(I32), 0)
         nc.gpsimd.memset(wgt_s[:].bitcast(I32), 0)
-        nc.scalar.copy(ident[:], ident0[:])
 
         wet_words_p = wet_words.rearrange("e s p i d -> p (e s) (i d)")
         a_p = a.rearrange("(p t) j -> p t j", t=PACK)
@@ -69,102 +68,98 @@ def tile_moe_hib_relu_kernel(
             nc.sync.dma_start(wet_w[f][:].bitcast(I32), wet_words_p[:, EPG * f : EPG * (f + 1), :].bitcast(I32))
 
         wet_rows = wet_scales.rearrange("e s b i -> (e s) b i")
-        load_list(dst_l, dst)
-        load_planes(dy_s, dy_scales.to_broadcast([8, 16, T]))
+        nc.sync.dma_start(dst_l[:], dst)
+        load_planes(nc.sync, dy_s, dy_scales.to_broadcast([8, 16, T]))
         nc.sync.dma_start(dy_w[:].bitcast(I32), dy_words.rearrange("s p t d -> p (s t d)").bitcast(I32))
         nc.sync.dma_start(gate_rows[:], gate.rearrange("r (e u) -> (r e) u", u=C2)[0:P, :])
         load_wet(0)
-        load_planes(wet_s[0], wet_rows)
-        load_list(offs2_l, offs2)
+        load_planes(nc.sync, wet_s[0], wet_rows)
+        nc.sync.dma_start(offs2_l[:], offs2)
         load_wet(1)
-        load_planes(wet_s[1], wet_rows[4:8])
+        load_planes(nc.sync, wet_s[1], wet_rows[4:8])
         for f in range(2, G):
             load_wet(f)
-        for f in range(G):
-            nc.sync.dma_start(a_sb[f][:], a_p[:, :, C1 * f : C1 * (f + 1)])
-        load_planes(wgt_s, wgt_scales.rearrange("f s b k -> (f s) b k"))
+        for h in range(2):
+            nc.sync.dma_start(a_sb[h][:], a_p[:, :, HALF * h : HALF * (h + 1)])
+        load_planes(nc.sync, wgt_s, wgt_scales.rearrange("f s b k -> (f s) b k"))
         nc.sync.dma_start(wgt_w[:].bitcast(I32), wgt_words.rearrange("f s p k d -> p (f s) (k d)").bitcast(I32))
-        load_list(offs_l, offs)
+        nc.sync.dma_start(offs_l[:], offs)
 
-        gate_ps = psum.tile([P, P], F32, name="gate_ps", tag="first", bufs=1)
+        gate_ps = psum.tile([P, P], F32, name="gate_ps", tag="dx", bufs=3)
         nc.tensor.transpose(gate_ps[:], gate_rows[:], ident[:])
         nc.scalar.copy(gate_col[:], gate_ps[:, 0:E])
 
         def cols(lo, hi):
             return slice(lo // PER_COL, hi // PER_COL)
 
-        def slot(name, shape, dtype, tag):
-            return keep.tile(shape, dtype, name=name, tag=tag, align_bytes=64)
-
         def gather(src, dtype, lo, hi, tag):
-            tile = slot(tag, [P, hi - lo], dtype, tag)
+            tile = slot("gq_%d_%d" % (lo, hi), [P, hi - lo], dtype, tag)
             nc.vector.tensor_copy(tile[:], src[:].indirect(dst_l[:, cols(lo, hi)]))
             return [tile[:, m - lo : m - lo + C2] for m in range(lo, hi, C2)]
 
-        gq_s = gather(dy_s, U8, 0, T // 2, "gq_s_first")
-        gq_w = gather(dy_w, U32, 0, C2, "gq_w0")
-        gq_w.extend(gather(dy_w, U32, C2, C1, "gq_w1"))
-        gq_w.extend(gather(dy_w, U32, C1, T, "gq_w2"))
+        gq_s = gather(dy_s, U8, 0, EARLY, "gq_s_first")
+        gq_w = gather(dy_w, U32, 0, C1, "gq_w0")
+        gq_w.extend(gather(dy_w, U32, C1, T, "gq_w1"))
 
-        z_first = [keep.tile([P, PACK, C2], F32, name="z_first%d" % h) for h in range(EPG)]
-        z = [None] + [keep.tile([P, PACK, C1], F32, name="z%d" % f) for f in range(1, G)]
-        dx = [[keep.tile([P, 2 * C1], F32, name="dx%d_%d" % (h, c)) for c in range(K // P)] for h in range(G // 2)]
+        zt = [slot("zt%d" % e, [P, PACK, C2], F32) for e in range(E)]
+        zt_ps = {}
 
-        def expert(e):
-            f, h = divmod(e, EPG)
-            zt_ps = psum.tile([P, H], F32, name="zt_ps", tag="first" if e == 0 or e % 2 else "second", bufs=1)
+        def product(e):
+            f, u = divmod(e, EPG)
+            zt_ps[e] = psum.tile([P, H], F32, name="zt_ps", tag="zt")
             nc.tensor.matmul_mx(
-                out=zt_ps[:],
+                out=zt_ps[e][:],
                 lhsT=gq_w[e].bitcast(FP8X4),
                 lhsT_scale=gq_s[e],
-                rhs=wet_w[f][:, h, :].bitcast(FP8X4),
+                rhs=wet_w[f][:, u, :].bitcast(FP8X4),
                 rhs_scale=wet_s[e // 4][4 * (e % 4) : P, :],
                 start=True,
                 stop=True,
             )
-            zt = slot("zt", [P, PACK, P], F32, "zt%d" % (0 if e == 2 else e))
-            step = 1 if e == 0 else PACK
-            for t0 in range(0, PACK, step):
-                ts = slice(t0, t0 + step)
-                nc.scalar.activation(
-                    zt[:, ts, :],
-                    zt_ps[:].rearrange("m (p t) -> m t p", t=PACK)[:, ts, :],
-                    ACT.Copy,
-                    scale=gate_col[:, e : e + 1],
-                )
-                z_ps = psum.tile([P, step, C2], F32, name="z_ps", tag="z")
-                for t in range(step):
-                    nc.tensor.transpose(z_ps[:, t, :], zt[:, t0 + t, :], ident[:])
-                if f == 0:
-                    nc.scalar.copy(z_first[h][:, ts, :], z_ps[:])
-                else:
-                    nc.scalar.copy(z[f][:, ts, C2 * h : C2 * (h + 1)], z_ps[:])
 
-        def scatter_z(win, f, t, lo, hi):
-            src = z_first[lo // C2] if f == 0 else z[f]
-            nc.vector.tensor_copy(win[:].indirect(offs2_l[:, cols(C1 * f + lo, C1 * f + hi)]), src[:, t, :])
+        def gate_and_sort(e, t0, t1):
+            nc.scalar.activation(
+                zt[e][:, t0:t1, :],
+                zt_ps[e][:].rearrange("m (p t) -> m t p", t=PACK)[:, t0:t1, :],
+                ACT.Copy,
+                scale=gate_col[:, e : e + 1],
+            )
 
-        def round_z(dz, win, f, t):
-            nc.scalar.copy(dz[:, t, :], win[:, C1 * f : C1 * (f + 1)])
+        def turn(t, e0, e1):
+            z_ps = psum.tile([P, (e1 - e0) * C2], F32, name="z_ps", tag="z", bufs=3)
+            for e in range(e0, e1):
+                nc.tensor.transpose(z_ps[:, C2 * (e - e0) : C2 * (e - e0 + 1)], zt[e][:, t, :], ident[:])
+            z = slot("z%d_%d" % (t, e0), [P, (e1 - e0) * C2], F32)
+            nc.scalar.copy(z[:], z_ps[:])
+            return z
 
-        def make_mask(f):
-            mask = slot("mask%d" % f, [P, C1, PACK], BF16, "mask%d" % f)
-            sign = slot("sign", [P, C1, PACK], BF16, "zt4")
-            nc.scalar.activation(sign[:], a_sb[f][:].rearrange("p t j -> p j t"), ACT.Sign)
+        def scatter_z(win, z, e0, e1):
+            nc.vector.tensor_copy(win[:].indirect(offs2_l[:, cols(C2 * e0, C2 * e1)]), z[:])
+
+        def make_mask(h, t):
+            sign = keep.tile([P, HALF], BF16, name="sign", bufs=2)
+            mask = slot("mask%d_%d" % (h, t), [P, HALF], BF16)
+            nc.scalar.activation(sign[:], a_sb[h][:, t, :], ACT.Sign)
             nc.scalar.activation(mask[:], sign[:], ACT.Relu)
             return mask
 
-        def apply_mask(da, dz, f):
-            js = slice(C1 * (f % 2), C1 * (f % 2 + 1))
-            nc.gpsimd.tensor_tensor(da[:, js, :], dz[:].rearrange("p t j -> p j t"), relu_mask[f][:], MULT)
+        def apply_mask(planar, win, mask, h, t):
+            nc.gpsimd.tensor_tensor(planar[:, t, :], win[:, HALF * h : HALF * (h + 1)], mask[:], MULT)
+
+        def interleave(h, planar, tag):
+            da = slot("da%d" % h, [P, HALF, PACK], BF16, tag)
+            nc.scalar.copy(da[:], planar[:].rearrange("p t j -> p j t"))
+            return da
+
+        dx = [[slot("dx%d_%d" % (h, c), [P, HALF], F32) for c in range(K // P)] for h in range(2)]
 
         def quantise_and_multiply(h, da):
-            da_w = ring.tile([P, 2 * C1], U32, name="da_w", align_bytes=64)
-            da_s = ring.tile([P, 2 * C1], U8, name="da_s", align_bytes=64)
+            da_w = slot("da_w%d" % h, [P, HALF], U32)
+            da_s = slot("da_s%d" % h, [P, HALF], U8)
             nc.vector.quantize_mx(out=da_w[:].bitcast(FP8X4), scales=da_s[:], in_=da[:].rearrange("p j t -> p (j t)"))
             for c in range(K // P):
                 ks = slice(P * c, P * (c + 1))
-                dx_ps = psum.tile([P, 2 * C1], F32, name="dx_ps", tag="dx", bufs=3)
+                dx_ps = psum.tile([P, HALF], F32, name="dx_ps", tag="dx", bufs=3)
                 for u in range(2):
                     js = slice(C1 * u, C1 * (u + 1))
                     nc.tensor.matmul_mx(
@@ -179,59 +174,56 @@ def tile_moe_hib_relu_kernel(
                 nc.scalar.copy(dx[h][c][:], dx_ps[:])
 
         def scatter_dx(win, h, c):
-            nc.vector.tensor_copy(win[:].indirect(offs_l[:, cols(2 * C1 * h, 2 * C1 * (h + 1))]), dx[h][c][:])
+            nc.vector.tensor_copy(win[:].indirect(offs_l[:, cols(HALF * h, HALF * (h + 1))]), dx[h][c][:])
 
-        def window(name, tag):
+        def window(name, tag=None):
             return slot(name, [P, T], F32, tag)
 
-        expert(0)
-        gq_s.extend(gather(dy_s, U8, T // 2, T, "gq_w0"))
-        for e in range(1, E):
-            expert(e)
+        product(0)
+        product(1)
+        gq_s.extend(gather(dy_s, U8, EARLY, T, "gq_w0"))
+        wins = [window("zwin0_%d" % t) for t in range(PACK)]
+        gate_and_sort(0, 0, 1)
+        scatter_z(wins[0], turn(0, 0, 1), 0, 1)
+        gate_and_sort(0, 1, PACK)
+        scatter_z(wins[1], turn(1, 0, 1), 0, 1)
+        gate_and_sort(1, 0, PACK)
+        for t in (2, 3):
+            scatter_z(wins[t], turn(t, 0, 2), 0, 2)
+        for e in range(2, 4):
+            product(e)
+            gate_and_sort(e, 0, PACK)
+        for t in (0, 1):
+            scatter_z(wins[t], turn(t, 1, 4), 1, 4)
+        for t in (2, 3):
+            scatter_z(wins[t], turn(t, 2, 4), 2, 4)
 
-        relu_mask = [make_mask(f) for f in range(2)]
-
-        da0 = slot("da0", [P, 2 * C1, PACK], BF16, "da")
-        dz = slot("dz0", [P, PACK, C1], BF16, "zt3")
-        wins = [window("zwin0_%d" % t, "zwin0_%d" % t) for t in range(PACK)]
+        for e in range(4, E):
+            product(e)
+            gate_and_sort(e, 0, PACK)
+        z_late = [turn(0, 4, E)]
+        planar0 = slot("planar0", [P, PACK, HALF], BF16)
         for t in range(PACK):
-            scatter_z(wins[t], 0, t, 0, C2)
-        for t in range(PACK):
-            scatter_z(wins[t], 0, t, C2, C1)
-            round_z(dz, wins[t], 0, t)
-        apply_mask(da0, dz, 0)
+            apply_mask(planar0, wins[t], make_mask(0, t), 0, t)
+        z_late.extend(turn(t, 4, E) for t in range(1, PACK))
+        mask_late = [make_mask(1, t) for t in range(PACK)]
+        da0 = interleave(0, planar0, "da0")
 
-        dz = slot("dz1", [P, PACK, C1], BF16, "zt5")
+        planar1 = slot("planar1", [P, PACK, HALF], BF16)
         for t in range(PACK):
-            win = window("zwin1_%d" % t, "zwin1_%d" % t)
-            scatter_z(win, 1, t, 0, C1)
-            round_z(dz, win, 1, t)
-        apply_mask(da0, dz, 1)
-
-        relu_mask.extend(make_mask(f) for f in range(2, G))
-        dz2 = slot("dz2", [P, PACK, C1], BF16, "zt7")
-        for t in range(PACK):
-            win = window("zwin2_%d" % t, "zwin2_%d" % t)
-            scatter_z(win, 2, t, 0, C1)
-            round_z(dz2, win, 2, t)
-
-        dz = slot("dz3", [P, PACK, C1], BF16, "dz3")
-        for t, tag in enumerate(["zwin3_0", "zwin3_1", "zt5", "mask1"]):
-            win = window("zwin3_%d" % t, tag)
-            scatter_z(win, 3, t, 0, C1)
-            round_z(dz, win, 3, t)
-            if t == 1:
+            if t == PACK - 1:
                 quantise_and_multiply(0, da0)
-                da1 = slot("da1", [P, 2 * C1, PACK], BF16, "da")
-                apply_mask(da1, dz2, 2)
-        apply_mask(da1, dz, 3)
+            win = window("zwin1_%d" % t, "planar0" if t == PACK - 1 else None)
+            scatter_z(win, z_late[t], 4, E)
+            apply_mask(planar1, win, mask_late[t], 1, t)
+        da1 = interleave(1, planar1, "da_w0")
 
         owin = []
-        for c, tag in enumerate(["owin0", "owin1", "dz3", "mask3"]):
-            owin.append(window("owin%d" % c, tag))
-            scatter_dx(owin[c], 0, c)
-            if c == 1:
+        for c in range(K // P):
+            if c == K // P - 1:
                 quantise_and_multiply(1, da1)
+            owin.append(window("owin%d" % c, "planar1" if c == K // P - 1 else None))
+            scatter_dx(owin[c], 0, c)
         for c in range(K // P):
             scatter_dx(owin[c], 1, c)
             nc.sync.dma_start(out[P * c : P * (c + 1), :], owin[c][:])

@@ -50,10 +50,10 @@ def tile_moe_hib_relu_kernel(
         gate_col = slot("gate_col", [P, E], F32)
         ident = slot("ident", [P, P], F32)
 
-        def load_planes(queue, tile, rows):
+        def load_planes(queues, tile, rows):
             n = rows.shape[0]
             for q in range(4):
-                queue.dma_start(
+                queues[q % len(queues)].dma_start(
                     tile[32 * q : 32 * q + 4 * n, :].bitcast(I32), rows[:, 4 * q : 4 * q + 4, :].bitcast(I32)
                 )
 
@@ -69,19 +69,19 @@ def tile_moe_hib_relu_kernel(
 
         wet_rows = wet_scales.rearrange("e s b i -> (e s) b i")
         nc.sync.dma_start(dst_l[:], dst)
-        load_planes(nc.sync, dy_s, dy_scales.to_broadcast([8, 16, T]))
+        load_planes([nc.scalar, nc.sync], dy_s, dy_scales.to_broadcast([8, 16, T]))
         nc.sync.dma_start(dy_w[:].bitcast(I32), dy_words.rearrange("s p t d -> p (s t d)").bitcast(I32))
         nc.sync.dma_start(gate_rows[:], gate.rearrange("r (e u) -> (r e) u", u=C2)[0:P, :])
         load_wet(0)
-        load_planes(nc.sync, wet_s[0], wet_rows)
+        load_planes([nc.sync], wet_s[0], wet_rows)
         nc.sync.dma_start(offs2_l[:], offs2)
         load_wet(1)
-        load_planes(nc.sync, wet_s[1], wet_rows[4:8])
+        load_planes([nc.sync], wet_s[1], wet_rows[4:8])
         for f in range(2, G):
             load_wet(f)
         for h in range(2):
             nc.sync.dma_start(a_sb[h][:], a_p[:, :, HALF * h : HALF * (h + 1)])
-        load_planes(nc.sync, wgt_s, wgt_scales.rearrange("f s b k -> (f s) b k"))
+        load_planes([nc.sync], wgt_s, wgt_scales.rearrange("f s b k -> (f s) b k"))
         nc.sync.dma_start(wgt_w[:].bitcast(I32), wgt_words.rearrange("f s p k d -> p (f s) (k d)").bitcast(I32))
         nc.sync.dma_start(offs_l[:], offs)
 
@@ -126,11 +126,13 @@ def tile_moe_hib_relu_kernel(
             )
 
         def turn(t, e0, e1):
-            z_ps = psum.tile([P, (e1 - e0) * C2], F32, name="z_ps", tag="z", bufs=3)
-            for e in range(e0, e1):
-                nc.tensor.transpose(z_ps[:, C2 * (e - e0) : C2 * (e - e0 + 1)], zt[e][:, t, :], ident[:])
             z = slot("z%d_%d" % (t, e0), [P, (e1 - e0) * C2], F32)
-            nc.scalar.copy(z[:], z_ps[:])
+            for b0 in range(e0, e1, PACK):
+                b1 = min(b0 + PACK, e1)
+                z_ps = psum.tile([P, (b1 - b0) * C2], F32, name="z_ps", tag="z", bufs=3)
+                for e in range(b0, b1):
+                    nc.tensor.transpose(z_ps[:, C2 * (e - b0) : C2 * (e - b0 + 1)], zt[e][:, t, :], ident[:])
+                nc.scalar.copy(z[:, C2 * (b0 - e0) : C2 * (b1 - e0)], z_ps[:])
             return z
 
         def scatter_z(win, z, e0, e1):
@@ -143,15 +145,14 @@ def tile_moe_hib_relu_kernel(
             nc.scalar.activation(mask[:], sign[:], ACT.Relu)
             return mask
 
-        def apply_mask(planar, win, mask, h, t):
-            nc.gpsimd.tensor_tensor(planar[:, t, :], win[:, HALF * h : HALF * (h + 1)], mask[:], MULT)
+        def apply_mask(planes, win, f, t):
+            js = slice(C1 * (f % 2), C1 * (f % 2 + 1))
+            nc.gpsimd.tensor_tensor(planes[:, t, :], win[:, C1 * f : C1 * (f + 1)], mask[f // 2][t][:, js], MULT)
 
-        def interleave(h, planar, tag):
-            da = slot("da%d" % h, [P, HALF, PACK], BF16, tag)
-            nc.scalar.copy(da[:], planar[:].rearrange("p t j -> p j t"))
-            return da
+        def interleave(da, planes, f):
+            nc.scalar.copy(da[:, C1 * (f % 2) : C1 * (f % 2 + 1), :], planes[:].rearrange("p t j -> p j t"))
 
-        dx = [[slot("dx%d_%d" % (h, c), [P, HALF], F32) for c in range(K // P)] for h in range(2)]
+        dx = [slot("dx%d" % c, [P, T], F32) for c in range(K // P)]
 
         def quantise_and_multiply(h, da):
             da_w = slot("da_w%d" % h, [P, HALF], U32)
@@ -171,10 +172,10 @@ def tile_moe_hib_relu_kernel(
                         start=True,
                         stop=True,
                     )
-                nc.scalar.copy(dx[h][c][:], dx_ps[:])
+                nc.scalar.copy(dx[c][:, HALF * h : HALF * (h + 1)], dx_ps[:])
 
-        def scatter_dx(win, h, c):
-            nc.vector.tensor_copy(win[:].indirect(offs_l[:, cols(HALF * h, HALF * (h + 1))]), dx[h][c][:])
+        def scatter_dx(win, c, lo, hi):
+            nc.vector.tensor_copy(win[:].indirect(offs_l[:, cols(lo, hi)]), dx[c][:, lo:hi])
 
         def window(name, tag=None):
             return slot(name, [P, T], F32, tag)
@@ -182,7 +183,7 @@ def tile_moe_hib_relu_kernel(
         product(0)
         product(1)
         gq_s.extend(gather(dy_s, U8, EARLY, T, "gq_w0"))
-        wins = [window("zwin0_%d" % t) for t in range(PACK)]
+        wins = [window("zwin%d" % t) for t in range(PACK)]
         gate_and_sort(0, 0, 1)
         scatter_z(wins[0], turn(0, 0, 1), 0, 1)
         gate_and_sort(0, 1, PACK)
@@ -195,35 +196,45 @@ def tile_moe_hib_relu_kernel(
             gate_and_sort(e, 0, PACK)
         for t in (0, 1):
             scatter_z(wins[t], turn(t, 1, 4), 1, 4)
-        for t in (2, 3):
-            scatter_z(wins[t], turn(t, 2, 4), 2, 4)
-
         for e in range(4, E):
             product(e)
             gate_and_sort(e, 0, PACK)
-        z_late = [turn(0, 4, E)]
-        planar0 = slot("planar0", [P, PACK, HALF], BF16)
-        for t in range(PACK):
-            apply_mask(planar0, wins[t], make_mask(0, t), 0, t)
-        z_late.extend(turn(t, 4, E) for t in range(1, PACK))
-        mask_late = [make_mask(1, t) for t in range(PACK)]
-        da0 = interleave(0, planar0, "da0")
+        late = [window("zlate%d" % t) for t in (2, 3)]
+        for t in (2, 3):
+            scatter_z(late[t - 2], turn(t, 2, E), 2, E)
+        z_last = [turn(t, 4, E) for t in (0, 1)]
+        mask = [[make_mask(h, t) for t in range(PACK)] for h in range(2)]
 
-        planar1 = slot("planar1", [P, PACK, HALF], BF16)
-        for t in range(PACK):
-            if t == PACK - 1:
-                quantise_and_multiply(0, da0)
-            win = window("zwin1_%d" % t, "planar0" if t == PACK - 1 else None)
-            scatter_z(win, z_late[t], 4, E)
-            apply_mask(planar1, win, mask_late[t], 1, t)
-        da1 = interleave(1, planar1, "da_w0")
+        da0 = slot("da0", [P, HALF, PACK], BF16)
+        planar = [slot("planar%d" % f, [P, PACK, C1], BF16) for f in range(G)]
+        for t in (2, 3, 0, 1):
+            apply_mask(planar[0], wins[t], 0, t)
+        interleave(da0, planar[0], 0)
+        for t, win in enumerate(wins[:2] + late):
+            apply_mask(planar[1], win, 1, t)
+        interleave(da0, planar[1], 1)
+        for f in (2, 3):
+            for t in (2, 3):
+                apply_mask(planar[f], late[t - 2], f, t)
 
-        owin = []
+        last = [window("zlast0")]
+        scatter_z(last[0], z_last[0], 4, E)
+        quantise_and_multiply(0, da0)
+        last.append(window("zlast1", "planar1"))
+        scatter_z(last[1], z_last[1], 4, E)
+        da1 = slot("da1", [P, HALF, PACK], BF16, "da_w0")
+        for t in (0, 1):
+            for f in (2, 3):
+                apply_mask(planar[f], last[t], f, t)
+        for f in (2, 3):
+            interleave(da1, planar[f], f)
+
+        owin = [slot("owin0", [P, 2 * T], F32), window("owin1"), window("owin2")]
+        for c in (1, 2):
+            scatter_dx(owin[c], c, 0, HALF)
+        quantise_and_multiply(1, da1)
+        owin.append(window("owin3", "planar3"))
+        scatter_dx(owin[3], 3, 0, HALF)
         for c in range(K // P):
-            if c == K // P - 1:
-                quantise_and_multiply(1, da1)
-            owin.append(window("owin%d" % c, "planar1" if c == K // P - 1 else None))
-            scatter_dx(owin[c], 0, c)
-        for c in range(K // P):
-            scatter_dx(owin[c], 1, c)
-            nc.sync.dma_start(out[P * c : P * (c + 1), :], owin[c][:])
+            scatter_dx(owin[c], c, HALF if c else 0, T)
+            nc.sync.dma_start(out[P * c : P * (c + 1), :], owin[c][:, 0:T])

@@ -145,12 +145,17 @@ def tile_moe_hib_relu_kernel(
             nc.scalar.activation(mask[:], sign[:], ACT.Relu)
             return mask
 
-        def apply_mask(planes, win, f, t):
-            js = slice(C1 * (f % 2), C1 * (f % 2 + 1))
-            nc.gpsimd.tensor_tensor(planes[:, t, :], win[:, C1 * f : C1 * (f + 1)], mask[f // 2][t][:, js], MULT)
+        def in_half(lo, hi):
+            h = lo // HALF
+            return h, slice(lo - HALF * h, hi - HALF * h)
 
-        def interleave(da, planes, f):
-            nc.scalar.copy(da[:, C1 * (f % 2) : C1 * (f % 2 + 1), :], planes[:].rearrange("p t j -> p j t"))
+        def apply_mask(win, t, lo, hi):
+            h, js = in_half(lo, hi)
+            nc.gpsimd.tensor_tensor(planar[h][:, t, js], win[:, lo:hi], mask[h][t][:, js], MULT)
+
+        def interleave(da, lo, hi):
+            h, js = in_half(lo, hi)
+            nc.scalar.copy(da[:, js, :], planar[h][:, :, js].rearrange("p t j -> p j t"))
 
         dx = [slot("dx%d" % c, [P, T], F32) for c in range(K // P)]
 
@@ -206,34 +211,32 @@ def tile_moe_hib_relu_kernel(
         mask = [[make_mask(h, t) for t in range(PACK)] for h in range(2)]
 
         da0 = slot("da0", [P, HALF, PACK], BF16)
-        planar = [slot("planar%d" % f, [P, PACK, C1], BF16) for f in range(G)]
-        for t in (2, 3, 0, 1):
-            apply_mask(planar[0], wins[t], 0, t)
-        interleave(da0, planar[0], 0)
-        for t, win in enumerate(wins[:2] + late):
-            apply_mask(planar[1], win, 1, t)
-        interleave(da0, planar[1], 1)
-        for f in (2, 3):
-            for t in (2, 3):
-                apply_mask(planar[f], late[t - 2], f, t)
+        planar = [slot("planar%d" % h, [P, PACK, HALF], BF16) for h in range(2)]
+        for t in (2, 3):
+            apply_mask(wins[t], t, 0, C1)
+        for t in (0, 1):
+            apply_mask(wins[t], t, 0, HALF)
+        interleave(da0, 0, C1)
+        for t in (2, 3):
+            apply_mask(late[t - 2], t, C1, HALF)
+            apply_mask(late[t - 2], t, HALF, T)
+        interleave(da0, C1, HALF)
 
         last = [window("zlast0")]
         scatter_z(last[0], z_last[0], 4, E)
         quantise_and_multiply(0, da0)
-        last.append(window("zlast1", "planar1"))
+        last.append(window("zlast1", "planar0"))
         scatter_z(last[1], z_last[1], 4, E)
         da1 = slot("da1", [P, HALF, PACK], BF16, "da_w0")
         for t in (0, 1):
-            for f in (2, 3):
-                apply_mask(planar[f], last[t], f, t)
-        for f in (2, 3):
-            interleave(da1, planar[f], f)
+            apply_mask(last[t], t, HALF, T)
+        interleave(da1, HALF, T)
 
         owin = [slot("owin0", [P, 2 * T], F32), window("owin1"), window("owin2")]
         for c in (1, 2):
             scatter_dx(owin[c], c, 0, HALF)
         quantise_and_multiply(1, da1)
-        owin.append(window("owin3", "planar3"))
+        owin.append(window("owin3", "planar1"))
         scatter_dx(owin[3], 3, 0, HALF)
         for c in range(K // P):
             scatter_dx(owin[c], c, HALF if c else 0, T)

@@ -46,7 +46,6 @@ def tile_moe_hib_relu_kernel(
         wgt_w = slot("wgt_w", [P, G, K], U32)
         wgt_s = slot("wgt_s", [P, K], U8)
         a_sb = [slot("a_sb%d" % h, [P, PACK, HALF], F32) for h in range(2)]
-        gate_rows = slot("gate_rows", [P, C2], F32)
         gate_col = slot("gate_col", [P, E], F32)
         ident = slot("ident", [P, P], F32)
 
@@ -57,7 +56,9 @@ def tile_moe_hib_relu_kernel(
                     tile[32 * q : 32 * q + 4 * n, :].bitcast(I32), rows[:, 4 * q : 4 * q + 4, :].bitcast(I32)
                 )
 
-        make_identity(nc, ident[:])
+        ident0 = slot("ident0", [P, P], F32)
+        make_identity(nc, ident0[:])
+        nc.scalar.copy(ident[:], ident0[:])
         nc.gpsimd.memset(wet_s[1][:].bitcast(I32), 0)
         nc.gpsimd.memset(wgt_s[:].bitcast(I32), 0)
 
@@ -71,9 +72,10 @@ def tile_moe_hib_relu_kernel(
         nc.sync.dma_start(dst_l[:], dst)
         load_planes([nc.scalar, nc.sync], dy_s, dy_scales.to_broadcast([8, 16, T]))
         nc.sync.dma_start(dy_w[:].bitcast(I32), dy_words.rearrange("s p t d -> p (s t d)").bitcast(I32))
-        nc.sync.dma_start(gate_rows[:], gate.rearrange("r (e u) -> (r e) u", u=C2)[0:P, :])
         load_wet(0)
         load_planes([nc.sync], wet_s[0], wet_rows)
+        with nc.allow_non_contiguous_dma(reason="one weight a partition and expert"):
+            nc.sync.dma_start(gate_col[:], gate[0:1, :].rearrange("r (e u) -> u (r e)", u=C2))
         nc.sync.dma_start(offs2_l[:], offs2)
         load_wet(1)
         load_planes([nc.sync], wet_s[1], wet_rows[4:8])
@@ -84,10 +86,6 @@ def tile_moe_hib_relu_kernel(
         load_planes([nc.sync], wgt_s, wgt_scales.rearrange("f s b k -> (f s) b k"))
         nc.sync.dma_start(wgt_w[:].bitcast(I32), wgt_words.rearrange("f s p k d -> p (f s) (k d)").bitcast(I32))
         nc.sync.dma_start(offs_l[:], offs)
-
-        gate_ps = psum.tile([P, P], F32, name="gate_ps", tag="dx", bufs=3)
-        nc.tensor.transpose(gate_ps[:], gate_rows[:], ident[:])
-        nc.scalar.copy(gate_col[:], gate_ps[:, 0:E])
 
         def cols(lo, hi):
             return slice(lo // PER_COL, hi // PER_COL)

@@ -41,7 +41,7 @@ def tile_moe_hib_relu_kernel(
         offs_l = keep.tile([P, T // PER_COL], U16, name="offs_l")
         dy_w = slot("dy_w", [P, T], U32)
         dy_s = slot("dy_s", [P, T], U8)
-        wet_w = [slot("wet_w%d" % f, [P, EPG, H], U32) for f in range(G)]
+        wet_w = []
         wet_s = [slot("wet_s%d" % h, [P, H], U8) for h in range(2)]
         wgt_w = slot("wgt_w", [P, G, K], U32)
         wgt_s = slot("wgt_s", [P, K], U8)
@@ -65,22 +65,24 @@ def tile_moe_hib_relu_kernel(
         wet_words_p = wet_words.rearrange("e s p i d -> p (e s) (i d)")
         a_p = a.rearrange("(p t) j -> p t j", t=PACK)
 
-        def load_wet(f):
-            nc.sync.dma_start(wet_w[f][:].bitcast(I32), wet_words_p[:, EPG * f : EPG * (f + 1), :].bitcast(I32))
+        def load_wet(e0, e1):
+            tile = slot("wet_w%d" % e0, [P, e1 - e0, H], U32)
+            nc.sync.dma_start(tile[:].bitcast(I32), wet_words_p[:, e0:e1, :].bitcast(I32))
+            wet_w.extend(tile[:, u, :] for u in range(e1 - e0))
 
         wet_rows = wet_scales.rearrange("e s b i -> (e s) b i")
         nc.sync.dma_start(dst_l[:], dst)
         load_planes([nc.scalar, nc.sync], dy_s, dy_scales.to_broadcast([8, 16, T]))
         nc.sync.dma_start(dy_w[:].bitcast(I32), dy_words.rearrange("s p t d -> p (s t d)").bitcast(I32))
-        load_wet(0)
+        load_wet(0, 1)
         load_planes([nc.sync], wet_s[0], wet_rows)
+        load_wet(1, 2)
         with nc.allow_non_contiguous_dma(reason="one weight a partition and expert"):
             nc.sync.dma_start(gate_col[:], gate[0:1, :].rearrange("r (e u) -> u (r e)", u=C2))
         nc.sync.dma_start(offs2_l[:], offs2)
-        load_wet(1)
+        load_wet(2, 4)
         load_planes([nc.sync], wet_s[1], wet_rows[4:8])
-        for f in range(2, G):
-            load_wet(f)
+        load_wet(4, E)
         for h in range(2):
             nc.sync.dma_start(a_sb[h][:], a_p[:, :, HALF * h : HALF * (h + 1)])
         load_planes([nc.sync], wgt_s, wgt_scales.rearrange("f s b k -> (f s) b k"))
@@ -103,13 +105,12 @@ def tile_moe_hib_relu_kernel(
         zt_ps = {}
 
         def product(e):
-            f, u = divmod(e, EPG)
             zt_ps[e] = psum.tile([P, H], F32, name="zt_ps", tag="zt")
             nc.tensor.matmul_mx(
                 out=zt_ps[e][:],
                 lhsT=gq_w[e].bitcast(FP8X4),
                 lhsT_scale=gq_s[e],
-                rhs=wet_w[f][:, u, :].bitcast(FP8X4),
+                rhs=wet_w[e].bitcast(FP8X4),
                 rhs_scale=wet_s[e // 4][4 * (e % 4) : P, :],
                 start=True,
                 stop=True,

@@ -45,8 +45,8 @@ def tile_moe_hib_relu_kernel(
         wet_s = [slot("wet_s%d" % h, [P, H], U8) for h in range(2)]
         wgt_w = slot("wgt_w", [P, G, K], U32)
         wgt_s = slot("wgt_s", [P, K], U8)
-        a_sb = [slot("a_sb%d" % h, [P, PACK, HALF], F32) for h in range(2)]
-        gate_col = slot("gate_col", [P, E], F32)
+        a_sb = slot("a_sb", [P, PACK, T], F32)
+        gate_col = []
         ident = slot("ident", [P, P], F32)
 
         def load_planes(queues, tile, rows):
@@ -70,21 +70,26 @@ def tile_moe_hib_relu_kernel(
             nc.sync.dma_start(tile[:].bitcast(I32), wet_words_p[:, e0:e1, :].bitcast(I32))
             wet_w.extend(tile[:, u, :] for u in range(e1 - e0))
 
+        def load_gate(e0, e1):
+            tile = slot("gate%d" % e0, [P, e1 - e0], F32)
+            with nc.allow_non_contiguous_dma(reason="one weight a partition and expert"):
+                nc.sync.dma_start(tile[:], gate[0:1, C2 * e0 : C2 * e1].rearrange("r (e u) -> u (r e)", u=C2))
+            gate_col.extend(tile[:, u : u + 1] for u in range(e1 - e0))
+
         wet_rows = wet_scales.rearrange("e s b i -> (e s) b i")
         nc.sync.dma_start(dst_l[:], dst)
-        load_planes([nc.scalar, nc.sync], dy_s, dy_scales.to_broadcast([8, 16, T]))
+        load_planes([nc.sync], dy_s, dy_scales.to_broadcast([8, 16, T]))
         nc.sync.dma_start(dy_w[:].bitcast(I32), dy_words.rearrange("s p t d -> p (s t d)").bitcast(I32))
         load_wet(0, 1)
         load_planes([nc.sync], wet_s[0], wet_rows)
+        load_gate(0, EPG)
         load_wet(1, 2)
-        with nc.allow_non_contiguous_dma(reason="one weight a partition and expert"):
-            nc.sync.dma_start(gate_col[:], gate[0:1, :].rearrange("r (e u) -> u (r e)", u=C2))
         nc.sync.dma_start(offs2_l[:], offs2)
+        load_gate(EPG, E)
         load_wet(2, 4)
         load_planes([nc.sync], wet_s[1], wet_rows[4:8])
         load_wet(4, E)
-        for h in range(2):
-            nc.sync.dma_start(a_sb[h][:], a_p[:, :, HALF * h : HALF * (h + 1)])
+        nc.sync.dma_start(a_sb[:], a_p)
         load_planes([nc.sync], wgt_s, wgt_scales.rearrange("f s b k -> (f s) b k"))
         nc.sync.dma_start(wgt_w[:].bitcast(I32), wgt_words.rearrange("f s p k d -> p (f s) (k d)").bitcast(I32))
         nc.sync.dma_start(offs_l[:], offs)
@@ -121,7 +126,7 @@ def tile_moe_hib_relu_kernel(
                 zt[e][:, t0:t1, :],
                 zt_ps[e][:].rearrange("m (p t) -> m t p", t=PACK)[:, t0:t1, :],
                 ACT.Copy,
-                scale=gate_col[:, e : e + 1],
+                scale=gate_col[e],
             )
 
         def turn(t, e0, e1):
@@ -140,7 +145,7 @@ def tile_moe_hib_relu_kernel(
         def make_mask(h, t):
             sign = keep.tile([P, HALF], BF16, name="sign", bufs=2)
             mask = slot("mask%d_%d" % (h, t), [P, HALF], BF16)
-            nc.scalar.activation(sign[:], a_sb[h][:, t, :], ACT.Sign)
+            nc.scalar.activation(sign[:], a_sb[:, t, HALF * h : HALF * (h + 1)], ACT.Sign)
             nc.scalar.activation(mask[:], sign[:], ACT.Relu)
             return mask
 
@@ -186,7 +191,7 @@ def tile_moe_hib_relu_kernel(
 
         product(0)
         product(1)
-        gq_s.extend(gather(dy_s, U8, EARLY, T, "gq_w0"))
+        gq_s.extend(gather(dy_s, U8, EARLY, T, "wet_w0"))
         wins = [window("zwin%d" % t) for t in range(PACK)]
         gate_and_sort(0, 0, 1)
         scatter_z(wins[0], turn(0, 0, 1), 0, 1)

@@ -20,14 +20,20 @@ P = 128
 PACK = 4
 PER_COL = 16
 EPG = E // G
+QUAD = 32
+QUADS = P // QUAD
+ROWS = 4
+SHARE = 4
+BANK = 4
+HALF = T // 2
+HALF_E = E // 2
+EARLY = 5 * C2
 
 
 def tile_moe_hib_relu_kernel(
     tc, dy_words, dy_scales, wet_words, wet_scales, wgt_words, wgt_scales, a, gate, offs, offs2, dst, out
 ):
     nc = tc.nc
-    HALF = T // 2
-    EARLY = 5 * C2
 
     with ExitStack() as ctx:
         keep = ctx.enter_context(tc.tile_pool(name="keep", bufs=1))
@@ -42,18 +48,19 @@ def tile_moe_hib_relu_kernel(
         dy_w = slot("dy_w", [P, T], U32)
         dy_s = slot("dy_s", [P, T], U8)
         wet_w = []
-        wet_s = [slot("wet_s%d" % h, [P, H], U8) for h in range(2)]
+        wet_s = [slot("wet_s%d" % h, [P, H], U8) for h in range(E // SHARE)]
         wgt_w = slot("wgt_w", [P, G, K], U32)
         wgt_s = slot("wgt_s", [P, K], U8)
         a_sb = slot("a_sb", [P, PACK, T], F32)
         gate_col = []
         ident = slot("ident", [P, P], F32)
 
-        def load_planes(queues, tile, rows):
-            n = rows.shape[0]
-            for q in range(4):
-                queues[q % len(queues)].dma_start(
-                    tile[32 * q : 32 * q + 4 * n, :].bitcast(I32), rows[:, 4 * q : 4 * q + 4, :].bitcast(I32)
+        def load_scales(tile, rows):
+            matrices = rows.shape[0]
+            for q in range(QUADS):
+                nc.sync.dma_start(
+                    tile[QUAD * q : QUAD * q + ROWS * matrices, :].bitcast(I32),
+                    rows[:, ROWS * q : ROWS * (q + 1), :].bitcast(I32),
                 )
 
         ident0 = slot("ident0", [P, P], F32)
@@ -76,21 +83,24 @@ def tile_moe_hib_relu_kernel(
                 nc.sync.dma_start(tile[:], gate[0:1, C2 * e0 : C2 * e1].rearrange("r (e u) -> u (r e)", u=C2))
             gate_col.extend(tile[:, u : u + 1] for u in range(e1 - e0))
 
-        wet_rows = wet_scales.rearrange("e s b i -> (e s) b i")
         nc.sync.dma_start(dst_l[:], dst)
-        load_planes([nc.sync], dy_s, dy_scales.to_broadcast([8, 16, T]))
+        load_scales(dy_s, dy_scales.to_broadcast([QUAD // ROWS, QUADS * ROWS, T]))
         nc.sync.dma_start(dy_w[:].bitcast(I32), dy_words.rearrange("s p t d -> p (s t d)").bitcast(I32))
         load_wet(0, 1)
-        load_planes([nc.sync], wet_s[0], wet_rows)
+        load_scales(wet_s[0], wet_scales.rearrange("e s b i -> (e s) b i"))
         load_gate(0, EPG)
-        load_wet(1, 2)
+        load_wet(1, EPG)
         nc.sync.dma_start(offs2_l[:], offs2)
         load_gate(EPG, E)
-        load_wet(2, 4)
-        load_planes([nc.sync], wet_s[1], wet_rows[4:8])
-        load_wet(4, E)
+        load_wet(EPG, HALF_E)
+        for q in range(QUADS):
+            nc.sync.dma_start(
+                wet_s[1][QUAD * q : QUAD * q + ROWS * SHARE, :].bitcast(I32),
+                wet_s[0][QUAD * q + ROWS * SHARE : QUAD * (q + 1), :].bitcast(I32),
+            )
+        load_wet(HALF_E, E)
         nc.sync.dma_start(a_sb[:], a_p)
-        load_planes([nc.sync], wgt_s, wgt_scales.rearrange("f s b k -> (f s) b k"))
+        load_scales(wgt_s, wgt_scales.rearrange("f s b k -> (f s) b k"))
         nc.sync.dma_start(wgt_w[:].bitcast(I32), wgt_words.rearrange("f s p k d -> p (f s) (k d)").bitcast(I32))
         nc.sync.dma_start(offs_l[:], offs)
 
@@ -116,7 +126,7 @@ def tile_moe_hib_relu_kernel(
                 lhsT=gq_w[e].bitcast(FP8X4),
                 lhsT_scale=gq_s[e],
                 rhs=wet_w[e].bitcast(FP8X4),
-                rhs_scale=wet_s[e // 4][4 * (e % 4) : P, :],
+                rhs_scale=wet_s[e // SHARE][ROWS * (e % SHARE) : P, :],
                 start=True,
                 stop=True,
             )
@@ -131,8 +141,8 @@ def tile_moe_hib_relu_kernel(
 
         def turn(t, e0, e1):
             z = slot("z%d_%d" % (t, e0), [P, (e1 - e0) * C2], F32)
-            for b0 in range(e0, e1, PACK):
-                b1 = min(b0 + PACK, e1)
+            for b0 in range(e0, e1, BANK):
+                b1 = min(b0 + BANK, e1)
                 z_ps = psum.tile([P, (b1 - b0) * C2], F32, name="z_ps", tag="z", bufs=3)
                 for e in range(b0, b1):
                     nc.tensor.transpose(z_ps[:, C2 * (e - b0) : C2 * (e - b0 + 1)], zt[e][:, t, :], ident[:])
@@ -144,10 +154,10 @@ def tile_moe_hib_relu_kernel(
 
         def make_mask(h, t):
             sign = keep.tile([P, HALF], BF16, name="sign", bufs=2)
-            mask = slot("mask%d_%d" % (h, t), [P, HALF], BF16)
+            positive = slot("mask%d_%d" % (h, t), [P, HALF], BF16)
             nc.scalar.activation(sign[:], a_sb[:, t, HALF * h : HALF * (h + 1)], ACT.Sign)
-            nc.scalar.activation(mask[:], sign[:], ACT.Relu)
-            return mask
+            nc.scalar.activation(positive[:], sign[:], ACT.Relu)
+            return positive
 
         def in_half(lo, hi):
             h = lo // HALF
@@ -170,12 +180,12 @@ def tile_moe_hib_relu_kernel(
             for c in range(K // P):
                 ks = slice(P * c, P * (c + 1))
                 dx_ps = psum.tile([P, HALF], F32, name="dx_ps", tag="dx", bufs=3)
-                for u in range(2):
+                for u in range(G // 2):
                     js = slice(C1 * u, C1 * (u + 1))
                     nc.tensor.matmul_mx(
                         out=dx_ps[:, js],
                         lhsT=wgt_w[:, 2 * h + u, ks].bitcast(FP8X4),
-                        lhsT_scale=wgt_s[4 * (2 * h + u) : P, ks],
+                        lhsT_scale=wgt_s[ROWS * (2 * h + u) : P, ks],
                         rhs=da_w[:, js].bitcast(FP8X4),
                         rhs_scale=da_s[:, js],
                         start=True,
@@ -192,45 +202,45 @@ def tile_moe_hib_relu_kernel(
         product(0)
         product(1)
         gq_s.extend(gather(dy_s, U8, EARLY, T, "wet_w0"))
-        wins = [window("zwin%d" % t) for t in range(PACK)]
+        first = [window("zwin%d" % t) for t in range(PACK)]
         gate_and_sort(0, 0, 1)
-        scatter_z(wins[0], turn(0, 0, 1), 0, 1)
+        scatter_z(first[0], turn(0, 0, 1), 0, 1)
         gate_and_sort(0, 1, PACK)
-        scatter_z(wins[1], turn(1, 0, 1), 0, 1)
+        scatter_z(first[1], turn(1, 0, 1), 0, 1)
         gate_and_sort(1, 0, PACK)
         for t in (2, 3):
-            scatter_z(wins[t], turn(t, 0, 2), 0, 2)
-        for e in range(2, 4):
+            scatter_z(first[t], turn(t, 0, EPG), 0, EPG)
+        for e in range(EPG, HALF_E):
             product(e)
             gate_and_sort(e, 0, PACK)
         for t in (0, 1):
-            scatter_z(wins[t], turn(t, 1, 4), 1, 4)
-        for e in range(4, E):
+            scatter_z(first[t], turn(t, 1, HALF_E), 1, HALF_E)
+        for e in range(HALF_E, E):
             product(e)
             gate_and_sort(e, 0, PACK)
-        late = [window("zlate%d" % t) for t in (2, 3)]
+        late = {t: window("zlate%d" % t) for t in (2, 3)}
         for t in (2, 3):
-            scatter_z(late[t - 2], turn(t, 2, E), 2, E)
-        z_last = [turn(t, 4, E) for t in (0, 1)]
+            scatter_z(late[t], turn(t, EPG, E), EPG, E)
+        z_last = [turn(t, HALF_E, E) for t in (0, 1)]
         mask = [[make_mask(h, t) for t in range(PACK)] for h in range(2)]
 
         da0 = slot("da0", [P, HALF, PACK], BF16)
         planar = [slot("planar%d" % h, [P, PACK, HALF], BF16) for h in range(2)]
         for t in (2, 3):
-            apply_mask(wins[t], t, 0, C1)
+            apply_mask(first[t], t, 0, C1)
         for t in (0, 1):
-            apply_mask(wins[t], t, 0, HALF)
+            apply_mask(first[t], t, 0, HALF)
         interleave(da0, 0, C1)
         for t in (2, 3):
-            apply_mask(late[t - 2], t, C1, HALF)
-            apply_mask(late[t - 2], t, HALF, T)
+            apply_mask(late[t], t, C1, HALF)
+            apply_mask(late[t], t, HALF, T)
         interleave(da0, C1, HALF)
 
         last = [window("zlast0")]
-        scatter_z(last[0], z_last[0], 4, E)
+        scatter_z(last[0], z_last[0], HALF_E, E)
         quantise_and_multiply(0, da0)
         last.append(window("zlast1", "planar0"))
-        scatter_z(last[1], z_last[1], 4, E)
+        scatter_z(last[1], z_last[1], HALF_E, E)
         da1 = slot("da1", [P, HALF, PACK], BF16, "da_w0")
         for t in (0, 1):
             apply_mask(last[t], t, HALF, T)

@@ -27,7 +27,7 @@ SHARE = 4
 BANK = 4
 HALF = T // 2
 HALF_E = E // 2
-EARLY = 5 * C2
+EARLY = 4 * C2
 
 
 def tile_moe_hib_relu_kernel(
@@ -205,11 +205,13 @@ def tile_moe_hib_relu_kernel(
         first = [window("zwin%d" % t) for t in range(PACK)]
         gate_and_sort(0, 0, 1)
         scatter_z(first[0], turn(0, 0, 1), 0, 1)
-        gate_and_sort(0, 1, PACK)
+        gate_and_sort(0, 1, 2)
         scatter_z(first[1], turn(1, 0, 1), 0, 1)
-        gate_and_sort(1, 0, PACK)
         for t in (2, 3):
+            gate_and_sort(0, t, t + 1)
+            gate_and_sort(1, t, t + 1)
             scatter_z(first[t], turn(t, 0, EPG), 0, EPG)
+        gate_and_sort(1, 0, 2)
         for e in range(EPG, HALF_E):
             product(e)
             gate_and_sort(e, 0, PACK)

@@ -152,12 +152,11 @@ def tile_moe_hib_relu_kernel(
         def scatter_z(win, z, e0, e1):
             nc.vector.tensor_copy(win[:].indirect(offs2_l[:, cols(C2 * e0, C2 * e1)]), z[:])
 
-        def make_mask(h, t):
+        def make_mask(h, t, positive):
             sign = keep.tile([P, HALF], BF16, name="sign", bufs=2)
-            positive = slot("mask%d_%d" % (h, t), [P, HALF], BF16)
             nc.scalar.activation(sign[:], a_sb[:, t, HALF * h : HALF * (h + 1)], ACT.Sign)
-            nc.scalar.activation(positive[:], sign[:], ACT.Relu)
-            return positive
+            nc.scalar.activation(positive, sign[:], ACT.Relu)
+            mask[h, t] = positive
 
         def in_half(lo, hi):
             h = lo // HALF
@@ -165,7 +164,7 @@ def tile_moe_hib_relu_kernel(
 
         def apply_mask(win, t, lo, hi):
             h, js = in_half(lo, hi)
-            nc.gpsimd.tensor_tensor(planar[h][:, t, js], win[:, lo:hi], mask[h][t][:, js], MULT)
+            nc.gpsimd.tensor_tensor(planar[h][:, t, js], win[:, lo:hi], mask[h, t][:, js], MULT)
 
         def interleave(da, lo, hi):
             h, js = in_half(lo, hi)
@@ -173,11 +172,11 @@ def tile_moe_hib_relu_kernel(
 
         dx = [slot("dx%d" % c, [P, T], F32) for c in range(K // P)]
 
-        def quantise_and_multiply(h, da):
+        def quantise_and_multiply(h, da, blocks):
             da_w = slot("da_w%d" % h, [P, HALF], U32)
             da_s = slot("da_s%d" % h, [P, HALF], U8)
             nc.vector.quantize_mx(out=da_w[:].bitcast(FP8X4), scales=da_s[:], in_=da[:].rearrange("p j t -> p (j t)"))
-            for c in range(K // P):
+            for c in blocks:
                 ks = slice(P * c, P * (c + 1))
                 dx_ps = psum.tile([P, HALF], F32, name="dx_ps", tag="dx", bufs=3)
                 for u in range(G // 2):
@@ -224,7 +223,10 @@ def tile_moe_hib_relu_kernel(
         for t in (2, 3):
             scatter_z(late[t], turn(t, EPG, E), EPG, E)
         z_last = [turn(t, HALF_E, E) for t in (0, 1)]
-        mask = [[make_mask(h, t) for t in range(PACK)] for h in range(2)]
+        mask = {}
+        for h, t in ((0, 0), (0, 1), (0, 2), (1, 2), (0, 3), (1, 3)):
+            tile = slot("mask%d_%d" % (h, t), [P, HALF], BF16)
+            make_mask(h, t, tile[:])
 
         da0 = slot("da0", [P, HALF, PACK], BF16)
         planar = [slot("planar%d" % h, [P, PACK, HALF], BF16) for h in range(2)]
@@ -233,14 +235,19 @@ def tile_moe_hib_relu_kernel(
         for t in (0, 1):
             apply_mask(first[t], t, 0, HALF)
         interleave(da0, 0, C1)
-        for t in (2, 3):
-            apply_mask(late[t], t, C1, HALF)
-            apply_mask(late[t], t, HALF, T)
-        interleave(da0, C1, HALF)
+        apply_mask(late[2], 2, C1, HALF)
+        apply_mask(late[2], 2, HALF, T)
+        for lo in range(C1, HALF, C2):
+            apply_mask(late[3], 3, lo, lo + C2)
+            interleave(da0, lo, lo + C2)
+        apply_mask(late[3], 3, HALF, T)
 
         last = [window("zlast0")]
         scatter_z(last[0], z_last[0], HALF_E, E)
-        quantise_and_multiply(0, da0)
+        quantise_and_multiply(0, da0, (1, 2, 3, 0))
+        mask_last = slot("mask_last", [P, 2, HALF], BF16, "da0")
+        for t in (0, 1):
+            make_mask(1, t, mask_last[:, t, :])
         last.append(window("zlast1", "planar0"))
         scatter_z(last[1], z_last[1], HALF_E, E)
         da1 = slot("da1", [P, HALF, PACK], BF16, "da_w0")
@@ -251,7 +258,7 @@ def tile_moe_hib_relu_kernel(
         owin = [slot("owin0", [P, 2 * T], F32), window("owin1"), window("owin2")]
         for c in (1, 2):
             scatter_dx(owin[c], c, 0, HALF)
-        quantise_and_multiply(1, da1)
+        quantise_and_multiply(1, da1, (0, 1, 2, 3))
         owin.append(window("owin3", "planar1"))
         scatter_dx(owin[3], 3, 0, HALF)
         for c in range(K // P):

@@ -27,7 +27,6 @@ SHARE = 4
 BANK = 4
 HALF = T // 2
 HALF_E = E // 2
-EARLY = 4 * C2
 
 
 def tile_moe_hib_relu_kernel(
@@ -51,8 +50,10 @@ def tile_moe_hib_relu_kernel(
         wet_s = [slot("wet_s%d" % h, [P, H], U8) for h in range(E // SHARE)]
         wgt_w = slot("wgt_w", [P, G, K], U32)
         wgt_s = slot("wgt_s", [P, K], U8)
-        a_sb = slot("a_sb", [P, PACK, T], F32)
-        gate_col = []
+        a_first = slot("a_first", [P, PACK, C1], F32)
+        a_rest = slot("a_rest", [P, PACK, T - C1], F32)
+        gate_rows = slot("gate_rows", [P, C1], F32)
+        gate_cols = slot("gate_cols", [P, E - EPG], F32)
         ident = slot("ident", [P, P], F32)
 
         def load_scales(tile, rows):
@@ -63,35 +64,27 @@ def tile_moe_hib_relu_kernel(
                     rows[:, ROWS * q : ROWS * (q + 1), :].bitcast(I32),
                 )
 
-        ident0 = slot("ident0", [P, P], F32)
-        make_identity(nc, ident0[:])
-        nc.scalar.copy(ident[:], ident0[:])
+        make_identity(nc, ident[:])
         nc.gpsimd.memset(wet_s[1][:].bitcast(I32), 0)
         nc.gpsimd.memset(wgt_s[:].bitcast(I32), 0)
 
         wet_words_p = wet_words.rearrange("e s p i d -> p (e s) (i d)")
-        a_p = a.rearrange("(p t) j -> p t j", t=PACK)
 
         def load_wet(e0, e1):
             tile = slot("wet_w%d" % e0, [P, e1 - e0, H], U32)
             nc.sync.dma_start(tile[:].bitcast(I32), wet_words_p[:, e0:e1, :].bitcast(I32))
             wet_w.extend(tile[:, u, :] for u in range(e1 - e0))
 
-        def load_gate(e0, e1):
-            tile = slot("gate%d" % e0, [P, e1 - e0], F32)
-            with nc.allow_non_contiguous_dma(reason="one weight a partition and expert"):
-                nc.sync.dma_start(tile[:], gate[0:1, C2 * e0 : C2 * e1].rearrange("r (e u) -> u (r e)", u=C2))
-            gate_col.extend(tile[:, u : u + 1] for u in range(e1 - e0))
-
         nc.sync.dma_start(dst_l[:], dst)
         load_scales(dy_s, dy_scales.to_broadcast([QUAD // ROWS, QUADS * ROWS, T]))
         nc.sync.dma_start(dy_w[:].bitcast(I32), dy_words.rearrange("s p t d -> p (s t d)").bitcast(I32))
         load_wet(0, 1)
         load_scales(wet_s[0], wet_scales.rearrange("e s b i -> (e s) b i"))
-        load_gate(0, EPG)
-        load_wet(1, EPG)
+        nc.sync.dma_start(gate_rows[:], gate[:, 0:C1])
         nc.sync.dma_start(offs2_l[:], offs2)
-        load_gate(EPG, E)
+        load_wet(1, EPG)
+        with nc.allow_non_contiguous_dma(reason="one weight a partition and expert"):
+            nc.sync.dma_start(gate_cols[:], gate[0:1, C1:T].rearrange("r (e u) -> u (r e)", u=C2))
         load_wet(EPG, HALF_E)
         for q in range(QUADS):
             nc.sync.dma_start(
@@ -99,7 +92,8 @@ def tile_moe_hib_relu_kernel(
                 wet_s[0][QUAD * q + ROWS * SHARE : QUAD * (q + 1), :].bitcast(I32),
             )
         load_wet(HALF_E, E)
-        nc.sync.dma_start(a_sb[:], a_p)
+        nc.sync.dma_start(a_first[:], a[:, 0:C1].rearrange("(c p) j -> p c j", p=P))
+        nc.sync.dma_start(a_rest[:], a[:, C1:T].rearrange("(p t) j -> p t j", t=PACK))
         load_scales(wgt_s, wgt_scales.rearrange("f s b k -> (f s) b k"))
         nc.sync.dma_start(wgt_w[:].bitcast(I32), wgt_words.rearrange("f s p k d -> p (f s) (k d)").bitcast(I32))
         nc.sync.dma_start(offs_l[:], offs)
@@ -112,63 +106,73 @@ def tile_moe_hib_relu_kernel(
             nc.vector.tensor_copy(tile[:], src[:].indirect(dst_l[:, cols(lo, hi)]))
             return [tile[:, m - lo : m - lo + C2] for m in range(lo, hi, C2)]
 
-        gq_s = gather(dy_s, U8, 0, EARLY, "gq_s_first")
-        gq_w = gather(dy_w, U32, 0, C1, "gq_w0")
-        gq_w.extend(gather(dy_w, U32, C1, T, "gq_w1"))
+        gq_s = gather(dy_s, U8, 0, HALF + C2, "gq_s_first")
+        gq_w = gather(dy_w, U32, 0, C2, "gq_w0")
+        gq_w.extend(gather(dy_w, U32, C2, T - C2, "gq_w1"))
+        gq_w.extend(gather(dy_w, U32, T - C2, T, "gq_w7"))
 
-        zt = [slot("zt%d" % e, [P, PACK, C2], F32) for e in range(E)]
-        zt_ps = {}
+        def wet_scale(e):
+            return wet_s[e // SHARE][ROWS * (e % SHARE) : P, :]
+
+        def first_group(z, c, e0, e1):
+            cs = slice(P * c, P * (c + 1))
+            z_ps = psum.tile([P, (e1 - e0) * C2], F32, name="z_ps", tag="z", bufs=3)
+            for e in range(e0, e1):
+                nc.tensor.matmul_mx(
+                    out=z_ps[:, C2 * (e - e0) : C2 * (e - e0 + 1)],
+                    lhsT=wet_w[e][:, cs].bitcast(FP8X4),
+                    lhsT_scale=wet_scale(e)[:, cs],
+                    rhs=gq_w[e].bitcast(FP8X4),
+                    rhs_scale=gq_s[e],
+                    start=True,
+                    stop=True,
+                )
+            sums = slot("sums%d_%d" % (c, e0), [P, (e1 - e0) * C2], F32)
+            nc.scalar.copy(sums[:], z_ps[:])
+            nc.gpsimd.tensor_tensor(z, sums[:], gate_rows[:, C2 * e0 : C2 * e1], MULT)
+
+        zt = {e: slot("zt%d" % e, [P, PACK, C2], F32) for e in range(EPG, E)}
 
         def product(e):
-            zt_ps[e] = psum.tile([P, H], F32, name="zt_ps", tag="zt")
+            zt_ps = psum.tile([P, H], F32, name="zt_ps", tag="zt")
             nc.tensor.matmul_mx(
-                out=zt_ps[e][:],
+                out=zt_ps[:],
                 lhsT=gq_w[e].bitcast(FP8X4),
                 lhsT_scale=gq_s[e],
                 rhs=wet_w[e].bitcast(FP8X4),
-                rhs_scale=wet_s[e // SHARE][ROWS * (e % SHARE) : P, :],
+                rhs_scale=wet_scale(e),
                 start=True,
                 stop=True,
             )
-
-        def gate_and_sort(e, t0, t1):
             nc.scalar.activation(
-                zt[e][:, t0:t1, :],
-                zt_ps[e][:].rearrange("m (p t) -> m t p", t=PACK)[:, t0:t1, :],
+                zt[e][:],
+                zt_ps[:].rearrange("m (p t) -> m t p", t=PACK),
                 ACT.Copy,
-                scale=gate_col[e],
+                scale=gate_cols[:, e - EPG : e - EPG + 1],
             )
 
-        def turn(t, e0, e1):
-            z = slot("z%d_%d" % (t, e0), [P, (e1 - e0) * C2], F32)
+        def turn(z, t, e0, e1):
             for b0 in range(e0, e1, BANK):
                 b1 = min(b0 + BANK, e1)
                 z_ps = psum.tile([P, (b1 - b0) * C2], F32, name="z_ps", tag="z", bufs=3)
                 for e in range(b0, b1):
                     nc.tensor.transpose(z_ps[:, C2 * (e - b0) : C2 * (e - b0 + 1)], zt[e][:, t, :], ident[:])
                 nc.scalar.copy(z[:, C2 * (b0 - e0) : C2 * (b1 - e0)], z_ps[:])
-            return z
+
+        def piece(t, e0, e1):
+            return slot("z%d_%d" % (t, e0), [P, (e1 - e0) * C2], F32)
 
         def scatter_z(win, z, e0, e1):
             nc.vector.tensor_copy(win[:].indirect(offs2_l[:, cols(C2 * e0, C2 * e1)]), z[:])
 
-        def make_mask(h, t, positive):
+        mask = {}
+
+        def make_mask(key, values, positive):
             sign = keep.tile([P, HALF], BF16, name="sign", bufs=2)
-            nc.scalar.activation(sign[:], a_sb[:, t, HALF * h : HALF * (h + 1)], ACT.Sign)
-            nc.scalar.activation(positive, sign[:], ACT.Relu)
-            mask[h, t] = positive
-
-        def in_half(lo, hi):
-            h = lo // HALF
-            return h, slice(lo - HALF * h, hi - HALF * h)
-
-        def apply_mask(win, t, lo, hi):
-            h, js = in_half(lo, hi)
-            nc.gpsimd.tensor_tensor(planar[h][:, t, js], win[:, lo:hi], mask[h, t][:, js], MULT)
-
-        def interleave(da, lo, hi):
-            h, js = in_half(lo, hi)
-            nc.scalar.copy(da[:, js, :], planar[h][:, :, js].rearrange("p t j -> p j t"))
+            width = values.shape[1]
+            nc.scalar.activation(sign[:, 0:width], values, ACT.Sign)
+            nc.scalar.activation(positive, sign[:, 0:width], ACT.Relu)
+            mask[key] = positive
 
         dx = [slot("dx%d" % c, [P, T], F32) for c in range(K // P)]
 
@@ -198,62 +202,91 @@ def tile_moe_hib_relu_kernel(
         def window(name, tag=None):
             return slot(name, [P, T], F32, tag)
 
-        product(0)
-        product(1)
-        gq_s.extend(gather(dy_s, U8, EARLY, T, "wet_w0"))
         first = [window("zwin%d" % t) for t in range(PACK)]
-        gate_and_sort(0, 0, 1)
-        scatter_z(first[0], turn(0, 0, 1), 0, 1)
-        gate_and_sort(0, 1, 2)
-        scatter_z(first[1], turn(1, 0, 1), 0, 1)
-        for t in (2, 3):
-            gate_and_sort(0, t, t + 1)
-            gate_and_sort(1, t, t + 1)
-            scatter_z(first[t], turn(t, 0, EPG), 0, EPG)
-        gate_and_sort(1, 0, 2)
+        for c in range(PACK):
+            e1 = 1 if c < 2 else EPG
+            z = piece(c, 0, e1)
+            first_group(z[:], c, 0, e1)
+            scatter_z(first[c], z, 0, e1)
+            if c < PACK - 1:
+                e = HALF_E + 1 + c
+                gq_s.extend(gather(dy_s, U8, C2 * e, C2 * (e + 1), "sums%d_0" % c))
+        second = [piece(t, 1, HALF_E) for t in (0, 1)]
+        for t in (0, 1):
+            first_group(second[t][:, 0:C2], t, 1, EPG)
         for e in range(EPG, HALF_E):
             product(e)
-            gate_and_sort(e, 0, PACK)
         for t in (0, 1):
-            scatter_z(first[t], turn(t, 1, HALF_E), 1, HALF_E)
+            turn(second[t][:, C2:], t, EPG, HALF_E)
+            scatter_z(first[t], second[t], 1, HALF_E)
         for e in range(HALF_E, E):
             product(e)
-            gate_and_sort(e, 0, PACK)
         late = {t: window("zlate%d" % t) for t in (2, 3)}
         for t in (2, 3):
-            scatter_z(late[t], turn(t, EPG, E), EPG, E)
-        z_last = [turn(t, HALF_E, E) for t in (0, 1)]
-        mask = {}
+            z = piece(t, EPG, E)
+            turn(z, t, EPG, E)
+            scatter_z(late[t], z, EPG, E)
+        z_last = [piece(t, HALF_E, E) for t in (0, 1)]
+        for t in (0, 1):
+            turn(z_last[t], t, HALF_E, E)
+
+        for c in (2, 0):
+            tile = slot("mask_first%d" % c, [P, 2 * C1], BF16)
+            make_mask(("first", c), a_first[:, c : c + 2, :].rearrange("p c j -> p (c j)"), tile[:])
         for h, t in ((0, 0), (0, 1), (0, 2), (1, 2), (0, 3), (1, 3)):
-            tile = slot("mask%d_%d" % (h, t), [P, HALF], BF16)
-            make_mask(h, t, tile[:])
+            lo, hi = (C1, HALF) if h == 0 else (HALF, T)
+            tile = slot("mask%d_%d" % (h, t), [P, hi - lo], BF16)
+            make_mask((h, t), a_rest[:, t, lo - C1 : hi - C1], tile[:])
 
         da0 = slot("da0", [P, HALF, PACK], BF16)
-        planar = [slot("planar%d" % h, [P, PACK, HALF], BF16) for h in range(2)]
-        for t in (2, 3):
-            apply_mask(first[t], t, 0, C1)
+        masked = slot("masked", [P, PACK, C1], F32)
+        for c in (2, 3, 0, 1):
+            m = mask["first", c - c % 2][:, C1 * (c % 2) : C1 * (c % 2 + 1)]
+            nc.gpsimd.tensor_tensor(masked[:, c, :], first[c][:, 0:C1], m, MULT)
+        for b in range(C1 // P):
+            js = slice(P * b, P * (b + 1))
+            rows_ps = psum.tile([P, H], F32, name="rows_ps", tag="zt")
+            for c in range(PACK):
+                nc.tensor.transpose(rows_ps[:, P * c : P * (c + 1)], masked[:, c, js], ident[:])
+            rows = slot("rows%d" % b, [P, H], BF16)
+            nc.scalar.copy(rows[:], rows_ps[:])
+            pairs_ps = psum.tile([P, 2, P], F32, name="pairs_ps", tag="z", bufs=3)
+            for u in range(2):
+                nc.tensor.transpose(pairs_ps[:, u, :], rows[:].bitcast(F32)[:, u : H // 2 : 2], ident[:])
+            nc.scalar.copy(da0[:, js, :].bitcast(F32), pairs_ps[:].rearrange("p u j -> p j u"))
+
+        planar = [slot("planar0", [P, PACK, C1], BF16), slot("planar1", [P, PACK, HALF], BF16)]
+        start = (C1, HALF)
+
+        def apply_mask(win, h, t, lo, hi):
+            js = slice(lo - start[h], hi - start[h])
+            nc.gpsimd.tensor_tensor(planar[h][:, t, js], win[:, lo:hi], mask[h, t][:, js], MULT)
+
+        def interleave(da, h, lo, hi):
+            js = slice(lo - start[h], hi - start[h])
+            nc.scalar.copy(da[:, lo - HALF * h : hi - HALF * h, :], planar[h][:, :, js].rearrange("p t j -> p j t"))
+
         for t in (0, 1):
-            apply_mask(first[t], t, 0, HALF)
-        interleave(da0, 0, C1)
-        apply_mask(late[2], 2, C1, HALF)
-        apply_mask(late[2], 2, HALF, T)
+            apply_mask(first[t], 0, t, C1, HALF)
+        apply_mask(late[2], 0, 2, C1, HALF)
+        apply_mask(late[2], 1, 2, HALF, T)
         for lo in range(C1, HALF, C2):
-            apply_mask(late[3], 3, lo, lo + C2)
-            interleave(da0, lo, lo + C2)
-        apply_mask(late[3], 3, HALF, T)
+            apply_mask(late[3], 0, 3, lo, lo + C2)
+            interleave(da0, 0, lo, lo + C2)
+        apply_mask(late[3], 1, 3, HALF, T)
 
         last = [window("zlast0")]
         scatter_z(last[0], z_last[0], HALF_E, E)
         quantise_and_multiply(0, da0, (1, 2, 3, 0))
         mask_last = slot("mask_last", [P, 2, HALF], BF16, "da0")
         for t in (0, 1):
-            make_mask(1, t, mask_last[:, t, :])
+            make_mask((1, t), a_rest[:, t, HALF - C1 : T - C1], mask_last[:, t, :])
         last.append(window("zlast1", "planar0"))
         scatter_z(last[1], z_last[1], HALF_E, E)
         da1 = slot("da1", [P, HALF, PACK], BF16, "da_w0")
         for t in (0, 1):
-            apply_mask(last[t], t, HALF, T)
-        interleave(da1, HALF, T)
+            apply_mask(last[t], 1, t, HALF, T)
+        interleave(da1, 1, HALF, T)
 
         owin = [slot("owin0", [P, 2 * T], F32), window("owin1"), window("owin2")]
         for c in (1, 2):

@@ -46,12 +46,12 @@ def tile_moe_hib_relu_kernel(
         offs_l = keep.tile([P, T // PER_COL], U16, name="offs_l")
         dy_w = slot("dy_w", [P, T], U32)
         dy_s = slot("dy_s", [P, T], U8)
-        wet_w = []
+        wet_w = {}
         wet_s = [slot("wet_s%d" % h, [P, H], U8) for h in range(E // SHARE)]
-        wgt_w = slot("wgt_w", [P, G, K], U32)
+        wgt_w = [slot("wgt_w%d" % f, [P, K], U32) for f in range(G)]
         wgt_s = slot("wgt_s", [P, K], U8)
         a_first = slot("a_first", [P, PACK, C1], F32)
-        a_rest = slot("a_rest", [P, PACK, T - C1], F32)
+        a_rest = [slot("a_rest%d" % t, [P, T - C1], F32) for t in range(PACK)]
         gate_rows = slot("gate_rows", [P, C1], F32)
         gate_cols = slot("gate_cols", [P, E - EPG], F32)
         ident = slot("ident", [P, P], F32)
@@ -73,14 +73,17 @@ def tile_moe_hib_relu_kernel(
         def load_wet(e0, e1):
             tile = slot("wet_w%d" % e0, [P, e1 - e0, H], U32)
             nc.sync.dma_start(tile[:].bitcast(I32), wet_words_p[:, e0:e1, :].bitcast(I32))
-            wet_w.extend(tile[:, u, :] for u in range(e1 - e0))
+            for e in range(e0, e1):
+                wet_w[e] = tile[:, e - e0, :]
 
         nc.sync.dma_start(dst_l[:], dst)
         load_scales(dy_s, dy_scales.to_broadcast([QUAD // ROWS, QUADS * ROWS, T]))
         nc.sync.dma_start(dy_w[:].bitcast(I32), dy_words.rearrange("s p t d -> p (s t d)").bitcast(I32))
-        load_wet(0, 1)
+        wet0 = [slot("wet0_first", [P, P], U32), slot("wet0_rest", [P, H - P], U32)]
+        nc.sync.dma_start(wet0[0][:].bitcast(I32), wet_words_p[:, 0, 0 : PACK * P].bitcast(I32))
         load_scales(wet_s[0], wet_scales.rearrange("e s b i -> (e s) b i"))
         nc.sync.dma_start(gate_rows[:], gate[:, 0:C1])
+        nc.sync.dma_start(wet0[1][:].bitcast(I32), wet_words_p[:, 0, PACK * P : PACK * H].bitcast(I32))
         nc.sync.dma_start(offs2_l[:], offs2)
         load_wet(1, EPG)
         with nc.allow_non_contiguous_dma(reason="one weight a partition and expert"):
@@ -93,9 +96,11 @@ def tile_moe_hib_relu_kernel(
             )
         load_wet(HALF_E, E)
         nc.sync.dma_start(a_first[:], a[:, 0:C1].rearrange("(c p) j -> p c j", p=P))
-        nc.sync.dma_start(a_rest[:], a[:, C1:T].rearrange("(p t) j -> p t j", t=PACK))
+        for t in range(PACK):
+            nc.sync.dma_start(a_rest[t][:], a[:, C1:T].rearrange("(p t) j -> p t j", t=PACK)[:, t, :])
         load_scales(wgt_s, wgt_scales.rearrange("f s b k -> (f s) b k"))
-        nc.sync.dma_start(wgt_w[:].bitcast(I32), wgt_words.rearrange("f s p k d -> p (f s) (k d)").bitcast(I32))
+        for f in range(G):
+            nc.sync.dma_start(wgt_w[f][:].bitcast(I32), wgt_words[f].rearrange("s p k d -> p (s k d)").bitcast(I32))
         nc.sync.dma_start(offs_l[:], offs)
 
         def cols(lo, hi):
@@ -109,10 +114,14 @@ def tile_moe_hib_relu_kernel(
         gq_s = gather(dy_s, U8, 0, HALF + C2, "gq_s_first")
         gq_w = gather(dy_w, U32, 0, C2, "gq_w0")
         gq_w.extend(gather(dy_w, U32, C2, T - C2, "gq_w1"))
-        gq_w.extend(gather(dy_w, U32, T - C2, T, "gq_w7"))
 
         def wet_scale(e):
             return wet_s[e // SHARE][ROWS * (e % SHARE) : P, :]
+
+        def wet_block(e, c):
+            if e:
+                return wet_w[e][:, P * c : P * (c + 1)]
+            return wet0[1][:, P * (c - 1) : P * c] if c else wet0[0][:]
 
         def first_group(z, c, e0, e1):
             cs = slice(P * c, P * (c + 1))
@@ -120,7 +129,7 @@ def tile_moe_hib_relu_kernel(
             for e in range(e0, e1):
                 nc.tensor.matmul_mx(
                     out=z_ps[:, C2 * (e - e0) : C2 * (e - e0 + 1)],
-                    lhsT=wet_w[e][:, cs].bitcast(FP8X4),
+                    lhsT=wet_block(e, c).bitcast(FP8X4),
                     lhsT_scale=wet_scale(e)[:, cs],
                     rhs=gq_w[e].bitcast(FP8X4),
                     rhs_scale=gq_s[e],
@@ -187,7 +196,7 @@ def tile_moe_hib_relu_kernel(
                     js = slice(C1 * u, C1 * (u + 1))
                     nc.tensor.matmul_mx(
                         out=dx_ps[:, js],
-                        lhsT=wgt_w[:, 2 * h + u, ks].bitcast(FP8X4),
+                        lhsT=wgt_w[2 * h + u][:, ks].bitcast(FP8X4),
                         lhsT_scale=wgt_s[ROWS * (2 * h + u) : P, ks],
                         rhs=da_w[:, js].bitcast(FP8X4),
                         rhs_scale=da_s[:, js],
@@ -211,6 +220,8 @@ def tile_moe_hib_relu_kernel(
             if c < PACK - 1:
                 e = HALF_E + 1 + c
                 gq_s.extend(gather(dy_s, U8, C2 * e, C2 * (e + 1), "sums%d_0" % c))
+            else:
+                gq_w.extend(gather(dy_w, U32, T - C2, T, "sums%d_0" % c))
         second = [piece(t, 1, HALF_E) for t in (0, 1)]
         for t in (0, 1):
             first_group(second[t][:, 0:C2], t, 1, EPG)
@@ -236,7 +247,7 @@ def tile_moe_hib_relu_kernel(
         for h, t in ((0, 0), (0, 1), (0, 2), (1, 2), (0, 3), (1, 3)):
             lo, hi = (C1, HALF) if h == 0 else (HALF, T)
             tile = slot("mask%d_%d" % (h, t), [P, hi - lo], BF16)
-            make_mask((h, t), a_rest[:, t, lo - C1 : hi - C1], tile[:])
+            make_mask((h, t), a_rest[t][:, lo - C1 : hi - C1], tile[:])
 
         da0 = slot("da0", [P, HALF, PACK], BF16)
         masked = slot("masked", [P, PACK, C1], F32)
@@ -280,7 +291,7 @@ def tile_moe_hib_relu_kernel(
         quantise_and_multiply(0, da0, (1, 2, 3, 0))
         mask_last = slot("mask_last", [P, 2, HALF], BF16, "da0")
         for t in (0, 1):
-            make_mask((1, t), a_rest[:, t, HALF - C1 : T - C1], mask_last[:, t, :])
+            make_mask((1, t), a_rest[t][:, HALF - C1 : T - C1], mask_last[:, t, :])
         last.append(window("zlast1", "planar0"))
         scatter_z(last[1], z_last[1], HALF_E, E)
         da1 = slot("da1", [P, HALF, PACK], BF16, "da_w0")

@@ -1,7 +1,6 @@
 from contextlib import ExitStack
 
 import concourse.mybir as mybir
-from concourse.masks import make_identity
 
 K, T, G, C1, E, C2, H, N = 512, 1024, 4, 256, 8, 128, 512, 512
 FLOPS = 2 * T * N * H + 2 * T * H * K
@@ -14,19 +13,18 @@ U16 = mybir.dt.uint16
 U8 = mybir.dt.uint8
 FP8X4 = mybir.dt.float8_e4m3fn_x4
 ACT = mybir.ActivationFunctionType
-MULT = mybir.AluOpType.mult
+ALU = mybir.AluOpType
 
 P = 128
 PACK = 4
+BLOCKS = 4
 PER_COL = 16
 EPG = E // G
 QUAD = 32
 QUADS = P // QUAD
 ROWS = 4
 SHARE = 4
-BANK = 4
 HALF = T // 2
-HALF_E = E // 2
 
 
 def tile_moe_hib_relu_kernel(
@@ -48,13 +46,11 @@ def tile_moe_hib_relu_kernel(
         dy_s = slot("dy_s", [P, T], U8)
         wet_w = {}
         wet_s = [slot("wet_s%d" % h, [P, H], U8) for h in range(E // SHARE)]
-        wgt_w = [slot("wgt_w%d" % f, [P, K], U32) for f in range(G)]
+        wgt_w = slot("wgt_w", [P, G, K], U32)
         wgt_s = slot("wgt_s", [P, K], U8)
-        a_first = slot("a_first", [P, PACK, C1], F32)
-        a_rest = [slot("a_rest%d" % t, [P, T - C1], F32) for t in range(PACK)]
-        gate_rows = slot("gate_rows", [P, C1], F32)
-        gate_cols = slot("gate_cols", [P, E - EPG], F32)
-        ident = slot("ident", [P, P], F32)
+        a_sb = [slot("a%d" % f, [P, PACK, C1], F32) for f in range(G)]
+        gate_first = slot("gate_first", [P, C1], F32)
+        gate_rest = slot("gate_rest", [P, T - C1], F32)
 
         def load_scales(tile, rows):
             matrices = rows.shape[0]
@@ -64,11 +60,11 @@ def tile_moe_hib_relu_kernel(
                     rows[:, ROWS * q : ROWS * (q + 1), :].bitcast(I32),
                 )
 
-        make_identity(nc, ident[:])
         nc.gpsimd.memset(wet_s[1][:].bitcast(I32), 0)
         nc.gpsimd.memset(wgt_s[:].bitcast(I32), 0)
 
         wet_words_p = wet_words.rearrange("e s p i d -> p (e s) (i d)")
+        wet_rows = wet_scales.rearrange("e s b i -> (e s) b i")
 
         def load_wet(e0, e1):
             tile = slot("wet_w%d" % e0, [P, e1 - e0, H], U32)
@@ -76,235 +72,151 @@ def tile_moe_hib_relu_kernel(
             for e in range(e0, e1):
                 wet_w[e] = tile[:, e - e0, :]
 
+        def load_a(f):
+            nc.sync.dma_start(a_sb[f][:], a[:, C1 * f : C1 * (f + 1)].rearrange("(p t) j -> p t j", t=PACK))
+
         nc.sync.dma_start(dst_l[:], dst)
         load_scales(dy_s, dy_scales.to_broadcast([QUAD // ROWS, QUADS * ROWS, T]))
         nc.sync.dma_start(dy_w[:].bitcast(I32), dy_words.rearrange("s p t d -> p (s t d)").bitcast(I32))
-        wet0 = [slot("wet0_first", [P, P], U32), slot("wet0_rest", [P, H - P], U32)]
-        nc.sync.dma_start(wet0[0][:].bitcast(I32), wet_words_p[:, 0, 0 : PACK * P].bitcast(I32))
-        load_scales(wet_s[0], wet_scales.rearrange("e s b i -> (e s) b i"))
-        nc.sync.dma_start(gate_rows[:], gate[:, 0:C1])
-        nc.sync.dma_start(wet0[1][:].bitcast(I32), wet_words_p[:, 0, PACK * P : PACK * H].bitcast(I32))
+        load_wet(0, 1)
+        load_scales(wet_s[0], wet_rows)
+        load_wet(1, 2)
+        nc.sync.dma_start(gate_first[:], gate[:, 0:C1])
         nc.sync.dma_start(offs2_l[:], offs2)
-        load_wet(1, EPG)
-        with nc.allow_non_contiguous_dma(reason="one weight a partition and expert"):
-            nc.sync.dma_start(gate_cols[:], gate[0:1, C1:T].rearrange("r (e u) -> u (r e)", u=C2))
-        load_wet(EPG, HALF_E)
-        for q in range(QUADS):
-            nc.sync.dma_start(
-                wet_s[1][QUAD * q : QUAD * q + ROWS * SHARE, :].bitcast(I32),
-                wet_s[0][QUAD * q + ROWS * SHARE : QUAD * (q + 1), :].bitcast(I32),
-            )
-        load_wet(HALF_E, E)
-        nc.sync.dma_start(a_first[:], a[:, 0:C1].rearrange("(c p) j -> p c j", p=P))
-        for t in range(PACK):
-            nc.sync.dma_start(a_rest[t][:], a[:, C1:T].rearrange("(p t) j -> p t j", t=PACK)[:, t, :])
+        load_wet(2, 4)
+        nc.sync.dma_start(gate_rest[:], gate[:, C1:T])
+        load_a(0)
+        load_a(1)
+        load_scales(wet_s[1], wet_rows[SHARE:E])
+        load_wet(4, 6)
+        load_a(2)
+        load_wet(6, 8)
+        load_a(3)
         load_scales(wgt_s, wgt_scales.rearrange("f s b k -> (f s) b k"))
-        for f in range(G):
-            nc.sync.dma_start(wgt_w[f][:].bitcast(I32), wgt_words[f].rearrange("s p k d -> p (s k d)").bitcast(I32))
+        nc.sync.dma_start(wgt_w[:].bitcast(I32), wgt_words.rearrange("f s p k d -> p (f s) (k d)").bitcast(I32))
         nc.sync.dma_start(offs_l[:], offs)
 
         def cols(lo, hi):
             return slice(lo // PER_COL, hi // PER_COL)
 
-        def gather(src, dtype, lo, hi, tag):
-            tile = slot("gq_%d_%d" % (lo, hi), [P, hi - lo], dtype, tag)
+        gq_w, gq_s = {}, {}
+
+        def gather(views, src, dtype, lo, hi, name, tag=None):
+            tile = slot(name, [P, hi - lo], dtype, tag)
             nc.vector.tensor_copy(tile[:], src[:].indirect(dst_l[:, cols(lo, hi)]))
-            return [tile[:, m - lo : m - lo + C2] for m in range(lo, hi, C2)]
+            for m in range(lo, hi, C2):
+                views[m // C2] = tile[:, m - lo : m - lo + C2]
 
-        gq_s = gather(dy_s, U8, 0, HALF + C2, "gq_s_first")
-        gq_w = gather(dy_w, U32, 0, C2, "gq_w0")
-        gq_w.extend(gather(dy_w, U32, C2, T - C2, "gq_w1"))
+        staged = {}
 
-        def wet_scale(e):
-            return wet_s[e // SHARE][ROWS * (e % SHARE) : P, :]
-
-        def wet_block(e, c):
-            if e:
-                return wet_w[e][:, P * c : P * (c + 1)]
-            return wet0[1][:, P * (c - 1) : P * c] if c else wet0[0][:]
-
-        def first_group(z, c, e0, e1):
-            cs = slice(P * c, P * (c + 1))
-            z_ps = psum.tile([P, (e1 - e0) * C2], F32, name="z_ps", tag="z", bufs=3)
-            for e in range(e0, e1):
-                nc.tensor.matmul_mx(
-                    out=z_ps[:, C2 * (e - e0) : C2 * (e - e0 + 1)],
-                    lhsT=wet_block(e, c).bitcast(FP8X4),
-                    lhsT_scale=wet_scale(e)[:, cs],
-                    rhs=gq_w[e].bitcast(FP8X4),
-                    rhs_scale=gq_s[e],
-                    start=True,
-                    stop=True,
-                )
-            sums = slot("sums%d_%d" % (c, e0), [P, (e1 - e0) * C2], F32)
-            nc.scalar.copy(sums[:], z_ps[:])
-            nc.gpsimd.tensor_tensor(z, sums[:], gate_rows[:, C2 * e0 : C2 * e1], MULT)
-
-        zt = {e: slot("zt%d" % e, [P, PACK, C2], F32) for e in range(EPG, E)}
-
-        def product(e):
-            zt_ps = psum.tile([P, H], F32, name="zt_ps", tag="zt")
-            nc.tensor.matmul_mx(
-                out=zt_ps[:],
-                lhsT=gq_w[e].bitcast(FP8X4),
-                lhsT_scale=gq_s[e],
-                rhs=wet_w[e].bitcast(FP8X4),
-                rhs_scale=wet_scale(e),
-                start=True,
-                stop=True,
-            )
-            nc.scalar.activation(
-                zt[e][:],
-                zt_ps[:].rearrange("m (p t) -> m t p", t=PACK),
-                ACT.Copy,
-                scale=gate_cols[:, e - EPG : e - EPG + 1],
-            )
-
-        def turn(z, t, e0, e1):
-            for b0 in range(e0, e1, BANK):
-                b1 = min(b0 + BANK, e1)
-                z_ps = psum.tile([P, (b1 - b0) * C2], F32, name="z_ps", tag="z", bufs=3)
-                for e in range(b0, b1):
-                    nc.tensor.transpose(z_ps[:, C2 * (e - b0) : C2 * (e - b0 + 1)], zt[e][:, t, :], ident[:])
-                nc.scalar.copy(z[:, C2 * (b0 - e0) : C2 * (b1 - e0)], z_ps[:])
-
-        def piece(t, e0, e1):
-            return slot("z%d_%d" % (t, e0), [P, (e1 - e0) * C2], F32)
-
-        def scatter_z(win, z, e0, e1):
-            nc.vector.tensor_copy(win[:].indirect(offs2_l[:, cols(C2 * e0, C2 * e1)]), z[:])
-
-        mask = {}
-
-        def make_mask(key, values, positive):
-            sign = keep.tile([P, HALF], BF16, name="sign", bufs=2)
-            width = values.shape[1]
-            nc.scalar.activation(sign[:, 0:width], values, ACT.Sign)
-            nc.scalar.activation(positive, sign[:, 0:width], ACT.Relu)
-            mask[key] = positive
-
-        dx = [slot("dx%d" % c, [P, T], F32) for c in range(K // P)]
-
-        def quantise_and_multiply(h, da, blocks):
-            da_w = slot("da_w%d" % h, [P, HALF], U32)
-            da_s = slot("da_s%d" % h, [P, HALF], U8)
-            nc.vector.quantize_mx(out=da_w[:].bitcast(FP8X4), scales=da_s[:], in_=da[:].rearrange("p j t -> p (j t)"))
-            for c in blocks:
-                ks = slice(P * c, P * (c + 1))
-                dx_ps = psum.tile([P, HALF], F32, name="dx_ps", tag="dx", bufs=3)
-                for u in range(G // 2):
-                    js = slice(C1 * u, C1 * (u + 1))
+        def first_product(f, pair):
+            z_ps = psum.tile([P, 2, C1], F32, name="z_ps", tag="z", bufs=4)
+            for u, c in enumerate(pair):
+                cs = slice(P * c, P * (c + 1))
+                for e in range(EPG * f, EPG * (f + 1)):
                     nc.tensor.matmul_mx(
-                        out=dx_ps[:, js],
-                        lhsT=wgt_w[2 * h + u][:, ks].bitcast(FP8X4),
-                        lhsT_scale=wgt_s[ROWS * (2 * h + u) : P, ks],
-                        rhs=da_w[:, js].bitcast(FP8X4),
-                        rhs_scale=da_s[:, js],
+                        out=z_ps[:, u, C2 * (e % EPG) : C2 * (e % EPG + 1)],
+                        lhsT=wet_w[e][:, cs].bitcast(FP8X4),
+                        lhsT_scale=wet_s[e // SHARE][ROWS * (e % SHARE) : P, cs],
+                        rhs=gq_w[e].bitcast(FP8X4),
+                        rhs_scale=gq_s[e],
                         start=True,
                         stop=True,
                     )
-                nc.scalar.copy(dx[c][:, HALF * h : HALF * (h + 1)], dx_ps[:])
+            z = slot("z%d_%d" % (f, pair[0]), [P, 2, C1], F32)
+            weights = gate_rest[:, C1 * (f - 1) : C1 * f] if f else gate_first[:]
+            nc.vector.tensor_tensor(z[:], z_ps[:], weights.unsqueeze(1).to_broadcast([P, 2, C1]), ALU.mult)
+            for u, c in enumerate(pair):
+                staged[f, c] = z[:, u, :]
 
-        def scatter_dx(win, c, lo, hi):
-            nc.vector.tensor_copy(win[:].indirect(offs_l[:, cols(lo, hi)]), dx[c][:, lo:hi])
-
-        def window(name, tag=None):
-            return slot(name, [P, T], F32, tag)
-
-        first = [window("zwin%d" % t) for t in range(PACK)]
-        for c in range(PACK):
-            e1 = 1 if c < 2 else EPG
-            z = piece(c, 0, e1)
-            first_group(z[:], c, 0, e1)
-            scatter_z(first[c], z, 0, e1)
-            if c < PACK - 1:
-                e = HALF_E + 1 + c
-                gq_s.extend(gather(dy_s, U8, C2 * e, C2 * (e + 1), "sums%d_0" % c))
+        def scatter(engine, win, offsets, values):
+            if engine == "vector":
+                nc.vector.tensor_copy(win[:].indirect(offsets), values)
             else:
-                gq_w.extend(gather(dy_w, U32, T - C2, T, "sums%d_0" % c))
-        second = [piece(t, 1, HALF_E) for t in (0, 1)]
-        for t in (0, 1):
-            first_group(second[t][:, 0:C2], t, 1, EPG)
-        for e in range(EPG, HALF_E):
-            product(e)
-        for t in (0, 1):
-            turn(second[t][:, C2:], t, EPG, HALF_E)
-            scatter_z(first[t], second[t], 1, HALF_E)
-        for e in range(HALF_E, E):
-            product(e)
-        late = {t: window("zlate%d" % t) for t in (2, 3)}
-        for t in (2, 3):
-            z = piece(t, EPG, E)
-            turn(z, t, EPG, E)
-            scatter_z(late[t], z, EPG, E)
-        z_last = [piece(t, HALF_E, E) for t in (0, 1)]
-        for t in (0, 1):
-            turn(z_last[t], t, HALF_E, E)
+                nc.scalar.activation(win[:].indirect(offsets), values, ACT.Copy)
 
-        for c in (2, 0):
-            tile = slot("mask_first%d" % c, [P, 2 * C1], BF16)
-            make_mask(("first", c), a_first[:, c : c + 2, :].rearrange("p c j -> p (c j)"), tile[:])
-        for h, t in ((0, 0), (0, 1), (0, 2), (1, 2), (0, 3), (1, 3)):
-            lo, hi = (C1, HALF) if h == 0 else (HALF, T)
-            tile = slot("mask%d_%d" % (h, t), [P, hi - lo], BF16)
-            make_mask((h, t), a_rest[t][:, lo - C1 : hi - C1], tile[:])
+        planes = [slot("planes%d" % f, [P, PACK, C1], F32) for f in range(G)]
 
-        da0 = slot("da0", [P, HALF, PACK], BF16)
-        masked = slot("masked", [P, PACK, C1], F32)
-        for c in (2, 3, 0, 1):
-            m = mask["first", c - c % 2][:, C1 * (c % 2) : C1 * (c % 2 + 1)]
-            nc.gpsimd.tensor_tensor(masked[:, c, :], first[c][:, 0:C1], m, MULT)
-        for b in range(C1 // P):
-            js = slice(P * b, P * (b + 1))
-            rows_ps = psum.tile([P, H], F32, name="rows_ps", tag="zt")
-            for c in range(PACK):
-                nc.tensor.transpose(rows_ps[:, P * c : P * (c + 1)], masked[:, c, js], ident[:])
-            rows = slot("rows%d" % b, [P, H], BF16)
-            nc.scalar.copy(rows[:], rows_ps[:])
-            pairs_ps = psum.tile([P, 2, P], F32, name="pairs_ps", tag="z", bufs=3)
-            for u in range(2):
-                nc.tensor.transpose(pairs_ps[:, u, :], rows[:].bitcast(F32)[:, u : H // 2 : 2], ident[:])
-            nc.scalar.copy(da0[:, js, :].bitcast(F32), pairs_ps[:].rearrange("p u j -> p j u"))
+        def scatter_z(engine, f, c, tag=None):
+            win = slot("zwin%d_%d" % (f, c), [P, T], F32, tag)
+            scatter(engine, win, offs2_l[:, cols(C1 * f, C1 * (f + 1))], staged[f, c])
+            nc.sync.dma_start(planes[f][QUAD * c : QUAD * (c + 1), :, :], win[:, C1 * f : C1 * (f + 1)])
 
-        planar = [slot("planar0", [P, PACK, C1], BF16), slot("planar1", [P, PACK, HALF], BF16)]
-        start = (C1, HALF)
+        mask = {}
 
-        def apply_mask(win, h, t, lo, hi):
-            js = slice(lo - start[h], hi - start[h])
-            nc.gpsimd.tensor_tensor(planar[h][:, t, js], win[:, lo:hi], mask[h, t][:, js], MULT)
+        def make_mask(f):
+            mask[f] = slot("mask%d" % f, [P, C1, PACK], BF16)
+            nc.vector.tensor_scalar(mask[f][:], a_sb[f][:].rearrange("p t j -> p j t"), 0.0, None, ALU.is_gt)
 
-        def interleave(da, h, lo, hi):
-            js = slice(lo - start[h], hi - start[h])
-            nc.scalar.copy(da[:, lo - HALF * h : hi - HALF * h, :], planar[h][:, :, js].rearrange("p t j -> p j t"))
+        dx_ps = {}
 
-        for t in (0, 1):
-            apply_mask(first[t], 0, t, C1, HALF)
-        apply_mask(late[2], 0, 2, C1, HALF)
-        apply_mask(late[2], 1, 2, HALF, T)
-        for lo in range(C1, HALF, C2):
-            apply_mask(late[3], 0, 3, lo, lo + C2)
-            interleave(da0, 0, lo, lo + C2)
-        apply_mask(late[3], 1, 3, HALF, T)
+        def quantise_and_multiply(f):
+            da = slot("da%d" % f, [P, C1, PACK], BF16, "da")
+            nc.gpsimd.tensor_tensor(da[:], planes[f][:].rearrange("p t j -> p j t"), mask[f][:], ALU.mult)
+            da_w = slot("da_w%d" % f, [P, C1], U32)
+            da_s = slot("da_s%d" % f, [P, C1], U8)
+            nc.vector.quantize_mx(out=da_w[:].bitcast(FP8X4), scales=da_s[:], in_=da[:].rearrange("p j t -> p (j t)"))
+            for engine, pair in (("scalar", (1, 3)), ("vector", (0, 2))):
+                bank = psum.tile([P, 2, C1], F32, name="dx_ps", tag="dx_" + engine)
+                for u, c in enumerate(pair):
+                    ks = slice(P * c, P * (c + 1))
+                    nc.tensor.matmul_mx(
+                        out=bank[:, u, :],
+                        lhsT=wgt_w[:, f, ks].bitcast(FP8X4),
+                        lhsT_scale=wgt_s[ROWS * f : P, ks],
+                        rhs=da_w[:].bitcast(FP8X4),
+                        rhs_scale=da_s[:],
+                        start=True,
+                        stop=True,
+                    )
+                dx_ps[f, engine] = bank
 
-        last = [window("zlast0")]
-        scatter_z(last[0], z_last[0], HALF_E, E)
-        quantise_and_multiply(0, da0, (1, 2, 3, 0))
-        mask_last = slot("mask_last", [P, 2, HALF], BF16, "da0")
-        for t in (0, 1):
-            make_mask((1, t), a_rest[t][:, HALF - C1 : T - C1], mask_last[:, t, :])
-        last.append(window("zlast1", "planar0"))
-        scatter_z(last[1], z_last[1], HALF_E, E)
-        da1 = slot("da1", [P, HALF, PACK], BF16, "da_w0")
-        for t in (0, 1):
-            apply_mask(last[t], 1, t, HALF, T)
-        interleave(da1, 1, HALF, T)
+        owin = {}
 
-        owin = [slot("owin0", [P, 2 * T], F32), window("owin1"), window("owin2")]
-        for c in (1, 2):
-            scatter_dx(owin[c], c, 0, HALF)
-        quantise_and_multiply(1, da1, (0, 1, 2, 3))
-        owin.append(window("owin3", "planar1"))
-        scatter_dx(owin[3], 3, 0, HALF)
-        for c in range(K // P):
-            scatter_dx(owin[c], c, HALF if c else 0, T)
-            nc.sync.dma_start(out[P * c : P * (c + 1), :], owin[c][:, 0:T])
+        def scatter_dx(f):
+            for engine, pair in (("scalar", (1, 3)), ("vector", (0, 2))):
+                held = engine == "vector" and f + 1 < G
+                dx = slot("dx%d_%s" % (f, engine), [P, 2, C1], F32, "planes%d" % (f + 1) if held else None)
+                if engine == "vector":
+                    nc.vector.tensor_copy(dx[:], dx_ps[f, engine][:])
+                else:
+                    nc.scalar.copy(dx[:], dx_ps[f, engine][:])
+                for u, c in enumerate(pair):
+                    if f == 0:
+                        owin[c] = slot("owin%d" % c, [P, T], F32, "zwin0_%d" % c)
+                    scatter(engine, owin[c], offs_l[:, cols(C1 * f, C1 * (f + 1))], dx[:, u, :])
+                    if f == G - 1:
+                        nc.sync.dma_start(out[P * c : P * (c + 1), :], owin[c][:])
+
+        gather(gq_s, dy_s, U8, 0, HALF, "gq_s0")
+        gather(gq_w, dy_w, U32, 0, HALF, "gq_w0")
+        first_product(0, (0, 3))
+        first_product(0, (1, 2))
+        for c in range(3):
+            scatter_z("scalar", 0, c)
+        scatter_z("vector", 0, 3)
+        gather(gq_s, dy_s, U8, HALF, T, "gq_s1", "gate_first")
+        first_product(1, (0, 3))
+        gather(gq_w, dy_w, U32, HALF, T, "gq_w1", "dy_s")
+        first_product(1, (1, 2))
+        for c in range(3):
+            scatter_z("scalar", 1, c)
+        scatter_z("vector", 1, 3)
+        for f in (2, 3):
+            first_product(f, (0, 3))
+            first_product(f, (1, 2))
+        for c in range(2):
+            scatter_z("scalar", 2, c)
+        scatter_z("vector", 2, 3)
+        scatter_z("vector", 2, 2)
+        for f in range(G):
+            make_mask(f)
+        quantise_and_multiply(0)
+        for c in range(2):
+            scatter_z("scalar", 3, c)
+        scatter_z("vector", 3, 3, "planes0")
+        scatter_z("vector", 3, 2, "mask0")
+        for f in range(G):
+            if f + 1 < G:
+                quantise_and_multiply(f + 1)
+            scatter_dx(f)

@@ -24,7 +24,8 @@ QUAD = 32
 QUADS = P // QUAD
 ROWS = 4
 SHARE = 4
-HALF = T // 2
+STEP = 64
+LINE = 4
 
 
 def tile_moe_hib_relu_kernel(
@@ -46,9 +47,8 @@ def tile_moe_hib_relu_kernel(
         dy_s = slot("dy_s", [P, T], U8)
         wet_w = {}
         wet_s = [slot("wet_s%d" % h, [P, H], U8) for h in range(E // SHARE)]
-        wgt_w = slot("wgt_w", [P, G, K], U32)
         wgt_s = slot("wgt_s", [P, K], U8)
-        a_sb = [slot("a%d" % f, [P, PACK, C1], F32) for f in range(G)]
+        a_sb = {}
         gate_first = slot("gate_first", [P, C1], F32)
         gate_rest = slot("gate_rest", [P, T - C1], F32)
 
@@ -72,29 +72,28 @@ def tile_moe_hib_relu_kernel(
             for e in range(e0, e1):
                 wet_w[e] = tile[:, e - e0, :]
 
-        def load_a(f):
-            nc.sync.dma_start(a_sb[f][:], a[:, C1 * f : C1 * (f + 1)].rearrange("(p t) j -> p t j", t=PACK))
+        def load_a(f0, f1, tag=None):
+            tile = slot("a%d" % f0, [P, PACK, (f1 - f0) * C1], F32, tag)
+            nc.sync.dma_start(tile[:], a[:, C1 * f0 : C1 * f1].rearrange("(p t) j -> p t j", t=PACK))
+            for f in range(f0, f1):
+                a_sb[f] = tile[:, :, C1 * (f - f0) : C1 * (f - f0 + 1)]
 
         nc.sync.dma_start(dst_l[:], dst)
         load_scales(dy_s, dy_scales.to_broadcast([QUAD // ROWS, QUADS * ROWS, T]))
-        nc.sync.dma_start(dy_w[:].bitcast(I32), dy_words.rearrange("s p t d -> p (s t d)").bitcast(I32))
-        load_wet(0, 1)
-        load_scales(wet_s[0], wet_rows)
-        load_wet(1, 2)
-        nc.sync.dma_start(gate_first[:], gate[:, 0:C1])
         nc.sync.dma_start(offs2_l[:], offs2)
+        nc.sync.dma_start(dy_w[:].bitcast(I32), dy_words.rearrange("s p t d -> p (s t d)").bitcast(I32))
+        load_wet(0, 2)
+        load_scales(wet_s[0], wet_rows)
+        nc.sync.dma_start(gate_first[:], gate[:, 0:C1])
         load_wet(2, 4)
         nc.sync.dma_start(gate_rest[:], gate[:, C1:T])
-        load_a(0)
-        load_a(1)
-        load_scales(wet_s[1], wet_rows[SHARE:E])
+        load_a(0, 1)
         load_wet(4, 6)
-        load_a(2)
+        load_scales(wet_s[1], wet_rows[SHARE:E])
+        load_a(1, 2)
         load_wet(6, 8)
-        load_a(3)
-        load_scales(wgt_s, wgt_scales.rearrange("f s b k -> (f s) b k"))
-        nc.sync.dma_start(wgt_w[:].bitcast(I32), wgt_words.rearrange("f s p k d -> p (f s) (k d)").bitcast(I32))
-        nc.sync.dma_start(offs_l[:], offs)
+        load_a(2, 3)
+        load_a(3, 4)
 
         def cols(lo, hi):
             return slice(lo // PER_COL, hi // PER_COL)
@@ -110,7 +109,7 @@ def tile_moe_hib_relu_kernel(
         staged = {}
 
         def first_product(f, pair):
-            z_ps = psum.tile([P, 2, C1], F32, name="z_ps", tag="z", bufs=4)
+            z_ps = psum.tile([P, len(pair), C1], F32, name="z_ps", tag="z", bufs=4)
             for u, c in enumerate(pair):
                 cs = slice(P * c, P * (c + 1))
                 for e in range(EPG * f, EPG * (f + 1)):
@@ -123,9 +122,9 @@ def tile_moe_hib_relu_kernel(
                         start=True,
                         stop=True,
                     )
-            z = slot("z%d_%d" % (f, pair[0]), [P, 2, C1], F32)
+            z = slot("z%d_%d" % (f, pair[0]), [P, len(pair), C1], F32)
             weights = gate_rest[:, C1 * (f - 1) : C1 * f] if f else gate_first[:]
-            nc.vector.tensor_tensor(z[:], z_ps[:], weights.unsqueeze(1).to_broadcast([P, 2, C1]), ALU.mult)
+            nc.vector.tensor_tensor(z[:], z_ps[:], weights.unsqueeze(1).to_broadcast([P, len(pair), C1]), ALU.mult)
             for u, c in enumerate(pair):
                 staged[f, c] = z[:, u, :]
 
@@ -144,16 +143,25 @@ def tile_moe_hib_relu_kernel(
 
         mask = {}
 
+        def by_lines(ap):
+            return ap.rearrange("p t (c i) -> p c t i", i=LINE)
+
         def make_mask(f):
-            mask[f] = slot("mask%d" % f, [P, C1, PACK], BF16)
-            nc.vector.tensor_scalar(mask[f][:], a_sb[f][:].rearrange("p t j -> p j t"), 0.0, None, ALU.is_gt)
+            mask[f] = slot("mask%d" % f, [P, C1 // LINE, PACK, LINE], BF16)
+            nc.vector.tensor_scalar(mask[f][:], by_lines(a_sb[f]), 0.0, None, ALU.is_gt)
 
         dx_ps = {}
 
-        def quantise_and_multiply(f):
-            da = slot("da%d" % f, [P, C1, PACK], BF16, "da")
-            nc.gpsimd.tensor_tensor(da[:], planes[f][:].rearrange("p t j -> p j t"), mask[f][:], ALU.mult)
-            da_w = slot("da_w%d" % f, [P, C1], U32)
+        def quantise_and_multiply(f, tag=None):
+            da = slot("da%d" % f, [P, C1, PACK], BF16)
+            for lo in range(0, C1, STEP):
+                nc.gpsimd.tensor_tensor(
+                    da[:, lo : lo + STEP, :].rearrange("p (c i) t -> p c t i", i=LINE),
+                    by_lines(planes[f][:, :, lo : lo + STEP]),
+                    mask[f][:, lo // LINE : (lo + STEP) // LINE, :, :],
+                    ALU.mult,
+                )
+            da_w = slot("da_w%d" % f, [P, C1], U32, tag)
             da_s = slot("da_s%d" % f, [P, C1], U8)
             nc.vector.quantize_mx(out=da_w[:].bitcast(FP8X4), scales=da_s[:], in_=da[:].rearrange("p j t -> p (j t)"))
             for engine, pair in (("scalar", (1, 3)), ("vector", (0, 2))):
@@ -173,50 +181,62 @@ def tile_moe_hib_relu_kernel(
 
         owin = {}
 
-        def scatter_dx(f):
-            for engine, pair in (("scalar", (1, 3)), ("vector", (0, 2))):
-                held = engine == "vector" and f + 1 < G
-                dx = slot("dx%d_%s" % (f, engine), [P, 2, C1], F32, "planes%d" % (f + 1) if held else None)
-                if engine == "vector":
-                    nc.vector.tensor_copy(dx[:], dx_ps[f, engine][:])
-                else:
-                    nc.scalar.copy(dx[:], dx_ps[f, engine][:])
-                for u, c in enumerate(pair):
-                    if f == 0:
-                        owin[c] = slot("owin%d" % c, [P, T], F32, "zwin0_%d" % c)
-                    scatter(engine, owin[c], offs_l[:, cols(C1 * f, C1 * (f + 1))], dx[:, u, :])
-                    if f == G - 1:
-                        nc.sync.dma_start(out[P * c : P * (c + 1), :], owin[c][:])
+        def scatter_dx(engine, f, c, values):
+            if f == 0:
+                owin[c] = slot("owin%d" % c, [P, T], F32, "zwin0_%d" % c)
+            scatter(engine, owin[c], offs_l[:, cols(C1 * f, C1 * (f + 1))], values)
+            if f == G - 1:
+                nc.sync.dma_start(out[P * c : P * (c + 1), :], owin[c][:])
 
-        gather(gq_s, dy_s, U8, 0, HALF, "gq_s0")
-        gather(gq_w, dy_w, U32, 0, HALF, "gq_w0")
-        first_product(0, (0, 3))
-        first_product(0, (1, 2))
+        def scalar_dx(f):
+            dx = slot("dx%d_scalar" % f, [P, 2, C1], F32)
+            nc.scalar.copy(dx[:], dx_ps[f, "scalar"][:])
+            for u, c in enumerate((1, 3)):
+                scatter_dx("scalar", f, c, dx[:, u, :])
+
+        def vector_dx(f, u0, u1, tag=None):
+            dx = slot("dx%d_vector%d" % (f, u0), [P, u1 - u0, C1], F32, tag)
+            nc.vector.tensor_copy(dx[:], dx_ps[f, "vector"][:, u0:u1, :])
+            for u in range(u0, u1):
+                scatter_dx("vector", f, 2 * u, dx[:, u - u0, :])
+
+        gather(gq_s, dy_s, U8, 0, 5 * C2, "gq_s0")
+        gather(gq_w, dy_w, U32, 0, 2 * C2, "gq_w0")
+        gather(gq_w, dy_w, U32, 2 * C2, 6 * C2, "gq_w1")
+        for pair in ((0,), (3, 1), (2,)):
+            first_product(0, pair)
         for c in range(3):
             scatter_z("scalar", 0, c)
         scatter_z("vector", 0, 3)
-        gather(gq_s, dy_s, U8, HALF, T, "gq_s1", "gate_first")
+        load_scales(wgt_s, wgt_scales.rearrange("f s b k -> (f s) b k"))
+        wgt_w = slot("wgt_w", [P, G, K], U32)
+        nc.sync.dma_start(wgt_w[:].bitcast(I32), wgt_words.rearrange("f s p k d -> p (f s) (k d)").bitcast(I32))
+        nc.sync.dma_start(offs_l[:], offs)
+        gather(gq_s, dy_s, U8, 5 * C2, T, "gq_s1", "gate_first")
         first_product(1, (0, 3))
-        gather(gq_w, dy_w, U32, HALF, T, "gq_w1", "dy_s")
+        gather(gq_w, dy_w, U32, 6 * C2, T, "gq_w2", "dy_s")
         first_product(1, (1, 2))
+        make_mask(0)
         for c in range(3):
             scatter_z("scalar", 1, c)
         scatter_z("vector", 1, 3)
-        for f in (2, 3):
-            first_product(f, (0, 3))
-            first_product(f, (1, 2))
-        for c in range(2):
+        make_mask(1)
+        for f, pair in ((2, (0, 3)), (2, (1, 2)), (3, (0, 1)), (3, (3,)), (3, (2,))):
+            first_product(f, pair)
+        for c in range(3):
             scatter_z("scalar", 2, c)
-        scatter_z("vector", 2, 3)
-        scatter_z("vector", 2, 2)
-        for f in range(G):
-            make_mask(f)
-        quantise_and_multiply(0)
         for c in range(2):
             scatter_z("scalar", 3, c)
-        scatter_z("vector", 3, 3, "planes0")
-        scatter_z("vector", 3, 2, "mask0")
-        for f in range(G):
-            if f + 1 < G:
-                quantise_and_multiply(f + 1)
-            scatter_dx(f)
+        make_mask(2)
+        scatter_z("vector", 2, 3, "a2")
+        make_mask(3)
+        scatter_z("vector", 3, 3, "a3")
+        quantise_and_multiply(0, "z3_3")
+        scatter_z("vector", 3, 2, "planes0")
+        for f in range(G - 1):
+            scalar_dx(f)
+            vector_dx(f, 0, 1)
+            quantise_and_multiply(f + 1, "planes%d" % f if f else None)
+            vector_dx(f, 1, 2, "planes%d" % (f + 1))
+        scalar_dx(3)
+        vector_dx(3, 0, 2)

@@ -24,8 +24,6 @@ QUAD = 32
 QUADS = P // QUAD
 ROWS = 4
 SHARE = 4
-STEP = 64
-LINE = 4
 
 
 def tile_moe_hib_relu_kernel(
@@ -45,8 +43,9 @@ def tile_moe_hib_relu_kernel(
         offs_l = keep.tile([P, T // PER_COL], U16, name="offs_l")
         dy_w = slot("dy_w", [P, T], U32)
         dy_s = slot("dy_s", [P, T], U8)
-        wet_w = {}
+        wet_w, wet_pair = {}, {}
         wet_s = [slot("wet_s%d" % h, [P, H], U8) for h in range(E // SHARE)]
+        wet_sp = [slot("wet_sp%d" % h, [P, H], U8) for h in range(E // SHARE)]
         wgt_s = slot("wgt_s", [P, K], U8)
         a_sb = {}
         gate_first = slot("gate_first", [P, C1], F32)
@@ -69,8 +68,18 @@ def tile_moe_hib_relu_kernel(
         def load_wet(e0, e1):
             tile = slot("wet_w%d" % e0, [P, e1 - e0, H], U32)
             nc.sync.dma_start(tile[:].bitcast(I32), wet_words_p[:, e0:e1, :].bitcast(I32))
+            wet_pair[e0 // EPG] = tile
             for e in range(e0, e1):
                 wet_w[e] = tile[:, e - e0, :]
+
+        wgt_words_p = wgt_words.rearrange("f s p k d -> p (f s) (k d)")
+        wgt_w = {}
+
+        def load_wgt(f0, f1):
+            tile = slot("wgt_w%d" % f0, [P, f1 - f0, K], U32)
+            nc.sync.dma_start(tile[:].bitcast(I32), wgt_words_p[:, f0:f1, :].bitcast(I32))
+            for f in range(f0, f1):
+                wgt_w[f] = tile[:, f - f0, :]
 
         def load_a(f0, f1, tag=None):
             tile = slot("a%d" % f0, [P, PACK, (f1 - f0) * C1], F32, tag)
@@ -90,10 +99,14 @@ def tile_moe_hib_relu_kernel(
         load_a(0, 1)
         load_wet(4, 6)
         load_scales(wet_s[1], wet_rows[SHARE:E])
-        load_a(1, 2)
         load_wet(6, 8)
+        load_a(1, 2)
         load_a(2, 3)
         load_a(3, 4)
+        load_scales(wgt_s, wgt_scales.rearrange("f s b k -> (f s) b k"))
+        load_wgt(0, 2)
+        nc.sync.dma_start(offs_l[:], offs)
+        load_wgt(2, 4)
 
         def cols(lo, hi):
             return slice(lo // PER_COL, hi // PER_COL)
@@ -106,17 +119,38 @@ def tile_moe_hib_relu_kernel(
             for m in range(lo, hi, C2):
                 views[m // C2] = tile[:, m - lo : m - lo + C2]
 
+        wet_p = {}
+
+        def by_planes(ap):
+            return ap.rearrange("p (t m) -> p m t", t=PACK)
+
+        def permute_first(e):
+            wet_p[e] = slot("wet_p%d" % e, [P, H], U32)
+            nc.scalar.copy(by_planes(wet_p[e][:]), wet_w[e].rearrange("p (m t) -> p m t", t=PACK))
+
+        def permute_group(f):
+            tile = slot("wet_p%d" % (EPG * f), [P, EPG, H], U32)
+            nc.vector.tensor_copy(
+                tile[:].rearrange("p e (t m) -> p e m t", t=PACK),
+                wet_pair[f][:].rearrange("p e (m t) -> p e m t", t=PACK),
+            )
+            for u in range(EPG):
+                wet_p[EPG * f + u] = tile[:, u, :]
+
+        def permute_scales(h):
+            nc.vector.tensor_copy(by_planes(wet_sp[h][:]), wet_s[h][:].rearrange("p (m t) -> p m t", t=PACK))
+
         staged = {}
 
         def first_product(f, pair):
-            z_ps = psum.tile([P, len(pair), C1], F32, name="z_ps", tag="z", bufs=4)
+            z_ps = psum.tile([P, len(pair), C1], F32, name="z_ps", tag="z", bufs=3)
             for u, c in enumerate(pair):
                 cs = slice(P * c, P * (c + 1))
                 for e in range(EPG * f, EPG * (f + 1)):
                     nc.tensor.matmul_mx(
                         out=z_ps[:, u, C2 * (e % EPG) : C2 * (e % EPG + 1)],
-                        lhsT=wet_w[e][:, cs].bitcast(FP8X4),
-                        lhsT_scale=wet_s[e // SHARE][ROWS * (e % SHARE) : P, cs],
+                        lhsT=wet_p[e][:, cs].bitcast(FP8X4),
+                        lhsT_scale=wet_sp[e // SHARE][ROWS * (e % SHARE) : P, cs],
                         rhs=gq_w[e].bitcast(FP8X4),
                         rhs_scale=gq_s[e],
                         start=True,
@@ -134,109 +168,110 @@ def tile_moe_hib_relu_kernel(
             else:
                 nc.scalar.activation(win[:].indirect(offsets), values, ACT.Copy)
 
-        planes = [slot("planes%d" % f, [P, PACK, C1], F32) for f in range(G)]
-
-        def scatter_z(engine, f, c, tag=None):
-            win = slot("zwin%d_%d" % (f, c), [P, T], F32, tag)
-            scatter(engine, win, offs2_l[:, cols(C1 * f, C1 * (f + 1))], staged[f, c])
-            nc.sync.dma_start(planes[f][QUAD * c : QUAD * (c + 1), :, :], win[:, C1 * f : C1 * (f + 1)])
-
-        mask = {}
-
-        def by_lines(ap):
-            return ap.rearrange("p t (c i) -> p c t i", i=LINE)
+        mask, planar = {}, {}
 
         def make_mask(f):
-            mask[f] = slot("mask%d" % f, [P, C1 // LINE, PACK, LINE], BF16)
-            nc.vector.tensor_scalar(mask[f][:], by_lines(a_sb[f]), 0.0, None, ALU.is_gt)
+            mask[f] = slot("mask%d" % f, [P, PACK, C1], BF16)
+            nc.vector.tensor_scalar(mask[f][:], a_sb[f], 0.0, None, ALU.is_gt)
+
+        zwin = {}
+
+        def scatter_z(engine, f, t, tag=None):
+            zwin[f, t] = slot("zwin%d_%d" % (f, t), [P, T], F32, tag)
+            scatter(engine, zwin[f, t], offs2_l[:, cols(C1 * f, C1 * (f + 1))], staged[f, t])
+
+        def apply_mask(f, planes):
+            planar[f] = slot("planar%d" % f, [P, PACK, C1], BF16, "planar")
+            for t in planes:
+                nc.gpsimd.tensor_tensor(planar[f][:, t, :], zwin[f, t][:, C1 * f : C1 * (f + 1)], mask[f][:, t, :], ALU.mult)
 
         dx_ps = {}
 
         def quantise_and_multiply(f, tag=None):
             da = slot("da%d" % f, [P, C1, PACK], BF16)
-            for lo in range(0, C1, STEP):
-                nc.gpsimd.tensor_tensor(
-                    da[:, lo : lo + STEP, :].rearrange("p (c i) t -> p c t i", i=LINE),
-                    by_lines(planes[f][:, :, lo : lo + STEP]),
-                    mask[f][:, lo // LINE : (lo + STEP) // LINE, :, :],
-                    ALU.mult,
-                )
+            nc.gpsimd.tensor_scalar(da[:], planar[f][:].rearrange("p t j -> p j t"), 1.0, 0.0, ALU.mult, ALU.add)
             da_w = slot("da_w%d" % f, [P, C1], U32, tag)
             da_s = slot("da_s%d" % f, [P, C1], U8)
             nc.vector.quantize_mx(out=da_w[:].bitcast(FP8X4), scales=da_s[:], in_=da[:].rearrange("p j t -> p (j t)"))
-            for engine, pair in (("scalar", (1, 3)), ("vector", (0, 2))):
-                bank = psum.tile([P, 2, C1], F32, name="dx_ps", tag="dx_" + engine)
-                for u, c in enumerate(pair):
-                    ks = slice(P * c, P * (c + 1))
-                    nc.tensor.matmul_mx(
-                        out=bank[:, u, :],
-                        lhsT=wgt_w[:, f, ks].bitcast(FP8X4),
-                        lhsT_scale=wgt_s[ROWS * f : P, ks],
-                        rhs=da_w[:].bitcast(FP8X4),
-                        rhs_scale=da_s[:],
-                        start=True,
-                        stop=True,
-                    )
-                dx_ps[f, engine] = bank
+            if f % 2 == 0:
+                for c in (2, 0) if f == 0 else (0, 2):
+                    dx_ps[f // 2, c] = psum.tile([P, 2, C1], F32, name="dx_ps", tag="dx_vector", bufs=3)
+            dx_ps[f, "scalar"] = psum.tile([P, 2, C1], F32, name="dx_ps", tag="dx_scalar")
+            for c in ((1, 3, 2, 0), (1, 3, 0, 2), (1, 3, 0, 2), (0, 1, 3, 2))[f]:
+                ks = slice(P * c, P * (c + 1))
+                nc.tensor.matmul_mx(
+                    out=dx_ps[f, "scalar"][:, c // 2, :] if c % 2 else dx_ps[f // 2, c][:, f % 2, :],
+                    lhsT=wgt_w[f][:, ks].bitcast(FP8X4),
+                    lhsT_scale=wgt_s[ROWS * f : P, ks],
+                    rhs=da_w[:].bitcast(FP8X4),
+                    rhs_scale=da_s[:],
+                    start=True,
+                    stop=True,
+                )
 
         owin = {}
 
-        def scatter_dx(engine, f, c, values):
-            if f == 0:
+        def scatter_dx(engine, f0, f1, c, values):
+            if f0 == 0:
                 owin[c] = slot("owin%d" % c, [P, T], F32, "zwin0_%d" % c)
-            scatter(engine, owin[c], offs_l[:, cols(C1 * f, C1 * (f + 1))], values)
-            if f == G - 1:
+            scatter(engine, owin[c], offs_l[:, cols(C1 * f0, C1 * f1)], values)
+            if f1 == G:
                 nc.sync.dma_start(out[P * c : P * (c + 1), :], owin[c][:])
 
         def scalar_dx(f):
             dx = slot("dx%d_scalar" % f, [P, 2, C1], F32)
             nc.scalar.copy(dx[:], dx_ps[f, "scalar"][:])
             for u, c in enumerate((1, 3)):
-                scatter_dx("scalar", f, c, dx[:, u, :])
+                scatter_dx("scalar", f, f + 1, c, dx[:, u, :])
 
-        def vector_dx(f, u0, u1, tag=None):
-            dx = slot("dx%d_vector%d" % (f, u0), [P, u1 - u0, C1], F32, tag)
-            nc.vector.tensor_copy(dx[:], dx_ps[f, "vector"][:, u0:u1, :])
-            for u in range(u0, u1):
-                scatter_dx("vector", f, 2 * u, dx[:, u - u0, :])
+        def vector_dx(c, f0, f1, tag=None):
+            dx = slot("dx%d_vector%d" % (f0, c), [P, f1 - f0, C1], F32, tag)
+            nc.vector.tensor_copy(dx[:], dx_ps[f0 // 2, c][:, f0 % 2 : (f1 - 1) % 2 + 1, :])
+            scatter_dx("vector", f0, f1, c, dx[:].rearrange("p f j -> p (f j)"))
 
-        gather(gq_s, dy_s, U8, 0, 5 * C2, "gq_s0")
+        gather(gq_s, dy_s, U8, 0, 4 * C2, "gq_s0")
         gather(gq_w, dy_w, U32, 0, 2 * C2, "gq_w0")
-        gather(gq_w, dy_w, U32, 2 * C2, 6 * C2, "gq_w1")
-        for pair in ((0,), (3, 1), (2,)):
+        gather(gq_w, dy_w, U32, 2 * C2, 5 * C2, "gq_w1")
+        permute_first(0)
+        permute_first(1)
+        permute_scales(0)
+        gather(gq_w, dy_w, U32, 5 * C2, T, "gq_w2", "wet_s0")
+        for pair in ((0,), (1, 2), (3,)):
             first_product(0, pair)
-        for c in range(3):
-            scatter_z("scalar", 0, c)
-        scatter_z("vector", 0, 3)
-        load_scales(wgt_s, wgt_scales.rearrange("f s b k -> (f s) b k"))
-        wgt_w = slot("wgt_w", [P, G, K], U32)
-        nc.sync.dma_start(wgt_w[:].bitcast(I32), wgt_words.rearrange("f s p k d -> p (f s) (k d)").bitcast(I32))
-        nc.sync.dma_start(offs_l[:], offs)
-        gather(gq_s, dy_s, U8, 5 * C2, T, "gq_s1", "gate_first")
-        first_product(1, (0, 3))
-        gather(gq_w, dy_w, U32, 6 * C2, T, "gq_w2", "dy_s")
-        first_product(1, (1, 2))
-        make_mask(0)
-        for c in range(3):
-            scatter_z("scalar", 1, c)
-        scatter_z("vector", 1, 3)
+        for t in range(PACK):
+            scatter_z("scalar", 0, t)
+        gather(gq_s, dy_s, U8, 4 * C2, T, "gq_s1", "gate_first")
+        for f in range(1, G):
+            if f == 2:
+                make_mask(0)
+                apply_mask(0, range(PACK))
+                permute_scales(1)
+            permute_group(f)
+            first_product(f, (0, 1))
+            first_product(f, (2, 3))
+        for f, planes in ((1, 4), (2, 2), (3, 2)):
+            for t in range(planes):
+                scatter_z("scalar", f, t)
+        scatter_z("vector", 2, 2)
         make_mask(1)
-        for f, pair in ((2, (0, 3)), (2, (1, 2)), (3, (0, 1)), (3, (3,)), (3, (2,))):
-            first_product(f, pair)
-        for c in range(3):
-            scatter_z("scalar", 2, c)
-        for c in range(2):
-            scatter_z("scalar", 3, c)
+        scatter_z("vector", 2, 3, "a1")
         make_mask(2)
-        scatter_z("vector", 2, 3, "a2")
+        quantise_and_multiply(0, "z2_2")
+        scatter_z("vector", 3, 2, "da0")
         make_mask(3)
+        apply_mask(1, range(PACK))
         scatter_z("vector", 3, 3, "a3")
-        quantise_and_multiply(0, "z3_3")
-        scatter_z("vector", 3, 2, "planes0")
-        for f in range(G - 1):
-            scalar_dx(f)
-            vector_dx(f, 0, 1)
-            quantise_and_multiply(f + 1, "planes%d" % f if f else None)
-            vector_dx(f, 1, 2, "planes%d" % (f + 1))
+        quantise_and_multiply(1, "z3_2")
+        scalar_dx(0)
+        vector_dx(2, 0, 1, "da1")
+        apply_mask(2, (2, 0, 3, 1))
+        quantise_and_multiply(2, "da1")
+        scalar_dx(1)
+        vector_dx(0, 0, 2, "da2")
+        apply_mask(3, (2, 0, 1, 3))
+        quantise_and_multiply(3, "da2")
+        vector_dx(2, 1, 2, "da3")
+        scalar_dx(2)
+        vector_dx(0, 2, 4)
         scalar_dx(3)
-        vector_dx(3, 0, 2)
+        vector_dx(2, 2, 4)

@@ -32,24 +32,31 @@ def tile_moe_hib_relu_kernel(
     nc = tc.nc
 
     with ExitStack() as ctx:
+        lists = ctx.enter_context(tc.tile_pool(name="lists", bufs=1))
         keep = ctx.enter_context(tc.tile_pool(name="keep", bufs=1))
+        placed = ctx.enter_context(tc.tile_pool(name="placed", bufs=1))
         psum = ctx.enter_context(tc.psum_pool(name="psum", bufs=2))
 
-        def slot(name, shape, dtype, tag=None):
-            return keep.tile(shape, dtype, name=name, tag=tag or name, align_bytes=64)
+        def slot(name, shape, dtype, over=None):
+            return keep.tile(shape, dtype, name=name, tag=over or name, align_bytes=64)
 
-        dst_l = keep.tile([P, T // PER_COL], U16, name="dst_l")
-        offs2_l = keep.tile([P, T // PER_COL], U16, name="offs2_l")
-        offs_l = keep.tile([P, T // PER_COL], U16, name="offs_l")
+        dst_l = lists.tile([P, T // PER_COL], U16, name="dst_l")
+        offs2_l = lists.tile([P, T // PER_COL], U16, name="offs2_l")
+        offs_l = lists.tile([P, T // PER_COL], U16, name="offs_l")
         dy_w = slot("dy_w", [P, T], U32)
         dy_s = slot("dy_s", [P, T], U8)
-        wet_w, wet_pair = {}, {}
         wet_s = [slot("wet_s%d" % h, [P, H], U8) for h in range(E // SHARE)]
         wet_sp = [slot("wet_sp%d" % h, [P, H], U8) for h in range(E // SHARE)]
         wgt_s = slot("wgt_s", [P, K], U8)
-        a_sb = {}
         gate_first = slot("gate_first", [P, C1], F32)
         gate_rest = slot("gate_rest", [P, T - C1], F32)
+        a_part = {
+            (0, 1): slot("a0", [P, PACK, C1], F32),
+            (1, 2): placed.tile([P, PACK, C1], F32, name="a1", offset=2 * T, align_bytes=64),
+            (2, 4): slot("a2", [P, PACK, 2 * C1], F32),
+        }
+        wet_w = [slot("wet_w%d" % f, [P, EPG, H], U32) for f in range(G)]
+        wgt_w = [slot("wgt_w%d" % h, [P, 2, K], U32) for h in range(2)]
 
         def load_scales(tile, rows):
             matrices = rows.shape[0]
@@ -63,58 +70,45 @@ def tile_moe_hib_relu_kernel(
         nc.gpsimd.memset(wgt_s[:].bitcast(I32), 0)
 
         wet_words_p = wet_words.rearrange("e s p i d -> p (e s) (i d)")
+        wgt_words_p = wgt_words.rearrange("f s p k d -> p (f s) (k d)")
         wet_rows = wet_scales.rearrange("e s b i -> (e s) b i")
 
-        def load_wet(e0, e1):
-            tile = slot("wet_w%d" % e0, [P, e1 - e0, H], U32)
-            nc.sync.dma_start(tile[:].bitcast(I32), wet_words_p[:, e0:e1, :].bitcast(I32))
-            wet_pair[e0 // EPG] = tile
-            for e in range(e0, e1):
-                wet_w[e] = tile[:, e - e0, :]
+        def load_wet(f):
+            nc.sync.dma_start(wet_w[f][:].bitcast(I32), wet_words_p[:, EPG * f : EPG * (f + 1), :].bitcast(I32))
 
-        wgt_words_p = wgt_words.rearrange("f s p k d -> p (f s) (k d)")
-        wgt_w = {}
+        def load_wgt(h):
+            nc.sync.dma_start(wgt_w[h][:].bitcast(I32), wgt_words_p[:, 2 * h : 2 * (h + 1), :].bitcast(I32))
 
-        def load_wgt(f0, f1):
-            tile = slot("wgt_w%d" % f0, [P, f1 - f0, K], U32)
-            nc.sync.dma_start(tile[:].bitcast(I32), wgt_words_p[:, f0:f1, :].bitcast(I32))
-            for f in range(f0, f1):
-                wgt_w[f] = tile[:, f - f0, :]
-
-        def load_a(f0, f1, tag=None):
-            tile = slot("a%d" % f0, [P, PACK, (f1 - f0) * C1], F32, tag)
-            nc.sync.dma_start(tile[:], a[:, C1 * f0 : C1 * f1].rearrange("(p t) j -> p t j", t=PACK))
-            for f in range(f0, f1):
-                a_sb[f] = tile[:, :, C1 * (f - f0) : C1 * (f - f0 + 1)]
+        def load_a(f0, f1):
+            nc.sync.dma_start(a_part[f0, f1][:], a[:, C1 * f0 : C1 * f1].rearrange("(p t) j -> p t j", t=PACK))
 
         nc.sync.dma_start(dst_l[:], dst)
         load_scales(dy_s, dy_scales.to_broadcast([QUAD // ROWS, QUADS * ROWS, T]))
         nc.sync.dma_start(offs2_l[:], offs2)
         nc.sync.dma_start(dy_w[:].bitcast(I32), dy_words.rearrange("s p t d -> p (s t d)").bitcast(I32))
-        load_wet(0, 2)
+        load_wet(0)
         load_scales(wet_s[0], wet_rows)
         nc.sync.dma_start(gate_first[:], gate[:, 0:C1])
-        load_wet(2, 4)
+        load_wet(1)
         nc.sync.dma_start(gate_rest[:], gate[:, C1:T])
         load_a(0, 1)
-        load_wet(4, 6)
+        load_wet(2)
         load_scales(wet_s[1], wet_rows[SHARE:E])
-        load_wet(6, 8)
+        load_wet(3)
         load_a(1, 2)
-        load_a(2, 3)
-        load_a(3, 4)
+        load_a(2, 4)
         load_scales(wgt_s, wgt_scales.rearrange("f s b k -> (f s) b k"))
-        load_wgt(0, 2)
+        load_wgt(0)
         nc.sync.dma_start(offs_l[:], offs)
-        load_wgt(2, 4)
+        load_wgt(1)
 
         def cols(lo, hi):
             return slice(lo // PER_COL, hi // PER_COL)
 
         gq_w, gq_s = {}, {}
 
-        def gather(views, src, dtype, lo, hi, name, tag=None):
-            tile = slot(name, [P, hi - lo], dtype, tag)
+        def gather(views, src, dtype, lo, hi, name, over=None):
+            tile = slot(name, [P, hi - lo], dtype, over)
             nc.vector.tensor_copy(tile[:], src[:].indirect(dst_l[:, cols(lo, hi)]))
             for m in range(lo, hi, C2):
                 views[m // C2] = tile[:, m - lo : m - lo + C2]
@@ -124,84 +118,102 @@ def tile_moe_hib_relu_kernel(
         def by_planes(ap):
             return ap.rearrange("p (t m) -> p m t", t=PACK)
 
-        def permute_first(e):
+        def as_loaded(ap):
+            return ap.rearrange("p (m t) -> p m t", t=PACK)
+
+        def permute_words(copy, e):
             wet_p[e] = slot("wet_p%d" % e, [P, H], U32)
-            nc.scalar.copy(by_planes(wet_p[e][:]), wet_w[e].rearrange("p (m t) -> p m t", t=PACK))
+            copy(by_planes(wet_p[e][:]), as_loaded(wet_w[e // EPG][:, e % EPG, :]))
 
         def permute_group(f):
             tile = slot("wet_p%d" % (EPG * f), [P, EPG, H], U32)
-            nc.vector.tensor_copy(
-                tile[:].rearrange("p e (t m) -> p e m t", t=PACK),
-                wet_pair[f][:].rearrange("p e (m t) -> p e m t", t=PACK),
+            nc.gpsimd.tensor_copy(
+                tile[:].rearrange("p e (t m) -> p e t m", t=PACK),
+                wet_w[f][:].rearrange("p e (m t) -> p e t m", t=PACK),
             )
             for u in range(EPG):
                 wet_p[EPG * f + u] = tile[:, u, :]
 
         def permute_scales(h):
-            nc.vector.tensor_copy(by_planes(wet_sp[h][:]), wet_s[h][:].rearrange("p (m t) -> p m t", t=PACK))
+            nc.vector.tensor_copy(by_planes(wet_sp[h][:]), as_loaded(wet_s[h][:]))
 
         staged = {}
 
-        def first_product(f, pair):
-            z_ps = psum.tile([P, len(pair), C1], F32, name="z_ps", tag="z", bufs=3)
-            for u, c in enumerate(pair):
-                cs = slice(P * c, P * (c + 1))
-                for e in range(EPG * f, EPG * (f + 1)):
-                    nc.tensor.matmul_mx(
-                        out=z_ps[:, u, C2 * (e % EPG) : C2 * (e % EPG + 1)],
-                        lhsT=wet_p[e][:, cs].bitcast(FP8X4),
-                        lhsT_scale=wet_sp[e // SHARE][ROWS * (e % SHARE) : P, cs],
-                        rhs=gq_w[e].bitcast(FP8X4),
-                        rhs_scale=gq_s[e],
-                        start=True,
-                        stop=True,
-                    )
-            z = slot("z%d_%d" % (f, pair[0]), [P, len(pair), C1], F32)
+        def first_product(f, cuts, over=None):
+            whole = slot("z%d" % f, [P, PACK, C1], F32, over) if over else None
             weights = gate_rest[:, C1 * (f - 1) : C1 * f] if f else gate_first[:]
-            nc.vector.tensor_tensor(z[:], z_ps[:], weights.unsqueeze(1).to_broadcast([P, len(pair), C1]), ALU.mult)
-            for u, c in enumerate(pair):
-                staged[f, c] = z[:, u, :]
+            for lo, hi in cuts:
+                z_ps = psum.tile([P, hi - lo, C1], F32, name="z_ps", tag="z", bufs=4)
+                for t in range(lo, hi):
+                    cs = slice(P * t, P * (t + 1))
+                    for e in range(EPG * f, EPG * (f + 1)):
+                        nc.tensor.matmul_mx(
+                            out=z_ps[:, t - lo, C2 * (e % EPG) : C2 * (e % EPG + 1)],
+                            lhsT=wet_p[e][:, cs].bitcast(FP8X4),
+                            lhsT_scale=wet_sp[e // SHARE][ROWS * (e % SHARE) : P, cs],
+                            rhs=gq_w[e].bitcast(FP8X4),
+                            rhs_scale=gq_s[e],
+                            start=True,
+                            stop=True,
+                        )
+                z = whole[:, lo:hi, :] if over else slot("z%d_%d" % (f, lo), [P, hi - lo, C1], F32)[:]
+                nc.vector.tensor_tensor(z, z_ps[:], weights.unsqueeze(1).to_broadcast([P, hi - lo, C1]), ALU.mult)
+                for t in range(lo, hi):
+                    staged[f, t] = z[:, t - lo, :]
 
-        def scatter(engine, win, offsets, values):
-            if engine == "vector":
-                nc.vector.tensor_copy(win[:].indirect(offsets), values)
-            else:
-                nc.scalar.activation(win[:].indirect(offsets), values, ACT.Copy)
+        def on_vector(win, offsets, values):
+            nc.vector.tensor_copy(win[:].indirect(offsets), values)
 
-        mask, planar = {}, {}
+        def on_scalar(win, offsets, values):
+            nc.scalar.activation(win[:].indirect(offsets), values, ACT.Copy)
 
-        def make_mask(f):
-            mask[f] = slot("mask%d" % f, [P, PACK, C1], BF16)
-            nc.vector.tensor_scalar(mask[f][:], a_sb[f], 0.0, None, ALU.is_gt)
+        mask = {}
+
+        def make_masks(f0, f1):
+            tile = slot("mask%d" % f0, [P, PACK, (f1 - f0) * C1], BF16)
+            nc.vector.tensor_scalar(tile[:], a_part[f0, f1][:], 0.0, None, ALU.is_gt)
+            for f in range(f0, f1):
+                mask[f] = tile[:, :, C1 * (f - f0) : C1 * (f - f0 + 1)]
 
         zwin = {}
 
-        def scatter_z(engine, f, t, tag=None):
-            zwin[f, t] = slot("zwin%d_%d" % (f, t), [P, T], F32, tag)
-            scatter(engine, zwin[f, t], offs2_l[:, cols(C1 * f, C1 * (f + 1))], staged[f, t])
+        def scatter_z(scatter, f, t, over=None, offset=None):
+            name = "zwin%d_%d" % (f, t)
+            if offset is None:
+                zwin[f, t] = slot(name, [P, T], F32, over)
+            else:
+                zwin[f, t] = placed.tile([P, T], F32, name=name, offset=offset, align_bytes=64)
+            scatter(zwin[f, t], offs2_l[:, cols(C1 * f, C1 * (f + 1))], staged[f, t])
 
-        def apply_mask(f, planes):
-            planar[f] = slot("planar%d" % f, [P, PACK, C1], BF16, "planar")
+        da = {}
+
+        def mask_and_interleave(f, planes):
+            planar = slot("planar%d" % f, [P, PACK, C1], BF16)
             for t in planes:
-                nc.gpsimd.tensor_tensor(planar[f][:, t, :], zwin[f, t][:, C1 * f : C1 * (f + 1)], mask[f][:, t, :], ALU.mult)
+                nc.gpsimd.tensor_tensor(
+                    planar[:, t, :],
+                    zwin[f, t][:, C1 * f : C1 * (f + 1)],
+                    mask[f][:, t, :],
+                    ALU.mult,
+                )
+            da[f] = slot("da%d" % f, [P, C1, PACK], BF16)
+            nc.gpsimd.tensor_scalar(da[f][:], planar[:].rearrange("p t j -> p j t"), 1.0, 0.0, ALU.mult, ALU.add)
 
         dx_ps = {}
 
-        def quantise_and_multiply(f, tag=None):
-            da = slot("da%d" % f, [P, C1, PACK], BF16)
-            nc.gpsimd.tensor_scalar(da[:], planar[f][:].rearrange("p t j -> p j t"), 1.0, 0.0, ALU.mult, ALU.add)
-            da_w = slot("da_w%d" % f, [P, C1], U32, tag)
+        def quantise_and_multiply(f, blocks):
+            da_w = slot("da_w%d" % f, [P, C1], U32)
             da_s = slot("da_s%d" % f, [P, C1], U8)
-            nc.vector.quantize_mx(out=da_w[:].bitcast(FP8X4), scales=da_s[:], in_=da[:].rearrange("p j t -> p (j t)"))
+            nc.vector.quantize_mx(out=da_w[:].bitcast(FP8X4), scales=da_s[:], in_=da[f][:].rearrange("p j t -> p (j t)"))
             if f % 2 == 0:
-                for c in (2, 0) if f == 0 else (0, 2):
-                    dx_ps[f // 2, c] = psum.tile([P, 2, C1], F32, name="dx_ps", tag="dx_vector", bufs=3)
-            dx_ps[f, "scalar"] = psum.tile([P, 2, C1], F32, name="dx_ps", tag="dx_scalar")
-            for c in ((1, 3, 2, 0), (1, 3, 0, 2), (1, 3, 0, 2), (0, 1, 3, 2))[f]:
+                for c in (0, 2):
+                    dx_ps[c, f // 2] = psum.tile([P, 2, C1], F32, name="dx_ps", tag="dx_vector")
+            dx_ps["scalar", f] = psum.tile([P, 2, C1], F32, name="dx_ps", tag="dx_scalar")
+            for c in blocks:
                 ks = slice(P * c, P * (c + 1))
                 nc.tensor.matmul_mx(
-                    out=dx_ps[f, "scalar"][:, c // 2, :] if c % 2 else dx_ps[f // 2, c][:, f % 2, :],
-                    lhsT=wgt_w[f][:, ks].bitcast(FP8X4),
+                    out=dx_ps["scalar", f][:, c // 2, :] if c % 2 else dx_ps[c, f // 2][:, f % 2, :],
+                    lhsT=wgt_w[f // 2][:, f % 2, ks].bitcast(FP8X4),
                     lhsT_scale=wgt_s[ROWS * f : P, ks],
                     rhs=da_w[:].bitcast(FP8X4),
                     rhs_scale=da_s[:],
@@ -209,69 +221,85 @@ def tile_moe_hib_relu_kernel(
                     stop=True,
                 )
 
+        dx = {}
+
+        def copy_dx(copy, who, n):
+            dx[who, n] = slot("dx_%s_%d" % (who, n), [P, 2, C1], F32)
+            copy(dx[who, n][:], dx_ps[who, n][:])
+
         owin = {}
 
-        def scatter_dx(engine, f0, f1, c, values):
-            if f0 == 0:
-                owin[c] = slot("owin%d" % c, [P, T], F32, "zwin0_%d" % c)
-            scatter(engine, owin[c], offs_l[:, cols(C1 * f0, C1 * f1)], values)
-            if f1 == G:
-                nc.sync.dma_start(out[P * c : P * (c + 1), :], owin[c][:])
+        def scatter_dx(scatter, c, lo, hi, values, over=None, queue=nc.sync):
+            if lo == 0:
+                owin[c] = slot("owin%d" % c, [P, T], F32, over)
+            scatter(owin[c], offs_l[:, cols(lo, hi)], values)
+            if hi == T:
+                queue.dma_start(out[P * c : P * (c + 1), :], owin[c][:])
 
-        def scalar_dx(f):
-            dx = slot("dx%d_scalar" % f, [P, 2, C1], F32)
-            nc.scalar.copy(dx[:], dx_ps[f, "scalar"][:])
-            for u, c in enumerate((1, 3)):
-                scatter_dx("scalar", f, f + 1, c, dx[:, u, :])
+        def scalar_dx(c, f, over=None, queue=nc.sync):
+            scatter_dx(on_scalar, c, C1 * f, C1 * (f + 1), dx["scalar", f][:, c // 2, :], over, queue)
 
-        def vector_dx(c, f0, f1, tag=None):
-            dx = slot("dx%d_vector%d" % (f0, c), [P, f1 - f0, C1], F32, tag)
-            nc.vector.tensor_copy(dx[:], dx_ps[f0 // 2, c][:, f0 % 2 : (f1 - 1) % 2 + 1, :])
-            scatter_dx("vector", f0, f1, c, dx[:].rearrange("p f j -> p (f j)"))
+        def vector_dx(c, h, over=None):
+            scatter_dx(on_vector, c, 2 * C1 * h, 2 * C1 * (h + 1), dx[c, h][:].rearrange("p f j -> p (f j)"), over)
 
+        halves = ((0, 2), (2, 4))
         gather(gq_s, dy_s, U8, 0, 4 * C2, "gq_s0")
         gather(gq_w, dy_w, U32, 0, 2 * C2, "gq_w0")
         gather(gq_w, dy_w, U32, 2 * C2, 5 * C2, "gq_w1")
-        permute_first(0)
-        permute_first(1)
+        for e in range(EPG):
+            permute_words(nc.scalar.copy, e)
         permute_scales(0)
         gather(gq_w, dy_w, U32, 5 * C2, T, "gq_w2", "wet_s0")
-        for pair in ((0,), (1, 2), (3,)):
-            first_product(0, pair)
+        first_product(0, ((0, 1), (1, 3), (3, 4)))
         for t in range(PACK):
-            scatter_z("scalar", 0, t)
+            scatter_z(on_scalar, 0, t)
         gather(gq_s, dy_s, U8, 4 * C2, T, "gq_s1", "gate_first")
         for f in range(1, G):
-            if f == 2:
-                make_mask(0)
-                apply_mask(0, range(PACK))
-                permute_scales(1)
             permute_group(f)
-            first_product(f, (0, 1))
-            first_product(f, (2, 3))
-        for f, planes in ((1, 4), (2, 2), (3, 2)):
-            for t in range(planes):
-                scatter_z("scalar", f, t)
-        scatter_z("vector", 2, 2)
-        make_mask(1)
-        scatter_z("vector", 2, 3, "a1")
-        make_mask(2)
-        quantise_and_multiply(0, "z2_2")
-        scatter_z("vector", 3, 2, "da0")
-        make_mask(3)
-        apply_mask(1, range(PACK))
-        scatter_z("vector", 3, 3, "a3")
-        quantise_and_multiply(1, "z3_2")
-        scalar_dx(0)
-        vector_dx(2, 0, 1, "da1")
-        apply_mask(2, (2, 0, 3, 1))
-        quantise_and_multiply(2, "da1")
-        scalar_dx(1)
-        vector_dx(0, 0, 2, "da2")
-        apply_mask(3, (2, 0, 1, 3))
-        quantise_and_multiply(3, "da2")
-        vector_dx(2, 1, 2, "da3")
-        scalar_dx(2)
-        vector_dx(0, 2, 4)
-        scalar_dx(3)
-        vector_dx(2, 2, 4)
+        make_masks(0, 1)
+        first_product(1, halves)
+        permute_scales(1)
+        first_product(2, halves)
+        make_masks(1, 2)
+        mask_and_interleave(0, range(PACK))
+        scatter_z(on_scalar, 1, 0)
+        scatter_z(on_scalar, 1, 1)
+        scatter_z(on_vector, 1, 2, offset=0)
+        scatter_z(on_vector, 1, 3, offset=4 * T)
+        mask_and_interleave(1, (2, 0, 3, 1))
+        first_product(3, halves, "z1_2")
+        make_masks(2, 4)
+        scatter_z(on_scalar, 2, 0)
+        scatter_z(on_scalar, 2, 1)
+        quantise_and_multiply(0, (1, 3, 0, 2))
+        scatter_z(on_vector, 2, 2, "planar0")
+        scatter_z(on_vector, 2, 3, "a2")
+        mask_and_interleave(2, (0, 2, 1, 3))
+        scatter_z(on_scalar, 3, 0)
+        scatter_z(on_scalar, 3, 2)
+        copy_dx(nc.scalar.copy, "scalar", 0)
+        scatter_z(on_scalar, 3, 1, "da_w0")
+        quantise_and_multiply(1, (0, 2, 1, 3))
+        scatter_z(on_vector, 3, 3, "planar1")
+        copy_dx(nc.vector.tensor_copy, 0, 0)
+        copy_dx(nc.vector.tensor_copy, 2, 0)
+        mask_and_interleave(3, (0, 2, 3, 1))
+        scalar_dx(3, 0, "da1")
+        copy_dx(nc.scalar.copy, "scalar", 1)
+        scalar_dx(1, 0, "da_s1")
+        scalar_dx(3, 1)
+        scalar_dx(1, 1)
+        quantise_and_multiply(2, (1, 3, 0, 2))
+        vector_dx(0, 0, "planar2")
+        copy_dx(nc.scalar.copy, "scalar", 2)
+        scalar_dx(1, 2)
+        scalar_dx(3, 2)
+        quantise_and_multiply(3, (0, 2, 1, 3))
+        vector_dx(2, 0, "planar3")
+        copy_dx(nc.vector.tensor_copy, 0, 1)
+        copy_dx(nc.vector.tensor_copy, 2, 1)
+        copy_dx(nc.scalar.copy, "scalar", 3)
+        scalar_dx(1, 3, queue=nc.scalar)
+        vector_dx(0, 1)
+        scalar_dx(3, 3, queue=nc.scalar)
+        vector_dx(2, 1)

@@ -127,9 +127,9 @@ def tile_moe_hib_relu_kernel(
 
         def permute_group(f):
             tile = slot("wet_p%d" % (EPG * f), [P, EPG, H], U32)
-            nc.gpsimd.tensor_copy(
-                tile[:].rearrange("p e (t m) -> p e t m", t=PACK),
-                wet_w[f][:].rearrange("p e (m t) -> p e t m", t=PACK),
+            nc.vector.tensor_copy(
+                tile[:].rearrange("p e (t m) -> p e m t", t=PACK),
+                wet_w[f][:].rearrange("p e (m t) -> p e m t", t=PACK),
             )
             for u in range(EPG):
                 wet_p[EPG * f + u] = tile[:, u, :]
@@ -201,9 +201,9 @@ def tile_moe_hib_relu_kernel(
 
         dx_ps = {}
 
-        def quantise_and_multiply(f, blocks):
+        def quantise_and_multiply(f, blocks, over=None):
             da_w = slot("da_w%d" % f, [P, C1], U32)
-            da_s = slot("da_s%d" % f, [P, C1], U8)
+            da_s = slot("da_s%d" % f, [P, C1], U8, over)
             nc.vector.quantize_mx(out=da_w[:].bitcast(FP8X4), scales=da_s[:], in_=da[f][:].rearrange("p j t -> p (j t)"))
             if f % 2 == 0:
                 for c in (0, 2):
@@ -253,13 +253,14 @@ def tile_moe_hib_relu_kernel(
         first_product(0, ((0, 1), (1, 3), (3, 4)))
         for t in range(PACK):
             scatter_z(on_scalar, 0, t)
+        permute_group(1)
         gather(gq_s, dy_s, U8, 4 * C2, T, "gq_s1", "gate_first")
-        for f in range(1, G):
-            permute_group(f)
-        make_masks(0, 1)
         first_product(1, halves)
         permute_scales(1)
+        permute_group(2)
+        make_masks(0, 1)
         first_product(2, halves)
+        permute_group(3)
         make_masks(1, 2)
         mask_and_interleave(0, range(PACK))
         scatter_z(on_scalar, 1, 0)
@@ -271,21 +272,21 @@ def tile_moe_hib_relu_kernel(
         make_masks(2, 4)
         scatter_z(on_scalar, 2, 0)
         scatter_z(on_scalar, 2, 1)
-        quantise_and_multiply(0, (1, 3, 0, 2))
-        scatter_z(on_vector, 2, 2, "planar0")
+        quantise_and_multiply(0, (1, 3, 0, 2), "gate_rest")
+        scatter_z(on_vector, 2, 2, "da0")
         scatter_z(on_vector, 2, 3, "a2")
         mask_and_interleave(2, (0, 2, 1, 3))
         scatter_z(on_scalar, 3, 0)
-        scatter_z(on_scalar, 3, 2)
+        scatter_z(on_scalar, 3, 1)
         copy_dx(nc.scalar.copy, "scalar", 0)
-        scatter_z(on_scalar, 3, 1, "da_w0")
+        scatter_z(on_scalar, 3, 2, "da_w0")
         quantise_and_multiply(1, (0, 2, 1, 3))
         scatter_z(on_vector, 3, 3, "planar1")
-        copy_dx(nc.vector.tensor_copy, 0, 0)
-        copy_dx(nc.vector.tensor_copy, 2, 0)
-        mask_and_interleave(3, (0, 2, 3, 1))
-        scalar_dx(3, 0, "da1")
+        mask_and_interleave(3, range(PACK))
+        copy_dx(nc.scalar.copy, 0, 0)
+        copy_dx(nc.scalar.copy, 2, 0)
         copy_dx(nc.scalar.copy, "scalar", 1)
+        scalar_dx(3, 0, "da_w1")
         scalar_dx(1, 0, "da_s1")
         scalar_dx(3, 1)
         scalar_dx(1, 1)

@@ -202,8 +202,8 @@ def tile_moe_hib_relu_kernel(
         dx_ps = {}
 
         def quantise_and_multiply(f, blocks, over=None):
-            da_w = slot("da_w%d" % f, [P, C1], U32)
-            da_s = slot("da_s%d" % f, [P, C1], U8, over)
+            da_w = slot("da_w%d" % f, [P, C1], U32, over)
+            da_s = slot("da_s%d" % f, [P, C1], U8)
             nc.vector.quantize_mx(out=da_w[:].bitcast(FP8X4), scales=da_s[:], in_=da[f][:].rearrange("p j t -> p (j t)"))
             if f % 2 == 0:
                 for c in (0, 2):
@@ -226,6 +226,11 @@ def tile_moe_hib_relu_kernel(
         def copy_dx(copy, who, n):
             dx[who, n] = slot("dx_%s_%d" % (who, n), [P, 2, C1], F32)
             copy(dx[who, n][:], dx_ps[who, n][:])
+
+        def vector_piece(c, f):
+            piece = slot("dx_piece%d" % f, [P, C1], F32)
+            nc.vector.tensor_copy(piece[:], dx_ps[c, f // 2][:, f % 2, :])
+            return piece
 
         owin = {}
 
@@ -270,37 +275,37 @@ def tile_moe_hib_relu_kernel(
         mask_and_interleave(1, (2, 0, 3, 1))
         first_product(3, halves, "z1_2")
         make_masks(2, 4)
-        scatter_z(on_scalar, 2, 0)
-        scatter_z(on_scalar, 2, 1)
+        for t in (0, 1, 3):
+            scatter_z(on_scalar, 2, t)
         quantise_and_multiply(0, (1, 3, 0, 2), "gate_rest")
-        scatter_z(on_vector, 2, 2, "da0")
-        scatter_z(on_vector, 2, 3, "a2")
-        mask_and_interleave(2, (0, 2, 1, 3))
+        scatter_z(on_vector, 2, 2, "a2")
+        mask_and_interleave(2, (0, 1, 3, 2))
         scatter_z(on_scalar, 3, 0)
-        scatter_z(on_scalar, 3, 1)
         copy_dx(nc.scalar.copy, "scalar", 0)
-        scatter_z(on_scalar, 3, 2, "da_w0")
-        quantise_and_multiply(1, (0, 2, 1, 3))
-        scatter_z(on_vector, 3, 3, "planar1")
-        mask_and_interleave(3, range(PACK))
+        scatter_z(on_scalar, 3, 1, "da_s0")
+        quantise_and_multiply(1, (0, 2, 1, 3), "z2_2")
+        scatter_z(on_vector, 3, 2, "da1")
+        scatter_z(on_vector, 3, 3, "a2")
+        mask_and_interleave(3, (0, 2, 1, 3))
         copy_dx(nc.scalar.copy, 0, 0)
         copy_dx(nc.scalar.copy, 2, 0)
         copy_dx(nc.scalar.copy, "scalar", 1)
-        scalar_dx(3, 0, "da_w1")
+        scalar_dx(3, 0, "z2_2")
         scalar_dx(1, 0, "da_s1")
         scalar_dx(3, 1)
         scalar_dx(1, 1)
-        quantise_and_multiply(2, (1, 3, 0, 2))
+        quantise_and_multiply(2, (0, 1, 3, 2))
         vector_dx(0, 0, "planar2")
+        scatter_dx(on_vector, 0, 2 * C1, 3 * C1, vector_piece(0, 2)[:])
         copy_dx(nc.scalar.copy, "scalar", 2)
         scalar_dx(1, 2)
         scalar_dx(3, 2)
         quantise_and_multiply(3, (0, 2, 1, 3))
         vector_dx(2, 0, "planar3")
-        copy_dx(nc.vector.tensor_copy, 0, 1)
+        last = vector_piece(0, 3)
         copy_dx(nc.vector.tensor_copy, 2, 1)
         copy_dx(nc.scalar.copy, "scalar", 3)
         scalar_dx(1, 3, queue=nc.scalar)
-        vector_dx(0, 1)
+        scatter_dx(on_vector, 0, 3 * C1, T, last[:])
         scalar_dx(3, 3, queue=nc.scalar)
         vector_dx(2, 1)

@@ -169,8 +169,8 @@ def tile_moe_hib_relu_kernel(
 
         mask = {}
 
-        def make_masks(f0, f1):
-            tile = slot("mask%d" % f0, [P, PACK, (f1 - f0) * C1], BF16)
+        def make_masks(f0, f1, over=None):
+            tile = slot("mask%d" % f0, [P, PACK, (f1 - f0) * C1], BF16, over)
             nc.vector.tensor_scalar(tile[:], a_part[f0, f1][:], 0.0, None, ALU.is_gt)
             for f in range(f0, f1):
                 mask[f] = tile[:, :, C1 * (f - f0) : C1 * (f - f0 + 1)]
@@ -227,8 +227,8 @@ def tile_moe_hib_relu_kernel(
             dx[who, n] = slot("dx_%s_%d" % (who, n), [P, 2, C1], F32)
             copy(dx[who, n][:], dx_ps[who, n][:])
 
-        def vector_piece(c, f):
-            piece = slot("dx_piece%d" % f, [P, C1], F32)
+        def vector_piece(c, f, over=None):
+            piece = slot("dx_piece%d" % f, [P, C1], F32, over)
             nc.vector.tensor_copy(piece[:], dx_ps[c, f // 2][:, f % 2, :])
             return piece
 
@@ -263,9 +263,9 @@ def tile_moe_hib_relu_kernel(
         first_product(1, halves)
         permute_scales(1)
         permute_group(2)
-        make_masks(0, 1)
-        first_product(2, halves)
         permute_group(3)
+        make_masks(0, 1, "wet_w3")
+        first_product(2, halves, "a0")
         make_masks(1, 2)
         mask_and_interleave(0, range(PACK))
         scatter_z(on_scalar, 1, 0)
@@ -283,25 +283,26 @@ def tile_moe_hib_relu_kernel(
         scatter_z(on_scalar, 3, 0)
         copy_dx(nc.scalar.copy, "scalar", 0)
         scatter_z(on_scalar, 3, 1, "da_s0")
-        quantise_and_multiply(1, (0, 2, 1, 3), "z2_2")
+        quantise_and_multiply(1, (0, 2, 1, 3), "a0")
         scatter_z(on_vector, 3, 2, "da1")
         scatter_z(on_vector, 3, 3, "a2")
         mask_and_interleave(3, (0, 2, 1, 3))
-        copy_dx(nc.scalar.copy, 0, 0)
-        copy_dx(nc.scalar.copy, 2, 0)
+        copy_dx(nc.vector.tensor_copy, 0, 0)
+        scalar_dx(3, 0, "a0")
         copy_dx(nc.scalar.copy, "scalar", 1)
-        scalar_dx(3, 0, "z2_2")
+        copy_dx(nc.scalar.copy, 2, 0)
         scalar_dx(1, 0, "da_s1")
         scalar_dx(3, 1)
         scalar_dx(1, 1)
+        vector_dx(0, 0)
         quantise_and_multiply(2, (0, 1, 3, 2))
-        vector_dx(0, 0, "planar2")
-        scatter_dx(on_vector, 0, 2 * C1, 3 * C1, vector_piece(0, 2)[:])
+        vector_dx(2, 0, "planar2")
         copy_dx(nc.scalar.copy, "scalar", 2)
         scalar_dx(1, 2)
         scalar_dx(3, 2)
+        cover = vector_piece(0, 2, "planar3")
         quantise_and_multiply(3, (0, 2, 1, 3))
-        vector_dx(2, 0, "planar3")
+        scatter_dx(on_vector, 0, 2 * C1, 3 * C1, cover[:])
         last = vector_piece(0, 3)
         copy_dx(nc.vector.tensor_copy, 2, 1)
         copy_dx(nc.scalar.copy, "scalar", 3)

@@ -295,7 +295,7 @@ def tile_moe_hib_relu_kernel(
         scalar_dx(3, 1)
         scalar_dx(1, 1)
         vector_dx(0, 0)
-        quantise_and_multiply(2, (0, 1, 3, 2))
+        quantise_and_multiply(2, (0, 1, 3, 2), "dx_0_0")
         vector_dx(2, 0, "planar2")
         copy_dx(nc.scalar.copy, "scalar", 2)
         scalar_dx(1, 2)

@@ -296,7 +296,7 @@ def tile_moe_hib_relu_kernel(
         scalar_dx(1, 1)
         vector_dx(0, 0)
         quantise_and_multiply(2, (0, 1, 3, 2), "dx_0_0")
-        vector_dx(2, 0, "planar2")
+        vector_dx(2, 0, "da2")
         copy_dx(nc.scalar.copy, "scalar", 2)
         scalar_dx(1, 2)
         scalar_dx(3, 2)

@@ -24,6 +24,20 @@ QUAD = 32
 QUADS = P // QUAD
 ROWS = 4
 SHARE = 4
+WINDOW = 4 * T
+PLACES = {
+    "z2": 0,
+    "a0": WINDOW // 2,
+    "zwin1_2": WINDOW,
+    "zwin1_3": 2 * WINDOW,
+    "owin2": 3 * WINDOW,
+    "planar2": 3 * WINDOW,
+    "dx_0_0": 3 * WINDOW + 3 * WINDOW // 4,
+    "da_w2": 4 * WINDOW,
+    "dx_piece1_3": 5 * WINDOW,
+    "dx_piece1_2": 5 * WINDOW + WINDOW // 8,
+    "dx_piece3_3": 5 * WINDOW + WINDOW // 4,
+}
 
 
 def tile_moe_hib_relu_kernel(
@@ -38,6 +52,8 @@ def tile_moe_hib_relu_kernel(
         psum = ctx.enter_context(tc.psum_pool(name="psum", bufs=2))
 
         def slot(name, shape, dtype, over=None):
+            if name in PLACES:
+                return placed.tile(shape, dtype, name=name, offset=PLACES[name], align_bytes=64)
             return keep.tile(shape, dtype, name=name, tag=over or name, align_bytes=64)
 
         dst_l = lists.tile([P, T // PER_COL], U16, name="dst_l")
@@ -51,8 +67,7 @@ def tile_moe_hib_relu_kernel(
         gate_first = slot("gate_first", [P, C1], F32)
         gate_rest = slot("gate_rest", [P, T - C1], F32)
         a_part = {
-            (0, 1): slot("a0", [P, PACK, C1], F32),
-            (1, 2): placed.tile([P, PACK, C1], F32, name="a1", offset=2 * T, align_bytes=64),
+            (0, 2): slot("a0", [P, PACK, 2 * C1], F32),
             (2, 4): slot("a2", [P, PACK, 2 * C1], F32),
         }
         wet_w = [slot("wet_w%d" % f, [P, EPG, H], U32) for f in range(G)]
@@ -91,11 +106,10 @@ def tile_moe_hib_relu_kernel(
         nc.sync.dma_start(gate_first[:], gate[:, 0:C1])
         load_wet(1)
         nc.sync.dma_start(gate_rest[:], gate[:, C1:T])
-        load_a(0, 1)
         load_wet(2)
         load_scales(wet_s[1], wet_rows[SHARE:E])
+        load_a(0, 2)
         load_wet(3)
-        load_a(1, 2)
         load_a(2, 4)
         load_scales(wgt_s, wgt_scales.rearrange("f s b k -> (f s) b k"))
         load_wgt(0)
@@ -139,8 +153,7 @@ def tile_moe_hib_relu_kernel(
 
         staged = {}
 
-        def first_product(f, cuts, over=None):
-            whole = slot("z%d" % f, [P, PACK, C1], F32, over) if over else None
+        def first_product(f, cuts, whole=None):
             weights = gate_rest[:, C1 * (f - 1) : C1 * f] if f else gate_first[:]
             for lo, hi in cuts:
                 z_ps = psum.tile([P, hi - lo, C1], F32, name="z_ps", tag="z", bufs=4)
@@ -156,7 +169,7 @@ def tile_moe_hib_relu_kernel(
                             start=True,
                             stop=True,
                         )
-                z = whole[:, lo:hi, :] if over else slot("z%d_%d" % (f, lo), [P, hi - lo, C1], F32)[:]
+                z = whole[:, lo:hi, :] if whole is not None else slot("z%d_%d" % (f, lo), [P, hi - lo, C1], F32)[:]
                 nc.vector.tensor_tensor(z, z_ps[:], weights.unsqueeze(1).to_broadcast([P, hi - lo, C1]), ALU.mult)
                 for t in range(lo, hi):
                     staged[f, t] = z[:, t - lo, :]
@@ -177,46 +190,41 @@ def tile_moe_hib_relu_kernel(
 
         zwin = {}
 
-        def scatter_z(scatter, f, t, over=None, offset=None):
-            name = "zwin%d_%d" % (f, t)
-            if offset is None:
-                zwin[f, t] = slot(name, [P, T], F32, over)
-            else:
-                zwin[f, t] = placed.tile([P, T], F32, name=name, offset=offset, align_bytes=64)
+        def scatter_z(scatter, f, t, over=None):
+            zwin[f, t] = slot("zwin%d_%d" % (f, t), [P, T], F32, over)
             scatter(zwin[f, t], offs2_l[:, cols(C1 * f, C1 * (f + 1))], staged[f, t])
 
-        da = {}
+        da_tiles = {(f0, f1): slot("da%d" % f0, [P, (f1 - f0) * C1, PACK], BF16) for f0, f1 in ((0, 2), (2, 3), (3, 4))}
+        da = {f: tile[:, C1 * (f - f0) : C1 * (f - f0 + 1), :] for (f0, f1), tile in da_tiles.items() for f in range(f0, f1)}
 
         def mask_and_interleave(f, planes):
             planar = slot("planar%d" % f, [P, PACK, C1], BF16)
             for t in planes:
-                nc.gpsimd.tensor_tensor(
-                    planar[:, t, :],
-                    zwin[f, t][:, C1 * f : C1 * (f + 1)],
-                    mask[f][:, t, :],
-                    ALU.mult,
-                )
-            da[f] = slot("da%d" % f, [P, C1, PACK], BF16)
-            nc.gpsimd.tensor_scalar(da[f][:], planar[:].rearrange("p t j -> p j t"), 1.0, 0.0, ALU.mult, ALU.add)
+                nc.gpsimd.tensor_tensor(planar[:, t, :], zwin[f, t][:, C1 * f : C1 * (f + 1)], mask[f][:, t, :], ALU.mult)
+            nc.gpsimd.tensor_scalar(da[f], planar[:].rearrange("p t j -> p j t"), 1.0, 0.0, ALU.mult, ALU.add)
 
         dx_ps = {}
 
-        def quantise_and_multiply(f, blocks, over=None):
-            da_w = slot("da_w%d" % f, [P, C1], U32, over)
-            da_s = slot("da_s%d" % f, [P, C1], U8)
-            nc.vector.quantize_mx(out=da_w[:].bitcast(FP8X4), scales=da_s[:], in_=da[f][:].rearrange("p j t -> p (j t)"))
-            if f % 2 == 0:
+        def quantise_and_multiply(f0, f1, blocks):
+            da_w = slot("da_w%d" % f0, [P, (f1 - f0) * C1], U32)
+            da_s = slot("da_s%d" % f0, [P, (f1 - f0) * C1], U8)
+            nc.vector.quantize_mx(
+                out=da_w[:].bitcast(FP8X4), scales=da_s[:], in_=da_tiles[f0, f1][:].rearrange("p j t -> p (j t)")
+            )
+            if f0 % 2 == 0:
                 for c in (0, 2):
-                    dx_ps[c, f // 2] = psum.tile([P, 2, C1], F32, name="dx_ps", tag="dx_vector")
-            dx_ps["scalar", f] = psum.tile([P, 2, C1], F32, name="dx_ps", tag="dx_scalar")
-            for c in blocks:
+                    dx_ps[c, f0 // 2] = psum.tile([P, 2, C1], F32, name="dx_ps", tag="dx_vector")
+            for f in range(f0, f1):
+                dx_ps["scalar", f] = psum.tile([P, 2, C1], F32, name="dx_ps", tag="dx_scalar")
+            for f, c in blocks:
                 ks = slice(P * c, P * (c + 1))
+                js = slice(C1 * (f - f0), C1 * (f - f0 + 1))
                 nc.tensor.matmul_mx(
                     out=dx_ps["scalar", f][:, c // 2, :] if c % 2 else dx_ps[c, f // 2][:, f % 2, :],
                     lhsT=wgt_w[f // 2][:, f % 2, ks].bitcast(FP8X4),
                     lhsT_scale=wgt_s[ROWS * f : P, ks],
-                    rhs=da_w[:].bitcast(FP8X4),
-                    rhs_scale=da_s[:],
+                    rhs=da_w[:, js].bitcast(FP8X4),
+                    rhs_scale=da_s[:, js],
                     start=True,
                     stop=True,
                 )
@@ -227,9 +235,12 @@ def tile_moe_hib_relu_kernel(
             dx[who, n] = slot("dx_%s_%d" % (who, n), [P, 2, C1], F32)
             copy(dx[who, n][:], dx_ps[who, n][:])
 
-        def vector_piece(c, f, over=None):
-            piece = slot("dx_piece%d" % f, [P, C1], F32, over)
-            nc.vector.tensor_copy(piece[:], dx_ps[c, f // 2][:, f % 2, :])
+        def copy_piece(c, f, over=None):
+            piece = slot("dx_piece%d_%d" % (c, f), [P, C1], F32, over)
+            if c % 2:
+                nc.scalar.copy(piece[:], dx_ps["scalar", f][:, c // 2, :])
+            else:
+                nc.vector.tensor_copy(piece[:], dx_ps[c, f // 2][:, f % 2, :])
             return piece
 
         owin = {}
@@ -263,50 +274,47 @@ def tile_moe_hib_relu_kernel(
         first_product(1, halves)
         permute_scales(1)
         permute_group(2)
+        make_masks(0, 2)
+        first_product(2, halves, slot("z2", [P, PACK, C1], F32))
         permute_group(3)
-        make_masks(0, 1, "wet_w3")
-        first_product(2, halves, "a0")
-        make_masks(1, 2)
         mask_and_interleave(0, range(PACK))
         scatter_z(on_scalar, 1, 0)
         scatter_z(on_scalar, 1, 1)
-        scatter_z(on_vector, 1, 2, offset=0)
-        scatter_z(on_vector, 1, 3, offset=4 * T)
-        mask_and_interleave(1, (2, 0, 3, 1))
-        first_product(3, halves, "z1_2")
+        scatter_z(on_vector, 1, 2)
+        scatter_z(on_vector, 1, 3)
+        mask_and_interleave(1, (0, 2, 1, 3))
+        first_product(3, halves)
         make_masks(2, 4)
         for t in (0, 1, 3):
             scatter_z(on_scalar, 2, t)
-        quantise_and_multiply(0, (1, 3, 0, 2), "gate_rest")
-        scatter_z(on_vector, 2, 2, "a2")
-        mask_and_interleave(2, (0, 1, 3, 2))
+        scatter_z(on_vector, 2, 2, "wet_p6")
+        mask_and_interleave(2, (0, 1, 2, 3))
         scatter_z(on_scalar, 3, 0)
-        copy_dx(nc.scalar.copy, "scalar", 0)
-        scatter_z(on_scalar, 3, 1, "da_s0")
-        quantise_and_multiply(1, (0, 2, 1, 3), "a0")
-        scatter_z(on_vector, 3, 2, "da1")
-        scatter_z(on_vector, 3, 3, "a2")
-        mask_and_interleave(3, (0, 2, 1, 3))
+        scatter_z(on_scalar, 3, 1)
+        scatter_z(on_vector, 3, 2)
+        quantise_and_multiply(0, 2, ((0, 1), (0, 3), (0, 0), (1, 0), (1, 1), (1, 3), (0, 2), (1, 2)))
+        scatter_z(on_vector, 3, 3, "planar1")
+        mask_and_interleave(3, (2, 0, 1, 3))
         copy_dx(nc.vector.tensor_copy, 0, 0)
-        scalar_dx(3, 0, "a0")
+        copy_dx(nc.vector.tensor_copy, 2, 0)
+        copy_dx(nc.scalar.copy, "scalar", 0)
         copy_dx(nc.scalar.copy, "scalar", 1)
-        copy_dx(nc.scalar.copy, 2, 0)
-        scalar_dx(1, 0, "da_s1")
+        scalar_dx(3, 0)
+        scalar_dx(1, 0)
         scalar_dx(3, 1)
         scalar_dx(1, 1)
         vector_dx(0, 0)
-        quantise_and_multiply(2, (0, 1, 3, 2), "dx_0_0")
-        vector_dx(2, 0, "da2")
-        copy_dx(nc.scalar.copy, "scalar", 2)
-        scalar_dx(1, 2)
-        scalar_dx(3, 2)
-        cover = vector_piece(0, 2, "planar3")
-        quantise_and_multiply(3, (0, 2, 1, 3))
+        quantise_and_multiply(2, 3, ((2, 0), (2, 1), (2, 3), (2, 2)))
+        vector_dx(2, 0)
+        pieces = {c: copy_piece(c, 2) for c in (1, 3)}
+        for c in (1, 3):
+            scatter_dx(on_scalar, c, 2 * C1, 3 * C1, pieces[c][:])
+        cover = copy_piece(0, 2, "planar3")
+        quantise_and_multiply(3, 4, ((3, 0), (3, 2), (3, 1), (3, 3)))
         scatter_dx(on_vector, 0, 2 * C1, 3 * C1, cover[:])
-        last = vector_piece(0, 3)
+        pieces = {c: copy_piece(c, 3) for c in (0, 1, 3)}
         copy_dx(nc.vector.tensor_copy, 2, 1)
-        copy_dx(nc.scalar.copy, "scalar", 3)
-        scalar_dx(1, 3, queue=nc.scalar)
-        scatter_dx(on_vector, 0, 3 * C1, T, last[:])
-        scalar_dx(3, 3, queue=nc.scalar)
+        scatter_dx(on_scalar, 1, 3 * C1, T, pieces[1][:], queue=nc.scalar)
+        scatter_dx(on_vector, 0, 3 * C1, T, pieces[0][:])
+        scatter_dx(on_scalar, 3, 3 * C1, T, pieces[3][:], queue=nc.scalar)
         vector_dx(2, 1)

@@ -30,13 +30,17 @@ PLACES = {
     "a0": WINDOW // 2,
     "zwin1_2": WINDOW,
     "zwin1_3": 2 * WINDOW,
-    "owin2": 3 * WINDOW,
-    "planar2": 3 * WINDOW,
-    "dx_0_0": 3 * WINDOW + 3 * WINDOW // 4,
-    "da_w2": 4 * WINDOW,
-    "dx_piece1_3": 5 * WINDOW,
-    "dx_piece1_2": 5 * WINDOW + WINDOW // 8,
-    "dx_piece3_3": 5 * WINDOW + WINDOW // 4,
+    "da0": 3 * WINDOW + WINDOW // 4,
+    "planar2": 4 * WINDOW,
+    "owin2": 4 * WINDOW,
+    "dx_0_0": 4 * WINDOW + 3 * WINDOW // 4,
+    "da_w2": 5 * WINDOW,
+    "dx_piece1_3": 6 * WINDOW,
+    "dx_piece1_2": 6 * WINDOW + WINDOW // 8,
+    "dx_piece3_3": 6 * WINDOW + WINDOW // 4,
+    "mask2": 7 * WINDOW,
+    "planar1": 7 * WINDOW + 3 * WINDOW // 4,
+    "zwin3_3": 8 * WINDOW,
 }
 
 
@@ -284,18 +288,18 @@ def tile_moe_hib_relu_kernel(
         scatter_z(on_vector, 1, 3)
         mask_and_interleave(1, (0, 2, 1, 3))
         first_product(3, halves)
-        make_masks(2, 4)
         for t in (0, 1, 3):
             scatter_z(on_scalar, 2, t)
         scatter_z(on_vector, 2, 2, "wet_p6")
-        mask_and_interleave(2, (0, 1, 2, 3))
         scatter_z(on_scalar, 3, 0)
         scatter_z(on_scalar, 3, 1)
         scatter_z(on_vector, 3, 2)
-        quantise_and_multiply(0, 2, ((0, 1), (0, 3), (0, 0), (1, 0), (1, 1), (1, 3), (0, 2), (1, 2)))
-        scatter_z(on_vector, 3, 3, "planar1")
+        make_masks(2, 4)
+        quantise_and_multiply(0, 2, ((0, 0), (1, 0), (0, 1), (0, 3), (0, 2), (1, 2), (1, 1), (1, 3)))
+        scatter_z(on_vector, 3, 3)
+        mask_and_interleave(2, range(PACK))
         mask_and_interleave(3, (2, 0, 1, 3))
-        copy_dx(nc.vector.tensor_copy, 0, 0)
+        copy_dx(nc.scalar.copy, 0, 0)
         copy_dx(nc.vector.tensor_copy, 2, 0)
         copy_dx(nc.scalar.copy, "scalar", 0)
         copy_dx(nc.scalar.copy, "scalar", 1)

@@ -139,9 +139,15 @@ def tile_moe_hib_relu_kernel(
         def as_loaded(ap):
             return ap.rearrange("p (m t) -> p m t", t=PACK)
 
-        def permute_words(copy, e):
-            wet_p[e] = slot("wet_p%d" % e, [P, H], U32)
-            copy(by_planes(wet_p[e][:]), as_loaded(wet_w[e // EPG][:, e % EPG, :]))
+        def permute_first(lo, hi):
+            tile = slot("wet_first%d" % lo, [P, EPG, hi - lo, P], U32)
+            nc.scalar.copy(
+                tile[:].rearrange("p e t m -> p e m t"),
+                wet_w[0][:].rearrange("p e (m t) -> p e m t", t=PACK)[:, :, :, lo:hi],
+            )
+            for e in range(EPG):
+                for t in range(lo, hi):
+                    wet_p[e, t] = tile[:, e, t - lo, :]
 
         def permute_group(f):
             tile = slot("wet_p%d" % (EPG * f), [P, EPG, H], U32)
@@ -150,7 +156,8 @@ def tile_moe_hib_relu_kernel(
                 wet_w[f][:].rearrange("p e (m t) -> p e m t", t=PACK),
             )
             for u in range(EPG):
-                wet_p[EPG * f + u] = tile[:, u, :]
+                for t in range(PACK):
+                    wet_p[EPG * f + u, t] = tile[:, u, P * t : P * (t + 1)]
 
         def permute_scales(h):
             nc.vector.tensor_copy(by_planes(wet_sp[h][:]), as_loaded(wet_s[h][:]))
@@ -166,7 +173,7 @@ def tile_moe_hib_relu_kernel(
                     for e in range(EPG * f, EPG * (f + 1)):
                         nc.tensor.matmul_mx(
                             out=z_ps[:, t - lo, C2 * (e % EPG) : C2 * (e % EPG + 1)],
-                            lhsT=wet_p[e][:, cs].bitcast(FP8X4),
+                            lhsT=wet_p[e, t].bitcast(FP8X4),
                             lhsT_scale=wet_sp[e // SHARE][ROWS * (e % SHARE) : P, cs],
                             rhs=gq_w[e].bitcast(FP8X4),
                             rhs_scale=gq_s[e],
@@ -266,8 +273,8 @@ def tile_moe_hib_relu_kernel(
         gather(gq_s, dy_s, U8, 0, 4 * C2, "gq_s0")
         gather(gq_w, dy_w, U32, 0, 2 * C2, "gq_w0")
         gather(gq_w, dy_w, U32, 2 * C2, 5 * C2, "gq_w1")
-        for e in range(EPG):
-            permute_words(nc.scalar.copy, e)
+        for lo, hi in halves:
+            permute_first(lo, hi)
         permute_scales(0)
         gather(gq_w, dy_w, U32, 5 * C2, T, "gq_w2", "wet_s0")
         first_product(0, ((0, 1), (1, 3), (3, 4)))
@@ -295,7 +302,7 @@ def tile_moe_hib_relu_kernel(
         scatter_z(on_scalar, 3, 1)
         scatter_z(on_vector, 3, 2)
         make_masks(2, 4)
-        quantise_and_multiply(0, 2, ((0, 0), (1, 0), (0, 1), (0, 3), (0, 2), (1, 2), (1, 1), (1, 3)))
+        quantise_and_multiply(0, 2, ((0, 0), (1, 0), (0, 2), (1, 2), (0, 1), (0, 3), (1, 1), (1, 3)))
         scatter_z(on_vector, 3, 3)
         mask_and_interleave(2, range(PACK))
         mask_and_interleave(3, (2, 0, 1, 3))

from contextlib import ExitStack

import concourse.mybir as mybir

K, T, G, C1, E, C2, H, N = 512, 1024, 4, 256, 8, 128, 512, 512
FLOPS = 2 * T * N * H + 2 * T * H * K

F32 = mybir.dt.float32
BF16 = mybir.dt.bfloat16
I32 = mybir.dt.int32
U32 = mybir.dt.uint32
U16 = mybir.dt.uint16
U8 = mybir.dt.uint8
FP8X4 = mybir.dt.float8_e4m3fn_x4
ACT = mybir.ActivationFunctionType
ALU = mybir.AluOpType

P = 128
PACK = 4
BLOCKS = 4
PER_COL = 16
EPG = E // G
QUAD = 32
QUADS = P // QUAD
ROWS = 4
SHARE = 4
WINDOW = 4 * T
PLACES = {
    "z2": 0,
    "a0": WINDOW // 2,
    "zwin1_2": WINDOW,
    "zwin1_3": 2 * WINDOW,
    "da0": 3 * WINDOW + WINDOW // 4,
    "planar2": 4 * WINDOW,
    "owin2": 4 * WINDOW,
    "dx_0_0": 4 * WINDOW + 3 * WINDOW // 4,
    "da_w2": 5 * WINDOW,
    "dx_piece1_3": 6 * WINDOW,
    "dx_piece1_2": 6 * WINDOW + WINDOW // 8,
    "dx_piece3_3": 6 * WINDOW + WINDOW // 4,
    "mask2": 7 * WINDOW,
    "planar1": 7 * WINDOW + 3 * WINDOW // 4,
    "zwin3_3": 8 * WINDOW,
}


def tile_moe_hib_relu_kernel(
    tc, dy_words, dy_scales, wet_words, wet_scales, wgt_words, wgt_scales, a, gate, offs, offs2, dst, out
):
    nc = tc.nc

    with ExitStack() as ctx:
        lists = ctx.enter_context(tc.tile_pool(name="lists", bufs=1))
        keep = ctx.enter_context(tc.tile_pool(name="keep", bufs=1))
        placed = ctx.enter_context(tc.tile_pool(name="placed", bufs=1))
        psum = ctx.enter_context(tc.psum_pool(name="psum", bufs=2))

        def slot(name, shape, dtype, over=None):
            if name in PLACES:
                return placed.tile(shape, dtype, name=name, offset=PLACES[name], align_bytes=64)
            return keep.tile(shape, dtype, name=name, tag=over or name, align_bytes=64)

        dst_l = lists.tile([P, T // PER_COL], U16, name="dst_l")
        offs2_l = lists.tile([P, T // PER_COL], U16, name="offs2_l")
        offs_l = lists.tile([P, T // PER_COL], U16, name="offs_l")
        dy_w = slot("dy_w", [P, T], U32)
        dy_s = slot("dy_s", [P, T], U8)
        wet_s = [slot("wet_s%d" % h, [P, H], U8) for h in range(E // SHARE)]
        wet_sp = [slot("wet_sp%d" % h, [P, H], U8) for h in range(E // SHARE)]
        wgt_s = slot("wgt_s", [P, K], U8)
        gate_first = slot("gate_first", [P, C1], F32)
        gate_rest = slot("gate_rest", [P, T - C1], F32)
        a_part = {
            (0, 2): slot("a0", [P, PACK, 2 * C1], F32),
            (2, 4): slot("a2", [P, PACK, 2 * C1], F32),
        }
        wet_w = [slot("wet_w%d" % f, [P, EPG, H], U32) for f in range(G)]
        wgt_w = [slot("wgt_w%d" % h, [P, 2, K], U32) for h in range(2)]

        def load_scales(tile, rows):
            matrices = rows.shape[0]
            for q in range(QUADS):
                nc.sync.dma_start(
                    tile[QUAD * q : QUAD * q + ROWS * matrices, :].bitcast(I32),
                    rows[:, ROWS * q : ROWS * (q + 1), :].bitcast(I32),
                )

        nc.gpsimd.memset(wet_s[1][:].bitcast(I32), 0)
        nc.gpsimd.memset(wgt_s[:].bitcast(I32), 0)

        wet_words_p = wet_words.rearrange("e s p i d -> p (e s) (i d)")
        wgt_words_p = wgt_words.rearrange("f s p k d -> p (f s) (k d)")
        wet_rows = wet_scales.rearrange("e s b i -> (e s) b i")

        def load_wet(f):
            nc.sync.dma_start(wet_w[f][:].bitcast(I32), wet_words_p[:, EPG * f : EPG * (f + 1), :].bitcast(I32))

        def load_wgt(h):
            nc.sync.dma_start(wgt_w[h][:].bitcast(I32), wgt_words_p[:, 2 * h : 2 * (h + 1), :].bitcast(I32))

        def load_a(f0, f1):
            nc.sync.dma_start(a_part[f0, f1][:], a[:, C1 * f0 : C1 * f1].rearrange("(p t) j -> p t j", t=PACK))

        nc.sync.dma_start(dst_l[:], dst)
        load_scales(dy_s, dy_scales.to_broadcast([QUAD // ROWS, QUADS * ROWS, T]))
        nc.sync.dma_start(offs2_l[:], offs2)
        nc.sync.dma_start(dy_w[:].bitcast(I32), dy_words.rearrange("s p t d -> p (s t d)").bitcast(I32))
        load_wet(0)
        load_scales(wet_s[0], wet_rows)
        nc.sync.dma_start(gate_first[:], gate[:, 0:C1])
        load_wet(1)
        nc.sync.dma_start(gate_rest[:], gate[:, C1:T])
        load_wet(2)
        load_scales(wet_s[1], wet_rows[SHARE:E])
        load_a(0, 2)
        load_wet(3)
        load_a(2, 4)
        load_scales(wgt_s, wgt_scales.rearrange("f s b k -> (f s) b k"))
        load_wgt(0)
        nc.sync.dma_start(offs_l[:], offs)
        load_wgt(1)

        def cols(lo, hi):
            return slice(lo // PER_COL, hi // PER_COL)

        gq_w, gq_s = {}, {}

        def gather(views, src, dtype, lo, hi, name, over=None):
            tile = slot(name, [P, hi - lo], dtype, over)
            nc.vector.tensor_copy(tile[:], src[:].indirect(dst_l[:, cols(lo, hi)]))
            for m in range(lo, hi, C2):
                views[m // C2] = tile[:, m - lo : m - lo + C2]

        wet_p = {}

        def by_planes(ap):
            return ap.rearrange("p (t m) -> p m t", t=PACK)

        def as_loaded(ap):
            return ap.rearrange("p (m t) -> p m t", t=PACK)

        def permute_first(lo, hi):
            tile = slot("wet_first%d" % lo, [P, EPG, hi - lo, P], U32)
            nc.scalar.copy(
                tile[:].rearrange("p e t m -> p e m t"),
                wet_w[0][:].rearrange("p e (m t) -> p e m t", t=PACK)[:, :, :, lo:hi],
            )
            for e in range(EPG):
                for t in range(lo, hi):
                    wet_p[e, t] = tile[:, e, t - lo, :]

        def permute_group(f):
            tile = slot("wet_p%d" % (EPG * f), [P, EPG, H], U32)
            nc.vector.tensor_copy(
                tile[:].rearrange("p e (t m) -> p e m t", t=PACK),
                wet_w[f][:].rearrange("p e (m t) -> p e m t", t=PACK),
            )
            for u in range(EPG):
                for t in range(PACK):
                    wet_p[EPG * f + u, t] = tile[:, u, P * t : P * (t + 1)]

        def permute_scales(h):
            nc.vector.tensor_copy(by_planes(wet_sp[h][:]), as_loaded(wet_s[h][:]))

        staged = {}

        def first_product(f, cuts, whole=None):
            weights = gate_rest[:, C1 * (f - 1) : C1 * f] if f else gate_first[:]
            for lo, hi in cuts:
                z_ps = psum.tile([P, hi - lo, C1], F32, name="z_ps", tag="z", bufs=4)
                for t in range(lo, hi):
                    cs = slice(P * t, P * (t + 1))
                    for e in range(EPG * f, EPG * (f + 1)):
                        nc.tensor.matmul_mx(
                            out=z_ps[:, t - lo, C2 * (e % EPG) : C2 * (e % EPG + 1)],
                            lhsT=wet_p[e, t].bitcast(FP8X4),
                            lhsT_scale=wet_sp[e // SHARE][ROWS * (e % SHARE) : P, cs],
                            rhs=gq_w[e].bitcast(FP8X4),
                            rhs_scale=gq_s[e],
                            start=True,
                            stop=True,
                        )
                z = whole[:, lo:hi, :] if whole is not None else slot("z%d_%d" % (f, lo), [P, hi - lo, C1], F32)[:]
                nc.vector.tensor_tensor(z, z_ps[:], weights.unsqueeze(1).to_broadcast([P, hi - lo, C1]), ALU.mult)
                for t in range(lo, hi):
                    staged[f, t] = z[:, t - lo, :]

        def on_vector(win, offsets, values):
            nc.vector.tensor_copy(win[:].indirect(offsets), values)

        def on_scalar(win, offsets, values):
            nc.scalar.activation(win[:].indirect(offsets), values, ACT.Copy)

        mask = {}

        def make_masks(f0, f1, over=None):
            tile = slot("mask%d" % f0, [P, PACK, (f1 - f0) * C1], BF16, over)
            nc.vector.tensor_scalar(tile[:], a_part[f0, f1][:], 0.0, None, ALU.is_gt)
            for f in range(f0, f1):
                mask[f] = tile[:, :, C1 * (f - f0) : C1 * (f - f0 + 1)]

        zwin = {}

        def scatter_z(scatter, f, t, over=None):
            zwin[f, t] = slot("zwin%d_%d" % (f, t), [P, T], F32, over)
            scatter(zwin[f, t], offs2_l[:, cols(C1 * f, C1 * (f + 1))], staged[f, t])

        da_tiles = {(f0, f1): slot("da%d" % f0, [P, (f1 - f0) * C1, PACK], BF16) for f0, f1 in ((0, 2), (2, 3), (3, 4))}
        da = {f: tile[:, C1 * (f - f0) : C1 * (f - f0 + 1), :] for (f0, f1), tile in da_tiles.items() for f in range(f0, f1)}

        def mask_and_interleave(f, planes):
            planar = slot("planar%d" % f, [P, PACK, C1], BF16)
            for t in planes:
                nc.gpsimd.tensor_tensor(planar[:, t, :], zwin[f, t][:, C1 * f : C1 * (f + 1)], mask[f][:, t, :], ALU.mult)
            nc.gpsimd.tensor_scalar(da[f], planar[:].rearrange("p t j -> p j t"), 1.0, 0.0, ALU.mult, ALU.add)

        dx_ps = {}

        def quantise_and_multiply(f0, f1, blocks):
            da_w = slot("da_w%d" % f0, [P, (f1 - f0) * C1], U32)
            da_s = slot("da_s%d" % f0, [P, (f1 - f0) * C1], U8)
            nc.vector.quantize_mx(
                out=da_w[:].bitcast(FP8X4), scales=da_s[:], in_=da_tiles[f0, f1][:].rearrange("p j t -> p (j t)")
            )
            if f0 % 2 == 0:
                for c in (0, 2):
                    dx_ps[c, f0 // 2] = psum.tile([P, 2, C1], F32, name="dx_ps", tag="dx_vector")
            for f in range(f0, f1):
                dx_ps["scalar", f] = psum.tile([P, 2, C1], F32, name="dx_ps", tag="dx_scalar")
            for f, c in blocks:
                ks = slice(P * c, P * (c + 1))
                js = slice(C1 * (f - f0), C1 * (f - f0 + 1))
                nc.tensor.matmul_mx(
                    out=dx_ps["scalar", f][:, c // 2, :] if c % 2 else dx_ps[c, f // 2][:, f % 2, :],
                    lhsT=wgt_w[f // 2][:, f % 2, ks].bitcast(FP8X4),
                    lhsT_scale=wgt_s[ROWS * f : P, ks],
                    rhs=da_w[:, js].bitcast(FP8X4),
                    rhs_scale=da_s[:, js],
                    start=True,
                    stop=True,
                )

        dx = {}

        def copy_dx(copy, who, n):
            dx[who, n] = slot("dx_%s_%d" % (who, n), [P, 2, C1], F32)
            copy(dx[who, n][:], dx_ps[who, n][:])

        def copy_piece(c, f, over=None):
            piece = slot("dx_piece%d_%d" % (c, f), [P, C1], F32, over)
            if c % 2:
                nc.scalar.copy(piece[:], dx_ps["scalar", f][:, c // 2, :])
            else:
                nc.vector.tensor_copy(piece[:], dx_ps[c, f // 2][:, f % 2, :])
            return piece

        owin = {}

        def scatter_dx(scatter, c, lo, hi, values, over=None, queue=nc.sync):
            if lo == 0:
                owin[c] = slot("owin%d" % c, [P, T], F32, over)
            scatter(owin[c], offs_l[:, cols(lo, hi)], values)
            if hi == T:
                queue.dma_start(out[P * c : P * (c + 1), :], owin[c][:])

        def scalar_dx(c, f, over=None, queue=nc.sync):
            scatter_dx(on_scalar, c, C1 * f, C1 * (f + 1), dx["scalar", f][:, c // 2, :], over, queue)

        def vector_dx(c, h, over=None):
            scatter_dx(on_vector, c, 2 * C1 * h, 2 * C1 * (h + 1), dx[c, h][:].rearrange("p f j -> p (f j)"), over)

        halves = ((0, 2), (2, 4))
        gather(gq_s, dy_s, U8, 0, 4 * C2, "gq_s0")
        gather(gq_w, dy_w, U32, 0, 2 * C2, "gq_w0")
        gather(gq_w, dy_w, U32, 2 * C2, 5 * C2, "gq_w1")
        for lo, hi in halves:
            permute_first(lo, hi)
        permute_scales(0)
        gather(gq_w, dy_w, U32, 5 * C2, T, "gq_w2", "wet_s0")
        first_product(0, ((0, 1), (1, 3), (3, 4)))
        for t in range(PACK):
            scatter_z(on_scalar, 0, t)
        permute_group(1)
        gather(gq_s, dy_s, U8, 4 * C2, T, "gq_s1", "gate_first")
        first_product(1, halves)
        permute_scales(1)
        permute_group(2)
        make_masks(0, 2)
        first_product(2, halves, slot("z2", [P, PACK, C1], F32))
        permute_group(3)
        mask_and_interleave(0, range(PACK))
        scatter_z(on_scalar, 1, 0)
        scatter_z(on_scalar, 1, 1)
        scatter_z(on_vector, 1, 2)
        scatter_z(on_vector, 1, 3)
        mask_and_interleave(1, (0, 2, 1, 3))
        first_product(3, halves)
        for t in (0, 1, 3):
            scatter_z(on_scalar, 2, t)
        scatter_z(on_vector, 2, 2, "wet_p6")
        scatter_z(on_scalar, 3, 0)
        scatter_z(on_scalar, 3, 1)
        scatter_z(on_vector, 3, 2)
        make_masks(2, 4)
        quantise_and_multiply(0, 2, ((0, 0), (1, 0), (0, 2), (1, 2), (0, 1), (0, 3), (1, 1), (1, 3)))
        scatter_z(on_vector, 3, 3)
        mask_and_interleave(2, range(PACK))
        mask_and_interleave(3, (2, 0, 1, 3))
        copy_dx(nc.scalar.copy, 0, 0)
        copy_dx(nc.vector.tensor_copy, 2, 0)
        copy_dx(nc.scalar.copy, "scalar", 0)
        copy_dx(nc.scalar.copy, "scalar", 1)
        scalar_dx(3, 0)
        scalar_dx(1, 0)
        scalar_dx(3, 1)
        scalar_dx(1, 1)
        vector_dx(0, 0)
        quantise_and_multiply(2, 3, ((2, 0), (2, 1), (2, 3), (2, 2)))
        vector_dx(2, 0)
        pieces = {c: copy_piece(c, 2) for c in (1, 3)}
        for c in (1, 3):
            scatter_dx(on_scalar, c, 2 * C1, 3 * C1, pieces[c][:])
        cover = copy_piece(0, 2, "planar3")
        quantise_and_multiply(3, 4, ((3, 0), (3, 2), (3, 1), (3, 3)))
        scatter_dx(on_vector, 0, 2 * C1, 3 * C1, cover[:])
        pieces = {c: copy_piece(c, 3) for c in (0, 1, 3)}
        copy_dx(nc.vector.tensor_copy, 2, 1)
        scatter_dx(on_scalar, 1, 3 * C1, T, pieces[1][:], queue=nc.scalar)
        scatter_dx(on_vector, 0, 3 * C1, T, pieces[0][:])
        scatter_dx(on_scalar, 3, 3 * C1, T, pieces[3][:], queue=nc.scalar)
        vector_dx(2, 1)
